import numpy as np, ml_dtypes
CORES = [16,17,18,19,32,33,34,35]
N = 8
BF = ml_dtypes.bfloat16
def f(rng, *shape):
    return (rng.standard_normal(shape, dtype=np.float32) * np.exp2(rng.integers(-2, 3, shape[:-1] + (1,)))).astype(BF)
def wide(rng, *shape):
    v = f(rng, *shape).astype(np.float32); k = shape[:-2] + (1, shape[-1])
    return (v * np.exp2(rng.integers(-6, 7, k)) * (rng.random(k) > 0.0625)).astype(BF)
S, R, B, CAP = 256, 128, 2, 96
L, IT, I = 1, 8, 8
D, TOP, F = 1, 1, 16
def where_to(rep):
    i = np.arange(N * S); first = np.maximum.accumulate(np.where(rep == 0, i, 0)); rec = np.add.accumulate((rep == 0).astype(np.int64)) - 1
    return rec, 0 * i, i - first
def count(rec):
    return np.bincount(np.arange(N * S) // S * N + rec // B % N, minlength=N * N)
def parts(rng, lens, total):
    diff = int(total - np.sum(lens)); room = I - lens if diff > 0 else lens - 1
    k = np.bincount(rng.permutation(np.repeat(np.arange(len(lens)), room))[:abs(diff)], minlength=len(lens))
    return lens + (k if diff > 0 else -k)
def rich(rng, n, total):
    return parts(rng, np.where(rng.random(n) * ((I - 1) * n) < 2 * (total - n), rng.integers(1, I + 1, n), 1), total)
def levels(rng, lens):
    if count(np.repeat(np.arange(len(lens)), lens)).max() > CAP:
        lens = np.diff(np.arange(N * R + 1) * (N * S) // (N * R))
    rep = np.full(N * S, TOP, np.int32); rep[np.add.accumulate(lens) - lens] = 0
    if L > 1:
        u = rng.random(N * S).tolist(); i = 0
        for n in lens.tolist():
            k = c = 1
            for j in range(1, n):
                if c == IT or (k < L and n - j <= (L - k) * IT and u[i + j] < 0.35):
                    rep[i + j] = 1; k += 1; c = 1
                else: c += 1
            i += n
    return rep
def values(rng):
    return f(rng, N, 128, S)
def make(rng, cols, p):
    rl = np.ascontiguousarray(np.stack([levels(rng, c) for c in cols]).reshape(8, N, S).transpose(1, 0, 2))
    dl = np.where(rng.random((N, 8, S)) < p, D, rng.integers(0, D, (N, 8, S))).astype(np.int32)
    return {"rl": rl, "dl": dl, "val": values(rng)}
def setup_inputs(rng):
    cols = [rich(rng, int(rng.integers(N * R * 3 // 4, N * R + 1)), N * S) for g in range(8)]
    return make(rng, cols, rng.integers(4, 16, (N, 8, 1)) * 0.0625)
def setup_inputs_full(rng):
    cols = []; mix = rng.permutation(8).tolist(); odd = mix[:4]; home = mix[4]; m = R // N
    for g in range(8):
        if g in odd: cols.append(rich(rng, N * R, N * S)); continue
        c = []
        for q in range(N):
            d = q if g == home else (q + 1 + g % (N - 1)) % N; own = np.arange(R) // B % N == d; v = np.ones(R, np.int64)
            v[own] = parts(rng, v[own], CAP); v[~own] = parts(rng, v[~own], S - CAP); c.append(v)
        cols.append(np.concatenate(c))
    return make(rng, cols, rng.choice(np.array([0.5, 1.0]), (N, 8, 1)))
def setup_inputs_edges(rng):
    cols = []
    for g in range(8):
        a = rng.integers(0, I + 1, N - 1); c = []; at = 0
        if g < 4: a[:] = (0, I, 1, I - 1)[g]
        for q in range(1, N + 1):
            end = q * S - int(a[q - 1]) if q < N else N * S; seg = end - at
            c.append(rich(rng, max(-(-seg // I), seg * R * int(rng.integers(12, 17)) // (16 * S)), seg))
            if q < N: c.append(np.array([I])); at = end + I
        cols.append(np.concatenate(c))
    return make(rng, cols, rng.integers(0, 3, (N, 8, 1)) * 0.5)
def setup_inputs_few(rng):
    cols = []
    for g in range(8):
        h = int(rng.integers(1, I + 1)) if g else I; k = (N * S - h) // I; t = N * S - h - k * I
        cols.append(np.array([h] + [I] * k + ([t] if t else [])))
    p = rng.integers(8, 17, (N, 8, 1)) * 0.0625; p[:, rng.integers(0, 8)] = 0
    return make(rng, cols, p)
def setup_inputs_spread(rng):
    cols = [rich(rng, int(rng.integers(N * S // I, N * R + 1)), N * S) for g in range(8)]
    d = make(rng, cols, rng.integers(1, 16, (N, 8, 1)) * 0.0625)
    d["val"] = wide(rng, N, 128, S)
    return d
def check_inputs(d):
    rl, dl, val = d["rl"], d["dl"], d["val"]; bad = []
    if not (((rl >= 0) & (rl <= TOP)).all() and ((dl >= 0) & (dl <= D)).all()): bad.append("levels")
    if not (rl[0, :, 0] == 0).all(): bad.append("first")
    if not (np.isfinite(val.astype(np.float32)).all()): bad.append("values")
    if bad: return bad
    for g in range(8):
        rec, lst, item = where_to(rl[:, g].reshape(-1))
        if rec[-1] >= N * R: bad.append("records")
        if lst.max() >= L or item.max() >= IT: bad.append("items")
        if count(rec).max() > CAP: bad.append("pairs")
    return sorted(set(bad))
def reference(rl, dl, val):
    y = np.full((N, 8, F, R * I), -2, np.float32); x = val.reshape(N, 8, F, S); q = np.arange(N * S) // S
    for g in range(8):
        rec, lst, item = where_to(rl[:, g].reshape(-1)); lev = dl[:, g].reshape(-1)
        has = (dl[:, g] == D).astype(np.int64); v = (np.add.accumulate(has, axis=1) - has).reshape(-1)
        e = np.where((lev == D)[:, None], x[q, g, :, v].astype(np.float32), (lev - D)[:, None])
        y[rec // B % N, g, :, (rec // (B * N) * B + rec % B) * I + lst * IT + item] = e
    return {"y": y.reshape(N, 8 * F, R * I).astype(BF)}

@@ -1,0 +1,313 @@
+from concourse.bass import DstId, RemoteDMATransfer
+from concourse.mybir import AluOpType as A, ActivationFunctionType as F
+
+W = 104
+YC = 4000
+
+SCRATCH = {
+    "J": ("sbuf", [128, 256], "int32"), "Pi": ("sbuf", [128, 1], "int32"), "pd": ("sbuf", [128, 2], "int32"),
+    "pc": ("sbuf", [128, 8], "float32"), "Kt": ("sbuf", [128, 256], "int32"), "Ct": ("sbuf", [128, 256], "int32"),
+    "BO": ("sbuf", [128, 128], "bfloat16"), "bj": ("sbuf", [128, 128], "float32"),
+    "Lo": ("sbuf", [128, 128], "bfloat16"), "Sh": ("sbuf", [128, 128], "bfloat16"), "Id": ("sbuf", [128, 128], "bfloat16"),
+    "S15": ("sbuf", [128, 128], "bfloat16"), "B64": ("sbuf", [128, 128], "bfloat16"),
+    "mask": ("sbuf", [128, 256], "bfloat16"), "seg": ("sbuf", [128, 256], "bfloat16"),
+    "repk": ("sbuf", [128, 16], "uint16"), "repr": ("sbuf", [128, 16], "uint16"),
+    "pick": ("sbuf", [128, 2048], "bfloat16"), "ones": ("sbuf", [128, 16], "bfloat16"),
+    "rli": ("sbuf", [128, 16], "int32"), "dli": ("sbuf", [128, 16], "int32"), "valt": ("sbuf", [128, 272], "bfloat16"),
+    "rb": ("sbuf", [128, 16], "bfloat16"), "z": ("sbuf", [128, 16], "bfloat16"), "hs": ("sbuf", [128, 32], "bfloat16"),
+    "rb8": ("sbuf", [128, 16], "bfloat16"), "lz": ("sbuf", [128, 16], "bfloat16"),
+    "land1": ("sbuf", [128, 256], "bfloat16"),
+    "Ri": ("sbuf", [128, 16], "int32"), "R15": ("sbuf", [128, 16], "int32"), "par": ("sbuf", [128, 16], "int32"),
+    "sgn": ("sbuf", [128, 16], "float32"), "p95": ("sbuf", [128, 16], "float32"),
+    "H": ("sbuf", [128, 256], "bfloat16"), "S": ("sbuf", [128, 256], "bfloat16"), "offb": ("sbuf", [128, 16], "bfloat16"),
+    "Q": ("sbuf", [128, 256], "bfloat16"), "mt": ("sbuf", [128, 16], "float32"), "m": ("sbuf", [128, 16], "int32"),
+    "db": ("sbuf", [128, 16], "bfloat16"), "cd": ("sbuf", [128, 16], "bfloat16"), "vx": ("sbuf", [128, 16], "float32"),
+    "vy": ("sbuf", [128, 16], "float32"), "l1": ("sbuf", [128, 16], "uint16"), "ev": ("sbuf", [128, 256], "bfloat16"),
+    "w8": ("sbuf", [128, 16], "float32"), "e1": ("sbuf", [128, 16], "float32"), "E": ("sbuf", [128, 16], "float32"),
+    "lead": ("sbuf", [128, 16], "float32"), "Aq": ("sbuf", [128, 16], "float32"), "Zi": ("sbuf", [128, 16], "int32"),
+    "ci": ("sbuf", [128, 1], "int32"), "c2": ("sbuf", [128, 1], "int32"), "cst": ("sbuf", [128, 1], "float32"),
+    "D": ("sbuf", [128, 16], "int32"), "Y1": ("sbuf", [128, 16], "int32"), "Y2": ("sbuf", [128, 16], "int32"),
+    "off": ("sbuf", [128, 16], "int32"), "off16": ("sbuf", [128, 16], "uint16"),
+    "rel0": ("sbuf", [128, 16], "float32"), "rel": ("sbuf", [128, 16], "float32"), "insl": ("sbuf", [128, 256], "bfloat16"),
+    "lw": ("sbuf", [128, 1024], "bfloat16"), "send": ("sbuf", [128, 1024], "bfloat16"), "zer": ("sbuf", [128, 8], "float32"),
+    "land": ("sbuf", [128, 8 * W], "bfloat16"), "Wt": ("sbuf", [128, 64], "uint16"), "Y": ("sbuf", [128, YC], "bfloat16"),
+    "ps1": ("psum", [128, 512], "float32"), "ps2": ("psum", [128, 512], "float32"), "ps3": ("psum", [128, 512], "float32"),
+    "ps4": ("psum", [128, 512], "float32"), "ps5": ("psum", [128, 512], "float32"), "ps6": ("psum", [128, 512], "float32"),
+    "ps7": ("psum", [128, 512], "float32"),
+}
+SEMAPHORES = (["qv", "qs", "qt", "qg", "drl", "ddl", "dval", "dy", "loc1", "loc2"]
+              + ["h%d" % i for i in range(8)] + ["p%d" % i for i in range(8)])
+
+
+def split(cores, me, later, topo):
+    c = cores[me]
+    ds = [d for d in range(len(cores)) if (d > me if later else d != me)]
+    return ([d for d in ds if topo.chip(cores[d]) == topo.chip(c)], [d for d in ds if topo.chip(cores[d]) != topo.chip(c)])
+
+
+def pow2(n):
+    k = 1
+    while 2 * k <= n:
+        k *= 2
+    return k
+
+
+def plan(cores, me, later, topo):
+    near, far = split(cores, me, later, topo)
+    c = cores[me]
+    out = []
+    used = []
+    if far:
+        es = topo.engines(c, cores[far[0]])
+        used = es
+        if later:
+            out.append((far, es[:pow2(len(es))]))
+        else:
+            k = pow2(len(es) // len(far))
+            out += [([d], es[i * k:(i + 1) * k]) for i, d in enumerate(far)]
+    if near:
+        es = [e for e in topo.engines(c, cores[near[0]]) if e not in used]
+        if later:
+            out.append((near, es[:pow2(len(es))]))
+        else:
+            k = pow2(len(es) // len(near))
+            out += [([d], es[i * k:(i + 1) * k]) for i, d in enumerate(near)]
+    return out
+
+
+def arrivals(cores, me, later, topo):
+    n = len(cores)
+    got = []
+    for s in range(n):
+        if s == me or (later and s > me):
+            continue
+        for ds, es in plan(cores, s, later, topo):
+            if me in ds:
+                got.append((topo.chip(cores[s]) != topo.chip(cores[me]), s, len(es)))
+    return [(s, k) for _, s, k in sorted(got)]
+
+
+def bits(es):
+    m = 0
+    for e in es:
+        m |= 1 << e
+    return m
+
+
+def rank_program(g, core, T, topo):
+    rank = T.rank_of(core)
+    if rank is None:
+        return
+    cores = list(T.cores)
+    q = {"qv": g.vector, "qs": g.scalar, "qt": g.tensor, "qg": g, "sync": g.sync}
+    cnt = {"qv": 0, "qs": 0, "qt": 0, "qg": 0}
+    seen = {e: {} for e in q}
+    lastw = {}
+    readers = {}
+
+    def need(e, deps):
+        best = {}
+        for s, n in deps:
+            if seen[e].get(s, 0) < n:
+                best[s] = max(best.get(s, 0), n)
+        for s, n in best.items():
+            q[e].wait_ge(T.sem[s], n)
+            seen[e][s] = n
+
+    def deps_of(e, r, w):
+        d = []
+        for k in list(r) + list(w):
+            if k in lastw:
+                d.append(lastw[k])
+        for k in w:
+            d += [x for x in readers.get(k, []) if x[0] != e]
+        return d
+
+    def note(tag, r, w):
+        for k in r:
+            readers.setdefault(k, []).append(tag)
+        for k in w:
+            lastw[k] = tag
+            readers[k] = []
+
+    def op(e, fn, r, w):
+        need(e, deps_of(e, r, w))
+        fn(q[e]).then_inc(T.sem[e], 1)
+        cnt[e] += 1
+        note((e, cnt[e]), r, w)
+
+    def dma(e, out, in_, sem, r, w):
+        need(e, deps_of(e, r, w))
+        q[e].dma_start(out, in_).then_inc(T.sem[sem], 16)
+        note((sem, 16), r, w)
+
+    def ts(out, in0, s1, s2, op0, op1, r, w):
+        if op1 is None:
+            op("qv", lambda v: v.tensor_scalar(out, in0, s1, s2, op0), r, w)
+        else:
+            op("qv", lambda v: v.tensor_scalar(out, in0, s1, s2, op0, op1), r, w)
+
+    def tt(out, a, b, o, r, w):
+        op("qv", lambda v: v.tensor_tensor(out, a, b, o), r, w)
+
+    def cp(out, a, r, w):
+        op("qv", lambda v: v.tensor_copy(out, a), r, w)
+
+    def ms(ap, c, w):
+        op("qv", lambda v: v.memset(ap, c), [], w)
+
+    def mm(out, l, rh, st, sp, r, w):
+        op("qt", lambda t: t.matmul(out, l, rh, st, sp), r, w)
+
+    def scan(out, a, b, init, r, w):
+        op("qv", lambda v: v.tensor_tensor_scan(out, a, b, init, A.mult, A.add), r, w)
+
+    dma("sync", T.rli[:], T.rl[:], "drl", [], ["rli"])
+    dma("qs", T.dli[:], T.dl[:], "ddl", [], ["dli"])
+    dma("sync", T.valt[:, 0:256], T.val[:], "dval", [], ["val0"])
+
+    op("qg", lambda x: x.iota(T.Pi[:], [[0, 1]], 0, 1), [], ["Pi"])
+    op("qg", lambda x: x.iota(T.J[:], [[1, 256]], 0, 0), [], ["J"])
+    ms(T.ones[:], 1.0, ["ones"])
+    ms(T.valt[:, 256:272], -1.0, ["val1"])
+    ms(T.pick[:], 0.0, ["pick"])
+    ts(T.pd[:, 0:1], T.Pi[:], 4, None, A.logical_shift_right, None, ["Pi"], ["pd0"])
+    ts(T.pd[:, 1:2], T.Pi[:], 15, None, A.bitwise_and, None, ["Pi"], ["pd1"])
+    ts(T.Kt[:], T.J[:], 4, None, A.logical_shift_right, None, ["J"], ["Kt"])
+    cp(T.pc[:, 0:1], T.pd[:, 0:1], ["pd0"], ["pc0"])
+    cp(T.pc[:, 2:3], T.Pi[:], ["Pi"], ["pc2"])
+    ts(T.pc[:, 3:4], T.Pi[:], 1.0, None, A.add, None, ["Pi"], ["pc3"])
+    ts(T.BO[:], T.Kt[:, 0:128], T.pc[:, 0:1], None, A.is_equal, None, ["Kt", "pc0"], ["BO"])
+    cp(T.pc[:, 1:2], T.pd[:, 1:2], ["pd1"], ["pc1"])
+    ts(T.pc[:, 4:5], T.pd[:, 1:2], 15.0, 8.0, A.is_equal, A.mult, ["pd1"], ["pc4"])
+    tt(T.bj[:], T.BO[:], T.J[:, 0:128], A.mult, ["BO", "J"], ["bj"])
+    ts(T.Lo[:], T.bj[:], T.pc[:, 2:3], None, A.is_gt, None, ["bj", "pc2"], ["Lo"])
+    ts(T.Sh[:], T.bj[:], T.pc[:, 3:4], 8.0, A.is_equal, A.mult, ["bj", "pc3"], ["Sh"])
+    for rho in range(16):
+        op("qs", lambda s: s.activation(T.pick[:, 129 * rho:128 * (rho + 1):16], T.BO[:, rho::16], F.Copy),
+           ["BO", "pick"], ["pickw%d" % rho])
+
+    cp(T.rb[:], T.rli[:], ["rli"], ["rb"])
+    ts(T.z[:], T.rli[:], -1.0, 1.0, A.mult, A.add, ["rli"], ["z"])
+    scan(T.hs[:, 16:32], T.rb[:], T.rb[:], 0.0, ["rb"], ["hsw"])
+    scan(T.hs[:, 0:16], T.ones[:], T.z[:], 0.0, ["ones", "z"], ["hsz"])
+    pl = plan(cores, rank, True, topo)
+    loc1 = 0
+    if pl:
+        need("qg", deps_of("qg", ["hsw", "hsz"], []))
+        trs = []
+        for ds, es in pl:
+            adr = [topo.addr(cores[d]) for d in ds]
+            trs.append(RemoteDMATransfer(srcs=[T.hs[:]], dsts=[T.land1[:, 32 * rank:32 * rank + 32] for d in ds],
+                                         dst_ids=[DstId(rid=a[0], pnc=a[1]) for a in adr],
+                                         dma_engine_mask=bits(es), remote_sem=T.sem["h%d" % rank]))
+            loc1 += len(es)
+        g.remote_dma_fused(trs, local_sem=T.sem.loc1)
+    op("qg", lambda x: x.iota(T.lw[:], [[0, 8], [1, 128]], 80, 0, allow_small_or_imprecise_dtypes=True), [], ["lw"])
+
+    mm(T.ps1[:, 0:1], T.Lo[:], T.hs[:, 15:16], True, True, ["Lo", "hsz"], ["ps1"])
+    mm(T.ps1[:, 1:2], T.Sh[:], T.hs[:, 31:32], True, True, ["Sh", "hsw"], ["ps1"])
+    ts(T.seg[:], T.J[:], 15, None, A.bitwise_and, None, ["J"], ["Ct"]) if False else \
+        ts(T.Ct[:], T.J[:], 15, None, A.bitwise_and, None, ["J"], ["Ct"])
+    ts(T.repr[:], T.J[:, 0:16], 0.0, T.pc[:, 1:2], A.mult, A.add, ["J", "pc1"], ["repr"])
+    ts(T.Ri[:], T.hs[:, 0:16], T.ps1[:, 0:1], None, A.add, None, ["hsz", "ps1"], ["Ri"])
+    ts(T.seg[:], T.Ct[:], 0.0, None, A.is_gt, None, ["Ct"], ["seg"])
+    ts(T.R15[:], T.Ri[:], 15, None, A.bitwise_and, None, ["Ri"], ["R15"])
+    cp(T.repk[:], T.J[:, 0:16], ["J"], ["repk"])
+    cp(T.db[:], T.dli[:], ["dli"], ["db"])
+    tt(T.H[:], T.R15[:, 0:16].indirect(T.repr[:, 0:16]), T.Kt[:], A.is_equal, ["R15", "repr", "Kt"], ["H"])
+    scan(T.cd[:], T.ones[:], T.db[:], 0.0, ["ones", "db"], ["cd"])
+    scan(T.S[:], T.seg[:], T.H[:], 0.0, ["seg", "H"], ["S"])
+    mm(T.ps2[:, 0:1], T.Lo[:], T.cd[:, 15:16], True, True, ["Lo", "cd"], ["ps2"])
+    mm(T.ps3[:, 0:16], T.Lo[:], T.S[:, 15::16], True, True, ["Lo", "S"], ["ps3"])
+    ts(T.vx[:], T.cd[:], T.ps2[:, 0:1], -257.0, A.add, A.add, ["cd", "ps2"], ["vx"])
+    ts(T.Id[:], T.J[:, 0:128], T.pc[:, 2:3], None, A.is_equal, None, ["J", "pc2"], ["Id"])
+    cp(T.offb[:], T.ps3[:, 0:16], ["ps3"], ["offb"])
+    tt(T.vy[:], T.vx[:], T.db[:], A.mult, ["vx", "db"], ["vy"])
+    ts(T.lz[:], T.hs[:, 0:16], 0.0, -1.0, A.is_equal, A.mult, ["hsz"], ["lz"])
+    tt(T.Q[:], T.offb[:, 0:16].indirect(T.repk[:, 0:16]), T.H[:], A.mult, ["offb", "repk", "H"], ["Q"])
+    ts(T.l1[:], T.vy[:], 256.0, None, A.add, None, ["vy"], ["l1"])
+    op("qs", lambda s: s.activation(T.ev[:], T.valt[:, 0:272].indirect(T.l1[:, 0:16]), F.Copy), ["val0", "val1", "l1"], ["ev"])
+    mm(T.ps4[:, 0:16], T.Id[:], T.hs[:, 16:32], True, False, ["Id", "hsw"], ["ps4"])
+    mm(T.ps4[:, 0:16], T.Id[:], T.lz[:], False, False, ["Id", "lz"], [])
+    for k in range(16):
+        mm(T.ps4[:, 0:16], T.Id[:], T.Q[:, 16 * k:16 * k + 16], False, k == 15, ["Q"], ["ps4"] if k == 15 else [])
+    ts(T.par[:], T.Ri[:], 1, None, A.bitwise_and, None, ["Ri"], ["par"])
+    ts(T.rb8[:], T.rli[:], 8.0, None, A.mult, None, ["rli"], ["rb8"])
+    ts(T.e1[:], T.Ri[:], 64.0, -64.0, A.mult, A.add, ["Ri"], ["e1"])
+    ts(T.sgn[:], T.par[:], -2.0, 1.0, A.mult, A.add, ["par"], ["sgn"])
+    scan(T.w8[:], T.rb[:], T.rb8[:], T.ps1[:, 1:2], ["rb", "rb8", "ps1"], ["w8"])
+    ts(T.p95[:], T.par[:], 95.0, None, A.mult, None, ["par"], ["p95"])
+    ts(T.lead[:], T.Ri[:], 0.0, None, A.is_equal, None, ["Ri"], ["lead"])
+    tt(T.E[:], T.e1[:], T.w8[:], A.add, ["e1", "w8"], ["E"])
+    ts(T.B64[:], T.BO[:], 64.0, None, A.mult, None, ["BO"], ["B64"])
+    ts(T.S15[:], T.BO[:], T.pc[:, 4:5], None, A.mult, None, ["BO", "pc4"], ["S15"])
+    ts(T.mask[:], T.Ct[:], T.pc[:, 1:2], None, A.is_equal, None, ["Ct", "pc1"], ["mask"])
+    tt(T.mt[:], T.ps4[:, 0:16], T.sgn[:], A.mult, ["ps4", "sgn"], ["mt"])
+    ms(T.send[:], -2.0, ["send"])
+    tt(T.m[:], T.mt[:], T.p95[:], A.add, ["mt", "p95"], ["m"])
+    ms(T.zer[:], 0.0, ["zer"])
+    ms(T.Y[:, 0:1024], -2.0, ["Y"])
+
+    arr = arrivals(cores, rank, True, topo)
+    if arr:
+        for i, (s, k) in enumerate(arr):
+            note(("h%d" % s, k), [], ["l1_%d" % s])
+        for i, (s, k) in enumerate(arr):
+            last = i == len(arr) - 1
+            if s == rank - 1:
+                mm(T.ps6[:, 0:1], T.S15[:], T.land1[:, 32 * s + 31:32 * s + 32], True, True, ["S15", "l1_%d" % s], ["ps6"])
+            mm(T.ps5[:, 0:1], T.B64[:], T.land1[:, 32 * s + 15:32 * s + 16], i == 0, last,
+               ["B64", "l1_%d" % s], ["ps5"] if last else [])
+        ts(T.Aq[:], T.lead[:], T.ps6[:, 0:1], T.ps5[:, 0:1], A.mult, A.add, ["lead", "ps6", "ps5"], ["Aq"])
+        ts(T.ci[:], T.ps5[:, 0:1], -64.0, None, A.add, None, ["ps5"], ["ci"])
+        tt(T.Zi[:], T.Aq[:], T.E[:], A.add, ["Aq", "E"], ["Zi"])
+        ts(T.c2[:], T.ci[:], 6, 0xFFF0, A.logical_shift_right, A.bitwise_and, ["ci"], ["c2"])
+    else:
+        cp(T.Zi[:], T.E[:], ["E"], ["Zi"])
+        ms(T.cst[:], 112.0, ["cst"])
+    ts(T.Y1[:], T.Zi[:], 6, 0xFFF0, A.logical_shift_right, A.bitwise_and, ["Zi"], ["Y1"])
+    ts(T.Y2[:], T.Zi[:], 3, 15, A.logical_shift_right, A.bitwise_and, ["Zi"], ["Y2"])
+    ts(T.D[:], T.Zi[:], 0x380, None, A.bitwise_and, None, ["Zi"], ["D"])
+    if arr:
+        ts(T.cst[:], T.c2[:], 128.0, None, A.add, None, ["c2"], ["cst"])
+    tt(T.rel0[:], T.Y1[:], T.Y2[:], A.add, ["Y1", "Y2"], ["rel0"])
+    tt(T.off[:], T.D[:], T.m[:], A.add, ["D", "m"], ["off"])
+    ts(T.rel[:], T.rel0[:], T.cst[:, 0:1], None, A.subtract, None, ["rel0", "cst"], ["rel"])
+    cp(T.off16[:], T.off[:], ["off"], ["off16"])
+    tt(T.insl[:], T.rel[:, 0:16].indirect(T.repk[:, 0:16]), T.mask[:], A.mult, ["rel", "repk", "mask"], ["insl"])
+    ts(T.send[:, 102::128], T.zer[:], T.cst[:, 0:1], None, A.add, None, ["zer", "cst", "send"], ["send"])
+    cp(T.lw[:, 0:1024].indirect(T.off16[:, 0:16]), T.insl[:], ["off16", "insl", "lw"], ["lw"])
+    for rho in range(16):
+        mm(T.ps7[:, 0:64], T.pick[:, 128 * rho:128 * rho + 128], T.lw[:, rho::16], rho == 0, rho == 15,
+           ["lw", "pick", "pickw%d" % rho], ["ps7"] if rho == 15 else [])
+    cp(T.send[:, 0:1024].indirect(T.off16[:, 0:16]), T.ev[:], ["off16", "ev", "send"], ["send"])
+    for k in range(6):
+        cp(T.send[:, 96 + k::128], T.ps7[:, k:64:8], ["ps7", "send"], ["sl%d" % k])
+
+    rd = ["send"] + ["sl%d" % k for k in range(6)]
+    need("qg", deps_of("qg", rd, []))
+    loc2 = 0
+    trs = []
+    for ds, es in plan(cores, rank, False, topo):
+        d = ds[0]
+        a = topo.addr(cores[d])
+        trs.append(RemoteDMATransfer(srcs=[T.send[:, 128 * d:128 * d + W]], dsts=[T.land[:, W * rank:W * rank + W]],
+                                     dst_ids=[DstId(rid=a[0], pnc=a[1])], dma_engine_mask=bits(es),
+                                     remote_sem=T.sem["p%d" % rank]))
+        loc2 += len(es)
+    g.remote_dma_fused(trs, local_sem=T.sem.loc2)
+
+    def place(s, buf, at, keys):
+        ts(T.Wt[:, 6 * s:6 * s + 6], buf[:, at + 96:at + 102], buf[:, at + 102:at + 103], None, A.add, None, keys, ["Wt%d" % s])
+        cp(T.Y[:, 0:YC].indirect(T.Wt[:, 6 * s:6 * s + 6]), buf[:, at:at + 96], keys + ["Wt%d" % s, "Y"], ["Y"])
+    place(rank, T.send, 128 * rank, rd)
+    for s, k in arrivals(cores, rank, False, topo):
+        note(("p%d" % s, k), [], ["in%d" % s])
+        place(s, T.land, W * s, ["in%d" % s])
+    dma("sync", T.y[:], T.Y[:, 0:1024], "dy", ["Y"], [])
+
+    g.wait_ge(T.sem.loc2, loc2)
+    if loc1:
+        g.wait_ge(T.sem.loc1, loc1)
+    need("qg", [(e, cnt[e]) for e in cnt if cnt[e]] + [("drl", 16), ("ddl", 16), ("dval", 16), ("dy", 16)])

@@ -1,90 +1,42 @@
 from concourse.bass import DstId, RemoteDMATransfer
 from concourse.mybir import AluOpType as A, ActivationFunctionType as F
 
-W = 104
-YC = 4000
+LV = 20
+BL = 272
+ST = 512
 
 SCRATCH = {
-    "J": ("sbuf", [128, 256], "int32"), "Pi": ("sbuf", [128, 1], "int32"), "pd": ("sbuf", [128, 2], "int32"),
-    "pc": ("sbuf", [128, 8], "float32"), "Kt": ("sbuf", [128, 256], "int32"), "Ct": ("sbuf", [128, 256], "int32"),
+    "Kt": ("sbuf", [128, 128], "bfloat16"), "J": ("sbuf", [128, 128], "bfloat16"), "Pi": ("sbuf", [128, 1], "int32"),
+    "K64": ("sbuf", [128, 64], "float32"), "KR": ("sbuf", [128, 64], "float32"), "VZ": ("sbuf", [128, 64], "float32"),
+    "pd": ("sbuf", [128, 2], "int32"), "pc": ("sbuf", [128, 8], "float32"),
     "BO": ("sbuf", [128, 128], "bfloat16"), "bj": ("sbuf", [128, 128], "float32"),
-    "Lo": ("sbuf", [128, 128], "bfloat16"), "Sh": ("sbuf", [128, 128], "bfloat16"), "Id": ("sbuf", [128, 128], "bfloat16"),
-    "S15": ("sbuf", [128, 128], "bfloat16"), "B64": ("sbuf", [128, 128], "bfloat16"),
-    "mask": ("sbuf", [128, 256], "bfloat16"), "seg": ("sbuf", [128, 256], "bfloat16"),
-    "repk": ("sbuf", [128, 16], "uint16"), "repr": ("sbuf", [128, 16], "uint16"),
-    "pick": ("sbuf", [128, 2048], "bfloat16"), "ones": ("sbuf", [128, 16], "bfloat16"),
+    "Lo": ("sbuf", [128, 128], "bfloat16"), "Sh": ("sbuf", [128, 128], "bfloat16"),
+    "S15": ("sbuf", [128, 128], "float32"), "S0": ("sbuf", [128, 128], "float32"), "Bk": ("sbuf", [128, 128], "float32"),
+    "ones": ("sbuf", [128, 16], "bfloat16"),
     "rli": ("sbuf", [128, 16], "int32"), "dli": ("sbuf", [128, 16], "int32"), "valt": ("sbuf", [128, 272], "bfloat16"),
-    "rb": ("sbuf", [128, 16], "bfloat16"), "z": ("sbuf", [128, 16], "bfloat16"), "hs": ("sbuf", [128, 32], "bfloat16"),
-    "rb8": ("sbuf", [128, 16], "bfloat16"), "lz": ("sbuf", [128, 16], "bfloat16"),
-    "land1": ("sbuf", [128, 256], "bfloat16"),
-    "Ri": ("sbuf", [128, 16], "int32"), "R15": ("sbuf", [128, 16], "int32"), "par": ("sbuf", [128, 16], "int32"),
-    "sgn": ("sbuf", [128, 16], "float32"), "p95": ("sbuf", [128, 16], "float32"),
-    "H": ("sbuf", [128, 256], "bfloat16"), "S": ("sbuf", [128, 256], "bfloat16"), "offb": ("sbuf", [128, 16], "bfloat16"),
-    "Q": ("sbuf", [128, 256], "bfloat16"), "mt": ("sbuf", [128, 16], "float32"), "m": ("sbuf", [128, 16], "int32"),
+    "rb": ("sbuf", [128, 16], "bfloat16"), "rw": ("sbuf", [128, 16], "bfloat16"), "z": ("sbuf", [128, 16], "bfloat16"),
+    "cz": ("sbuf", [128, 16], "bfloat16"), "w0": ("sbuf", [128, 16], "bfloat16"),
+    "e1": ("sbuf", [128, 16], "float32"), "w1": ("sbuf", [128, 16], "float32"),
+    "lv": ("sbuf", [128, 8 * LV], "float32"),
     "db": ("sbuf", [128, 16], "bfloat16"), "cd": ("sbuf", [128, 16], "bfloat16"), "vx": ("sbuf", [128, 16], "float32"),
-    "vy": ("sbuf", [128, 16], "float32"), "l1": ("sbuf", [128, 16], "uint16"), "ev": ("sbuf", [128, 256], "bfloat16"),
-    "w8": ("sbuf", [128, 16], "float32"), "e1": ("sbuf", [128, 16], "float32"), "E": ("sbuf", [128, 16], "float32"),
-    "lead": ("sbuf", [128, 16], "float32"), "Aq": ("sbuf", [128, 16], "float32"), "Zi": ("sbuf", [128, 16], "int32"),
-    "ci": ("sbuf", [128, 1], "int32"), "c2": ("sbuf", [128, 1], "int32"), "cst": ("sbuf", [128, 1], "float32"),
-    "D": ("sbuf", [128, 16], "int32"), "Y1": ("sbuf", [128, 16], "int32"), "Y2": ("sbuf", [128, 16], "int32"),
-    "off": ("sbuf", [128, 16], "int32"), "off16": ("sbuf", [128, 16], "uint16"),
-    "rel0": ("sbuf", [128, 16], "float32"), "rel": ("sbuf", [128, 16], "float32"), "insl": ("sbuf", [128, 256], "bfloat16"),
-    "lw": ("sbuf", [128, 1024], "bfloat16"), "send": ("sbuf", [128, 1024], "bfloat16"), "zer": ("sbuf", [128, 8], "float32"),
-    "land": ("sbuf", [128, 8 * W], "bfloat16"), "Wt": ("sbuf", [128, 64], "uint16"), "Y": ("sbuf", [128, YC], "bfloat16"),
-    "ps1": ("psum", [128, 512], "float32"), "ps2": ("psum", [128, 512], "float32"), "ps3": ("psum", [128, 512], "float32"),
-    "ps4": ("psum", [128, 512], "float32"), "ps5": ("psum", [128, 512], "float32"), "ps6": ("psum", [128, 512], "float32"),
-    "ps7": ("psum", [128, 512], "float32"),
+    "vy": ("sbuf", [128, 16], "float32"), "l1": ("sbuf", [128, 16], "uint16"),
+    "ev": ("sbuf", [128, 256], "bfloat16"), "pv": ("sbuf", [128, 256], "bfloat16"),
+    "bt": ("sbuf", [128, 9], "float32"), "ki": ("sbuf", [128, 8], "int32"), "k2": ("sbuf", [128, 8], "int32"),
+    "kf": ("sbuf", [128, 8], "float32"), "lead": ("sbuf", [128, 32], "float32"), "Aq": ("sbuf", [128, 32], "float32"),
+    "Zi": ("sbuf", [128, 32], "int32"), "D": ("sbuf", [128, 32], "int32"), "Y1": ("sbuf", [128, 32], "int32"),
+    "Y2": ("sbuf", [128, 32], "int32"), "s1": ("sbuf", [128, 32], "int32"), "s2": ("sbuf", [128, 32], "int32"),
+    "off": ("sbuf", [128, 32], "uint16"),
+    "WA": ("sbuf", [128, 8 * ST], "bfloat16"), "WB": ("sbuf", [128, 8 * ST], "bfloat16"),
+    "LD": ("sbuf", [128, 8 * BL + 16], "bfloat16"),
+    "vs": ("sbuf", [128, 8], "float32"), "vt": ("sbuf", [128, 8], "float32"), "vq": ("sbuf", [128, 8], "float32"),
+    "dk": ("sbuf", [128, 8], "float32"), "dl2": ("sbuf", [128, 8], "float32"),
+    "cm": ("sbuf", [128, 8 * 64], "float32"), "ac": ("sbuf", [128, 9 * 64], "float32"),
+    "Wt": ("sbuf", [128, 64], "uint16"), "Y": ("sbuf", [128, 1024], "bfloat16"),
+    "ps1": ("psum", [128, 512], "float32"), "ps2": ("psum", [128, 512], "float32"),
+    "pn": ("psum", [128, 512], "float32"), "pw": ("psum", [128, 512], "float32"), "pl": ("psum", [128, 512], "float32"),
 }
-SEMAPHORES = (["qv", "qs", "qt", "qg", "drl", "ddl", "dval", "dy", "loc1", "loc2"]
-              + ["h%d" % i for i in range(8)] + ["p%d" % i for i in range(8)])
-
-
-def split(cores, me, later, topo):
-    c = cores[me]
-    ds = [d for d in range(len(cores)) if (d > me if later else d != me)]
-    return ([d for d in ds if topo.chip(cores[d]) == topo.chip(c)], [d for d in ds if topo.chip(cores[d]) != topo.chip(c)])
-
-
-def pow2(n):
-    k = 1
-    while 2 * k <= n:
-        k *= 2
-    return k
-
-
-def plan(cores, me, later, topo):
-    near, far = split(cores, me, later, topo)
-    c = cores[me]
-    out = []
-    used = []
-    if far:
-        es = topo.engines(c, cores[far[0]])
-        used = es
-        if later:
-            out.append((far, es[:pow2(len(es))]))
-        else:
-            k = pow2(len(es) // len(far))
-            out += [([d], es[i * k:(i + 1) * k]) for i, d in enumerate(far)]
-    if near:
-        es = [e for e in topo.engines(c, cores[near[0]]) if e not in used]
-        if later:
-            out.append((near, es[:pow2(len(es))]))
-        else:
-            k = pow2(len(es) // len(near))
-            out += [([d], es[i * k:(i + 1) * k]) for i, d in enumerate(near)]
-    return out
-
-
-def arrivals(cores, me, later, topo):
-    n = len(cores)
-    got = []
-    for s in range(n):
-        if s == me or (later and s > me):
-            continue
-        for ds, es in plan(cores, s, later, topo):
-            if me in ds:
-                got.append((topo.chip(cores[s]) != topo.chip(cores[me]), s, len(es)))
-    return [(s, k) for _, s, k in sorted(got)]
+SEMAPHORES = (["qv", "qs", "qt", "qg", "drl", "ddl", "dval", "dy", "dz", "loc"]
+              + ["%s%d" % (x, i) for x in "hvab" for i in range(8)])
 
 
 def bits(es):
@@ -99,6 +51,18 @@ def rank_program(g, core, T, topo):
     if rank is None:
         return
     cores = list(T.cores)
+    n = len(cores)
+    near = [r for r in range(n) if r != rank and topo.chip(cores[r]) == topo.chip(core)]
+    home = sorted(near + [rank])
+    far = [r for r in range(n) if r not in home]
+
+    def peer_of(r):
+        return far[home.index(r)]
+    peer = peer_of(rank)
+    efar = topo.engines(core, cores[far[0]])
+    eall = topo.engines(core, cores[near[0]])
+    enear = [e for e in eall if e not in efar]
+
     q = {"qv": g.vector, "qs": g.scalar, "qt": g.tensor, "qg": g, "sync": g.sync}
     cnt = {"qv": 0, "qs": 0, "qt": 0, "qg": 0}
     seen = {e: {} for e in q}
@@ -107,18 +71,15 @@ def rank_program(g, core, T, topo):
 
     def need(e, deps):
         best = {}
-        for s, n in deps:
-            if seen[e].get(s, 0) < n:
-                best[s] = max(best.get(s, 0), n)
-        for s, n in best.items():
-            q[e].wait_ge(T.sem[s], n)
-            seen[e][s] = n
+        for s, k in deps:
+            if seen[e].get(s, 0) < k:
+                best[s] = max(best.get(s, 0), k)
+        for s, k in best.items():
+            q[e].wait_ge(T.sem[s], k)
+            seen[e][s] = k
 
     def deps_of(e, r, w):
-        d = []
-        for k in list(r) + list(w):
-            if k in lastw:
-                d.append(lastw[k])
+        d = [lastw[k] for k in list(r) + list(w) if k in lastw]
         for k in w:
             d += [x for x in readers.get(k, []) if x[0] != e]
         return d
@@ -156,158 +117,161 @@ def rank_program(g, core, T, topo):
     def ms(ap, c, w):
         op("qv", lambda v: v.memset(ap, c), [], w)
 
-    def mm(out, l, rh, st, sp, r, w):
-        op("qt", lambda t: t.matmul(out, l, rh, st, sp), r, w)
+    def mm(out, l, rh, r, w):
+        op("qt", lambda t: t.matmul(out, l, rh, True, True), r, w)
 
     def scan(out, a, b, init, r, w):
         op("qv", lambda v: v.tensor_tensor_scan(out, a, b, init, A.mult, A.add), r, w)
+
+    loc = [0]
+
+    def send(parts, r):
+        need("qg", deps_of("qg", r, []))
+        trs = []
+        for src, dst, ds, es, sem in parts:
+            ad = [topo.addr(cores[d]) for d in ds]
+            trs.append(RemoteDMATransfer(srcs=[src], dsts=[dst for d in ds], dst_ids=[DstId(rid=a[0], pnc=a[1]) for a in ad],
+                                         dma_engine_mask=bits(es), remote_sem=T.sem[sem]))
+            loc[0] += len(es)
+        g.remote_dma_fused(trs, local_sem=T.sem.loc)
 
     dma("sync", T.rli[:], T.rl[:], "drl", [], ["rli"])
     dma("qs", T.dli[:], T.dl[:], "ddl", [], ["dli"])
     dma("sync", T.valt[:, 0:256], T.val[:], "dval", [], ["val0"])
 
     op("qg", lambda x: x.iota(T.Pi[:], [[0, 1]], 0, 1), [], ["Pi"])
-    op("qg", lambda x: x.iota(T.J[:], [[1, 256]], 0, 0), [], ["J"])
+    op("qg", lambda x: x.iota(T.Kt[:], [[1, 8], [0, 16]], 0, 0, allow_small_or_imprecise_dtypes=True), [], ["Kt"])
+    op("qg", lambda x: x.iota(T.J[:], [[1, 128]], 0, 0, allow_small_or_imprecise_dtypes=True), [], ["J"])
+    op("qg", lambda x: x.iota(T.K64[:], [[16, 64]], 0, 0, allow_small_or_imprecise_dtypes=True), [], ["K64"])
     ms(T.ones[:], 1.0, ["ones"])
     ms(T.valt[:, 256:272], -1.0, ["val1"])
-    ms(T.pick[:], 0.0, ["pick"])
+    ms(T.bt[:, 0:1], -256.0, ["bt0"])
+    ms(T.kf[:, 0:1], -16.0, ["kf0"])
+    ms(T.LD[:, 8 * BL:8 * BL + 16], -2.0, ["LDend"])
+    for d in home[:3]:
+        ms(T.WA[:, ST * d:ST * d + BL], -2.0, ["WA"])
     ts(T.pd[:, 0:1], T.Pi[:], 4, None, A.logical_shift_right, None, ["Pi"], ["pd0"])
     ts(T.pd[:, 1:2], T.Pi[:], 15, None, A.bitwise_and, None, ["Pi"], ["pd1"])
-    ts(T.Kt[:], T.J[:], 4, None, A.logical_shift_right, None, ["J"], ["Kt"])
-    cp(T.pc[:, 0:1], T.pd[:, 0:1], ["pd0"], ["pc0"])
     cp(T.pc[:, 2:3], T.Pi[:], ["Pi"], ["pc2"])
     ts(T.pc[:, 3:4], T.Pi[:], 1.0, None, A.add, None, ["Pi"], ["pc3"])
-    ts(T.BO[:], T.Kt[:, 0:128], T.pc[:, 0:1], None, A.is_equal, None, ["Kt", "pc0"], ["BO"])
-    cp(T.pc[:, 1:2], T.pd[:, 1:2], ["pd1"], ["pc1"])
-    ts(T.pc[:, 4:5], T.pd[:, 1:2], 15.0, 8.0, A.is_equal, A.mult, ["pd1"], ["pc4"])
-    tt(T.bj[:], T.BO[:], T.J[:, 0:128], A.mult, ["BO", "J"], ["bj"])
+    cp(T.pc[:, 0:1], T.pd[:, 0:1], ["pd0"], ["pc0"])
+    ts(T.pc[:, 4:5], T.pd[:, 1:2], 15.0, 32.0, A.is_equal, A.mult, ["pd1"], ["pc4"])
+    ts(T.BO[:], T.Kt[:], T.pc[:, 0:1], None, A.is_equal, None, ["Kt", "pc0"], ["BO"])
+    tt(T.bj[:], T.BO[:], T.J[:], A.mult, ["BO", "J"], ["bj"])
+    ts(T.Bk[:], T.BO[:], 256.0, None, A.mult, None, ["BO"], ["Bk"])
     ts(T.Lo[:], T.bj[:], T.pc[:, 2:3], None, A.is_gt, None, ["bj", "pc2"], ["Lo"])
-    ts(T.Sh[:], T.bj[:], T.pc[:, 3:4], 8.0, A.is_equal, A.mult, ["bj", "pc3"], ["Sh"])
-    for rho in range(16):
-        op("qs", lambda s: s.activation(T.pick[:, 129 * rho:128 * (rho + 1):16], T.BO[:, rho::16], F.Copy),
-           ["BO", "pick"], ["pickw%d" % rho])
+    ts(T.Sh[:], T.bj[:], T.pc[:, 3:4], 32.0, A.is_equal, A.mult, ["bj", "pc3"], ["Sh"])
 
-    cp(T.rb[:], T.rli[:], ["rli"], ["rb"])
+    at = LV * rank
     ts(T.z[:], T.rli[:], -1.0, 1.0, A.mult, A.add, ["rli"], ["z"])
-    scan(T.hs[:, 16:32], T.rb[:], T.rb[:], 0.0, ["rb"], ["hsw"])
-    scan(T.hs[:, 0:16], T.ones[:], T.z[:], 0.0, ["ones", "z"], ["hsz"])
-    pl = plan(cores, rank, True, topo)
-    loc1 = 0
-    if pl:
-        need("qg", deps_of("qg", ["hsw", "hsz"], []))
-        trs = []
-        for ds, es in pl:
-            adr = [topo.addr(cores[d]) for d in ds]
-            trs.append(RemoteDMATransfer(srcs=[T.hs[:]], dsts=[T.land1[:, 32 * rank:32 * rank + 32] for d in ds],
-                                         dst_ids=[DstId(rid=a[0], pnc=a[1]) for a in adr],
-                                         dma_engine_mask=bits(es), remote_sem=T.sem["h%d" % rank]))
-            loc1 += len(es)
-        g.remote_dma_fused(trs, local_sem=T.sem.loc1)
-    op("qg", lambda x: x.iota(T.lw[:], [[0, 8], [1, 128]], 80, 0, allow_small_or_imprecise_dtypes=True), [], ["lw"])
-
-    mm(T.ps1[:, 0:1], T.Lo[:], T.hs[:, 15:16], True, True, ["Lo", "hsz"], ["ps1"])
-    mm(T.ps1[:, 1:2], T.Sh[:], T.hs[:, 31:32], True, True, ["Sh", "hsw"], ["ps1"])
-    ts(T.seg[:], T.J[:], 15, None, A.bitwise_and, None, ["J"], ["Ct"]) if False else \
-        ts(T.Ct[:], T.J[:], 15, None, A.bitwise_and, None, ["J"], ["Ct"])
-    ts(T.repr[:], T.J[:, 0:16], 0.0, T.pc[:, 1:2], A.mult, A.add, ["J", "pc1"], ["repr"])
-    ts(T.Ri[:], T.hs[:, 0:16], T.ps1[:, 0:1], None, A.add, None, ["hsz", "ps1"], ["Ri"])
-    ts(T.seg[:], T.Ct[:], 0.0, None, A.is_gt, None, ["Ct"], ["seg"])
-    ts(T.R15[:], T.Ri[:], 15, None, A.bitwise_and, None, ["Ri"], ["R15"])
-    cp(T.repk[:], T.J[:, 0:16], ["J"], ["repk"])
+    cp(T.rb[:], T.rli[:], ["rli"], ["rb"])
+    scan(T.cz[:], T.ones[:], T.z[:], 0.0, ["ones", "z"], ["cz"])
+    scan(T.w0[:], T.rb[:], T.rb[:], 0.0, ["rb"], ["w0"])
+    mm(T.ps1[:, 0:1], T.Lo[:], T.cz[:, 15:16], ["Lo", "cz"], ["ps1"])
+    mm(T.ps1[:, 1:2], T.Sh[:], T.w0[:, 15:16], ["Sh", "w0"], ["ps1"])
+    ts(T.rw[:], T.rb[:], 32.0, None, A.mult, None, ["rb"], ["rw"])
+    cp(T.lv[:, at + 16:at + 17], T.cz[:, 15:16], ["cz"], ["lva"])
+    cp(T.lv[:, at + 17:at + 18], T.w0[:, 15:16], ["w0"], ["lvb"])
+    cp(T.lv[:, at + 18:at + 19], T.rb[:, 0:1], ["rb"], ["lvc"])
+    ts(T.e1[:], T.cz[:], T.ps1[:, 0:1], 256.0, A.add, A.mult, ["cz", "ps1"], ["e1"])
+    scan(T.w1[:], T.rb[:], T.rw[:], T.ps1[:, 1:2], ["rb", "rw", "ps1"], ["w1"])
     cp(T.db[:], T.dli[:], ["dli"], ["db"])
-    tt(T.H[:], T.R15[:, 0:16].indirect(T.repr[:, 0:16]), T.Kt[:], A.is_equal, ["R15", "repr", "Kt"], ["H"])
+    tt(T.lv[:, at:at + 16], T.e1[:], T.w1[:], A.add, ["e1", "w1"], ["E%d" % rank])
+    own = ["lva", "lvb", "lvc", "E%d" % rank]
+    sl = T.lv[:, at:at + 19]
+    send([(sl, sl, far, efar, "h%d" % rank), (sl, sl, near, enear, "h%d" % rank)], own)
+
     scan(T.cd[:], T.ones[:], T.db[:], 0.0, ["ones", "db"], ["cd"])
-    scan(T.S[:], T.seg[:], T.H[:], 0.0, ["seg", "H"], ["S"])
-    mm(T.ps2[:, 0:1], T.Lo[:], T.cd[:, 15:16], True, True, ["Lo", "cd"], ["ps2"])
-    mm(T.ps3[:, 0:16], T.Lo[:], T.S[:, 15::16], True, True, ["Lo", "S"], ["ps3"])
+    mm(T.ps2[:, 0:1], T.Lo[:], T.cd[:, 15:16], ["Lo", "cd"], ["ps2"])
+    ts(T.S15[:], T.BO[:], T.pc[:, 4:5], None, A.mult, None, ["BO", "pc4"], ["S15"])
     ts(T.vx[:], T.cd[:], T.ps2[:, 0:1], -257.0, A.add, A.add, ["cd", "ps2"], ["vx"])
-    ts(T.Id[:], T.J[:, 0:128], T.pc[:, 2:3], None, A.is_equal, None, ["J", "pc2"], ["Id"])
-    cp(T.offb[:], T.ps3[:, 0:16], ["ps3"], ["offb"])
     tt(T.vy[:], T.vx[:], T.db[:], A.mult, ["vx", "db"], ["vy"])
-    ts(T.lz[:], T.hs[:, 0:16], 0.0, -1.0, A.is_equal, A.mult, ["hsz"], ["lz"])
-    tt(T.Q[:], T.offb[:, 0:16].indirect(T.repk[:, 0:16]), T.H[:], A.mult, ["offb", "repk", "H"], ["Q"])
     ts(T.l1[:], T.vy[:], 256.0, None, A.add, None, ["vy"], ["l1"])
     op("qs", lambda s: s.activation(T.ev[:], T.valt[:, 0:272].indirect(T.l1[:, 0:16]), F.Copy), ["val0", "val1", "l1"], ["ev"])
-    mm(T.ps4[:, 0:16], T.Id[:], T.hs[:, 16:32], True, False, ["Id", "hsw"], ["ps4"])
-    mm(T.ps4[:, 0:16], T.Id[:], T.lz[:], False, False, ["Id", "lz"], [])
-    for k in range(16):
-        mm(T.ps4[:, 0:16], T.Id[:], T.Q[:, 16 * k:16 * k + 16], False, k == 15, ["Q"], ["ps4"] if k == 15 else [])
-    ts(T.par[:], T.Ri[:], 1, None, A.bitwise_and, None, ["Ri"], ["par"])
-    ts(T.rb8[:], T.rli[:], 8.0, None, A.mult, None, ["rli"], ["rb8"])
-    ts(T.e1[:], T.Ri[:], 64.0, -64.0, A.mult, A.add, ["Ri"], ["e1"])
-    ts(T.sgn[:], T.par[:], -2.0, 1.0, A.mult, A.add, ["par"], ["sgn"])
-    scan(T.w8[:], T.rb[:], T.rb8[:], T.ps1[:, 1:2], ["rb", "rb8", "ps1"], ["w8"])
-    ts(T.p95[:], T.par[:], 95.0, None, A.mult, None, ["par"], ["p95"])
-    ts(T.lead[:], T.Ri[:], 0.0, None, A.is_equal, None, ["Ri"], ["lead"])
-    tt(T.E[:], T.e1[:], T.w8[:], A.add, ["e1", "w8"], ["E"])
-    ts(T.B64[:], T.BO[:], 64.0, None, A.mult, None, ["BO"], ["B64"])
-    ts(T.S15[:], T.BO[:], T.pc[:, 4:5], None, A.mult, None, ["BO", "pc4"], ["S15"])
-    ts(T.mask[:], T.Ct[:], T.pc[:, 1:2], None, A.is_equal, None, ["Ct", "pc1"], ["mask"])
-    tt(T.mt[:], T.ps4[:, 0:16], T.sgn[:], A.mult, ["ps4", "sgn"], ["mt"])
-    ms(T.send[:], -2.0, ["send"])
-    tt(T.m[:], T.mt[:], T.p95[:], A.add, ["mt", "p95"], ["m"])
-    ms(T.zer[:], 0.0, ["zer"])
-    ms(T.Y[:, 0:1024], -2.0, ["Y"])
+    send([(T.ev[:], T.pv[:], [peer], efar, "v%d" % rank)], ["ev"])
 
-    arr = arrivals(cores, rank, True, topo)
-    if arr:
-        for i, (s, k) in enumerate(arr):
-            note(("h%d" % s, k), [], ["l1_%d" % s])
-        for i, (s, k) in enumerate(arr):
-            last = i == len(arr) - 1
-            if s == rank - 1:
-                mm(T.ps6[:, 0:1], T.S15[:], T.land1[:, 32 * s + 31:32 * s + 32], True, True, ["S15", "l1_%d" % s], ["ps6"])
-            mm(T.ps5[:, 0:1], T.B64[:], T.land1[:, 32 * s + 15:32 * s + 16], i == 0, last,
-               ["B64", "l1_%d" % s], ["ps5"] if last else [])
-        ts(T.Aq[:], T.lead[:], T.ps6[:, 0:1], T.ps5[:, 0:1], A.mult, A.add, ["lead", "ps6", "ps5"], ["Aq"])
-        ts(T.ci[:], T.ps5[:, 0:1], -64.0, None, A.add, None, ["ps5"], ["ci"])
-        tt(T.Zi[:], T.Aq[:], T.E[:], A.add, ["Aq", "E"], ["Zi"])
-        ts(T.c2[:], T.ci[:], 6, 0xFFF0, A.logical_shift_right, A.bitwise_and, ["ci"], ["c2"])
-    else:
-        cp(T.Zi[:], T.E[:], ["E"], ["Zi"])
-        ms(T.cst[:], 112.0, ["cst"])
-    ts(T.Y1[:], T.Zi[:], 6, 0xFFF0, A.logical_shift_right, A.bitwise_and, ["Zi"], ["Y1"])
-    ts(T.Y2[:], T.Zi[:], 3, 15, A.logical_shift_right, A.bitwise_and, ["Zi"], ["Y2"])
-    ts(T.D[:], T.Zi[:], 0x380, None, A.bitwise_and, None, ["Zi"], ["D"])
-    if arr:
-        ts(T.cst[:], T.c2[:], 128.0, None, A.add, None, ["c2"], ["cst"])
-    tt(T.rel0[:], T.Y1[:], T.Y2[:], A.add, ["Y1", "Y2"], ["rel0"])
-    tt(T.off[:], T.D[:], T.m[:], A.add, ["D", "m"], ["off"])
-    ts(T.rel[:], T.rel0[:], T.cst[:, 0:1], None, A.subtract, None, ["rel0", "cst"], ["rel"])
-    cp(T.off16[:], T.off[:], ["off"], ["off16"])
-    tt(T.insl[:], T.rel[:, 0:16].indirect(T.repk[:, 0:16]), T.mask[:], A.mult, ["rel", "repk", "mask"], ["insl"])
-    ts(T.send[:, 102::128], T.zer[:], T.cst[:, 0:1], None, A.add, None, ["zer", "cst", "send"], ["send"])
-    cp(T.lw[:, 0:1024].indirect(T.off16[:, 0:16]), T.insl[:], ["off16", "insl", "lw"], ["lw"])
-    for rho in range(16):
-        mm(T.ps7[:, 0:64], T.pick[:, 128 * rho:128 * rho + 128], T.lw[:, rho::16], rho == 0, rho == 15,
-           ["lw", "pick", "pickw%d" % rho], ["ps7"] if rho == 15 else [])
-    cp(T.send[:, 0:1024].indirect(T.off16[:, 0:16]), T.ev[:], ["off16", "ev", "send"], ["send"])
-    for k in range(6):
-        cp(T.send[:, 96 + k::128], T.ps7[:, k:64:8], ["ps7", "send"], ["sl%d" % k])
+    ts(T.pc[:, 5:6], T.pd[:, 1:2], 0.0, None, A.is_equal, None, ["pd1"], ["pc5"])
+    ts(T.pc[:, 6:7], T.pd[:, 1:2], 16.0, None, A.add, None, ["pd1"], ["pc6"])
+    ts(T.pc[:, 7:8], T.pd[:, 1:2], 32.0, 512.0 * rank - 256.0, A.mult, A.add, ["pd1"], ["pc7"])
+    ts(T.S0[:], T.BO[:], T.pc[:, 5:6], None, A.mult, None, ["BO", "pc5"], ["S0"])
+    ts(T.KR[:], T.K64[:], T.pc[:, 6:7], None, A.add, None, ["K64", "pc6"], ["KR"])
+    ts(T.VZ[:], T.K64[:], 256.0, T.pc[:, 7:8], A.mult, A.add, ["K64", "pc7"], ["VZ"])
+    for d in home[3:]:
+        ms(T.WA[:, ST * d:ST * d + BL], -2.0, ["WA"])
+    for d in home:
+        ms(T.WB[:, ST * d:ST * d + BL], -2.0, ["WB"])
+    ts(T.lead[:, 0:16], T.lv[:, at:at + 16], 256.0, None, A.is_lt, None, ["E%d" % rank], ["lead0"])
 
-    rd = ["send"] + ["sl%d" % k for k in range(6)]
-    need("qg", deps_of("qg", rd, []))
-    loc2 = 0
-    trs = []
-    for ds, es in plan(cores, rank, False, topo):
-        d = ds[0]
-        a = topo.addr(cores[d])
-        trs.append(RemoteDMATransfer(srcs=[T.send[:, 128 * d:128 * d + W]], dsts=[T.land[:, W * rank:W * rank + W]],
-                                     dst_ids=[DstId(rid=a[0], pnc=a[1])], dma_engine_mask=bits(es),
-                                     remote_sem=T.sem["p%d" % rank]))
-        loc2 += len(es)
-    g.remote_dma_fused(trs, local_sem=T.sem.loc2)
+    for s in near:
+        note(("h%d" % s, len(enear)), [], ["E%d" % s])
+    for s in far:
+        note(("h%d" % s, len(efar)), [], ["E%d" % s])
+    note(("v%d" % peer, len(efar)), [], ["pv"])
+    every = ["E%d" % s for s in near + far] + own
+    mm(T.pn[:, 0:8], T.Bk[:], T.lv[:, 16:8 * LV:LV], every + ["Bk"], ["pn"])
+    mm(T.pw[:, 0:8], T.S15[:], T.lv[:, 17:8 * LV:LV], every + ["S15"], ["pw"])
+    mm(T.pl[:, 0:8], T.S0[:], T.lv[:, 18:8 * LV:LV], every + ["S0"], ["pl"])
 
-    def place(s, buf, at, keys):
-        ts(T.Wt[:, 6 * s:6 * s + 6], buf[:, at + 96:at + 102], buf[:, at + 102:at + 103], None, A.add, None, keys, ["Wt%d" % s])
-        cp(T.Y[:, 0:YC].indirect(T.Wt[:, 6 * s:6 * s + 6]), buf[:, at:at + 96], keys + ["Wt%d" % s, "Y"], ["Y"])
-    place(rank, T.send, 128 * rank, rd)
-    for s, k in arrivals(cores, rank, False, topo):
-        note(("p%d" % s, k), [], ["in%d" % s])
-        place(s, T.land, W * s, ["in%d" % s])
-    dma("sync", T.y[:], T.Y[:, 0:1024], "dy", ["Y"], [])
+    pa = LV * peer
+    ts(T.lead[:, 16:32], T.lv[:, pa:pa + 16], 256.0, None, A.is_lt, None, ["E%d" % peer], ["lead1"])
+    scan(T.bt[:, 1:9], T.ones[:, 0:8], T.pn[:, 0:8], -256.0, ["ones", "pn"], ["bt"])
+    pages = [rank, peer]
+    for i, p in enumerate(pages):
+        ts(T.Aq[:, 16 * i:16 * i + 16], T.lead[:, 16 * i:16 * i + 16], T.pw[:, p - 1:p] if p else 0.0, T.bt[:, p:p + 1],
+           A.mult, A.add, ["lead%d" % i, "pw", "bt", "bt0"], ["A%d" % i])
+    cp(T.ki[:, 1:8], T.bt[:, 1:8], ["bt"], ["ki"])
+    for i, p in enumerate(pages):
+        tt(T.Zi[:, 16 * i:16 * i + 16], T.Aq[:, 16 * i:16 * i + 16], T.lv[:, LV * p:LV * p + 16], A.add,
+           ["A%d" % i, "E%d" % p], ["Z%d" % i])
+    ts(T.k2[:, 1:8], T.ki[:, 1:8], 8, 0xFFF0, A.logical_shift_right, A.bitwise_and, ["ki"], ["k2"])
+    zk = ["Z0", "Z1"]
+    ts(T.Y1[:], T.Zi[:], 8, 0xFFF0, A.logical_shift_right, A.bitwise_and, zk, ["Y1"])
+    ts(T.Y2[:], T.Zi[:], 5, 15, A.logical_shift_right, A.bitwise_and, zk, ["Y2"])
+    ts(T.D[:], T.Zi[:], 0xE00, None, A.bitwise_and, None, zk, ["D"])
+    tt(T.s1[:], T.Y1[:], T.Y2[:], A.add, ["Y1", "Y2"], ["s1"])
+    cp(T.kf[:, 1:8], T.k2[:, 1:8], ["k2"], ["kf"])
+    tt(T.s2[:], T.s1[:], T.D[:], A.add, ["s1", "D"], ["s2"])
+    for i, p in enumerate(pages):
+        ts(T.off[:, 16 * i:16 * i + 16], T.s2[:, 16 * i:16 * i + 16], T.kf[:, p:p + 1], None, A.subtract, None,
+           ["s2", "kf", "kf0"], ["off%d" % i])
+    k = len(eall) // 4
+    for i, (win, val, vk, tag) in enumerate([(T.WA, T.ev, "ev", "a"), (T.WB, T.pv, "pv", "b")]):
+        wk = "WA" if i == 0 else "WB"
+        cp(win[:, 0:8 * ST].indirect(T.off[:, 16 * i:16 * i + 16]), val[:], ["off%d" % i, vk, wk], [wk])
+        p = pages[i]
+        send([(win[:, ST * d:ST * d + BL], T.LD[:, BL * p:BL * p + BL], [d],
+               [eall[(k * (j + i) + x) % len(eall)] for x in range(k)], "%s%d" % (tag, rank)) for j, d in enumerate(near)], [wk])
 
-    g.wait_ge(T.sem.loc2, loc2)
-    if loc1:
-        g.wait_ge(T.sem.loc1, loc1)
-    need("qg", [(e, cnt[e]) for e in cnt if cnt[e]] + [("drl", 16), ("ddl", 16), ("dval", 16), ("dy", 16)])
+    ts(T.vs[:, 0:7], T.pw[:, 0:7], -224.0, None, A.add, None, ["pw"], ["vs"])
+    tt(T.dk[:, 0:7], T.kf[:, 0:7], T.kf[:, 1:8], A.subtract, ["kf", "kf0"], ["dk"])
+    tt(T.vt[:, 0:7], T.vs[:, 0:7], T.pl[:, 1:8], A.mult, ["vs", "pl"], ["vt"])
+    ts(T.dl2[:, 0:7], T.dk[:, 0:7], float(BL), None, A.add, None, ["dk"], ["dl2"])
+    tt(T.vq[:, 0:7], T.vt[:, 0:7], T.bt[:, 1:8], A.add, ["vt", "bt"], ["vq"])
+    for x in range(8):
+        lim = T.vq[:, x:x + 1] if x < 7 else T.bt[:, 8:9]
+        ts(T.cm[:, 64 * x:64 * x + 64], T.VZ[:], lim, T.dl2[:, x:x + 1] if x < 7 else 16384.0, A.is_ge, A.mult,
+           ["VZ", "vq", "bt", "dl2"], ["cm%d" % x])
+    cm = [T.cm[:, 64 * x:64 * x + 64] for x in range(8)]
+    ac = [T.ac[:, 64 * x:64 * x + 64] for x in range(8)]
+    for x in range(4):
+        tt(ac[x], cm[2 * x], cm[2 * x + 1], A.add, ["cm%d" % (2 * x), "cm%d" % (2 * x + 1)], ["ac%d" % x])
+    for x in range(2):
+        tt(ac[4 + x], ac[2 * x], ac[2 * x + 1], A.add, ["ac%d" % (2 * x), "ac%d" % (2 * x + 1)], ["ac%d" % (4 + x)])
+    for i, (win, wk) in enumerate([(T.WA, "WA"), (T.WB, "WB")]):
+        p = pages[i]
+        cp(T.LD[:, BL * p:BL * p + BL], win[:, ST * rank:ST * rank + BL], [wk], ["L%d" % p])
+    tt(ac[6], ac[4], T.KR[:], A.add, ["ac4", "KR"], ["ac6"])
+    tt(ac[7], ac[6], ac[5], A.add, ["ac6", "ac5"], ["ac7"])
+    ts(T.Wt[:], ac[7], float(8 * BL), None, A.min, None, ["ac7"], ["Wt"])
+
+    for s in near:
+        note(("a%d" % s, k), [], ["L%d" % s])
+        note(("b%d" % s, k), [], ["L%d" % peer_of(s)])
+    rd = ["L%d" % s for s in home + far] + ["LDend", "Wt"]
+    op("qs", lambda s: s.activation(T.Y[:, 512:1024], T.LD[:, 0:8 * BL + 16].indirect(T.Wt[:, 32:64]), F.Copy), rd, ["Yb"])
+    cp(T.Y[:, 0:512], T.LD[:, 0:8 * BL + 16].indirect(T.Wt[:, 0:32]), rd, ["Ya"])
+    dma("qs", T.y[:, 512:1024], T.Y[:, 512:1024], "dz", ["Yb"], [])
+    dma("sync", T.y[:, 0:512], T.Y[:, 0:512], "dy", ["Ya"], [])
+
+    g.wait_ge(T.sem.loc, loc[0])
+    need("qg", [(e, cnt[e]) for e in cnt if cnt[e]] + [(s, 16) for s in ("drl", "ddl", "dval", "dy", "dz")])

@@ -1,28 +1,29 @@
 from concourse.bass import DstId, RemoteDMATransfer
 from concourse.mybir import AluOpType as A, ActivationFunctionType as F
 
-LV = 20
+LV = 56
+LW = 50
 BL = 272
 ST = 512
+RND = 12582912.0
 
 SCRATCH = {
     "Kt": ("sbuf", [128, 128], "bfloat16"), "J": ("sbuf", [128, 128], "bfloat16"), "Pi": ("sbuf", [128, 1], "int32"),
-    "K64": ("sbuf", [128, 64], "float32"), "KR": ("sbuf", [128, 64], "float32"), "VZ": ("sbuf", [128, 64], "float32"),
+    "VZ": ("sbuf", [128, 64], "float32"), "Id": ("sbuf", [128, 128], "bfloat16"),
     "pd": ("sbuf", [128, 2], "int32"), "pc": ("sbuf", [128, 8], "float32"),
-    "BO": ("sbuf", [128, 128], "bfloat16"), "bj": ("sbuf", [128, 128], "float32"),
+    "BO": ("sbuf", [128, 128], "bfloat16"), "bj": ("sbuf", [128, 128], "bfloat16"),
     "Lo": ("sbuf", [128, 128], "bfloat16"), "Sh": ("sbuf", [128, 128], "bfloat16"),
-    "S15": ("sbuf", [128, 128], "float32"), "S0": ("sbuf", [128, 128], "float32"), "Bk": ("sbuf", [128, 128], "float32"),
-    "ones": ("sbuf", [128, 16], "bfloat16"),
+    "S15": ("sbuf", [128, 128], "bfloat16"), "S0": ("sbuf", [128, 128], "bfloat16"), "Bk": ("sbuf", [128, 128], "bfloat16"),
+    "ones": ("sbuf", [128, 16], "bfloat16"), "neg": ("sbuf", [128, 16], "bfloat16"), "neg2": ("sbuf", [128, 16], "bfloat16"),
     "rli": ("sbuf", [128, 16], "int32"), "dli": ("sbuf", [128, 16], "int32"), "valt": ("sbuf", [128, 272], "bfloat16"),
     "rb": ("sbuf", [128, 16], "bfloat16"), "rw": ("sbuf", [128, 16], "bfloat16"), "z": ("sbuf", [128, 16], "bfloat16"),
     "cz": ("sbuf", [128, 16], "bfloat16"), "w0": ("sbuf", [128, 16], "bfloat16"),
-    "e1": ("sbuf", [128, 16], "float32"), "w1": ("sbuf", [128, 16], "float32"),
-    "lv": ("sbuf", [128, 8 * LV], "float32"),
+    "lv": ("sbuf", [128, 8 * LV], "bfloat16"),
     "db": ("sbuf", [128, 16], "bfloat16"), "cd": ("sbuf", [128, 16], "bfloat16"), "vx": ("sbuf", [128, 16], "float32"),
     "vy": ("sbuf", [128, 16], "float32"), "l1": ("sbuf", [128, 16], "uint16"),
     "ev": ("sbuf", [128, 256], "bfloat16"), "pv": ("sbuf", [128, 256], "bfloat16"),
-    "bt": ("sbuf", [128, 9], "float32"), "ki": ("sbuf", [128, 8], "int32"), "k2": ("sbuf", [128, 8], "int32"),
-    "kf": ("sbuf", [128, 8], "float32"), "lead": ("sbuf", [128, 32], "float32"), "Aq": ("sbuf", [128, 32], "float32"),
+    "kr": ("sbuf", [128, 8], "float32"), "kf": ("sbuf", [128, 8], "float32"), "lead": ("sbuf", [128, 32], "float32"),
+    "X1": ("sbuf", [128, 32], "float32"), "X2": ("sbuf", [128, 32], "float32"),
     "Zi": ("sbuf", [128, 32], "int32"), "D": ("sbuf", [128, 32], "int32"), "Y1": ("sbuf", [128, 32], "int32"),
     "Y2": ("sbuf", [128, 32], "int32"), "s1": ("sbuf", [128, 32], "int32"), "s2": ("sbuf", [128, 32], "int32"),
     "off": ("sbuf", [128, 32], "uint16"),
@@ -30,10 +31,11 @@ SCRATCH = {
     "LD": ("sbuf", [128, 8 * BL + 16], "bfloat16"),
     "vs": ("sbuf", [128, 8], "float32"), "vt": ("sbuf", [128, 8], "float32"), "vq": ("sbuf", [128, 8], "float32"),
     "dk": ("sbuf", [128, 8], "float32"), "dl2": ("sbuf", [128, 8], "float32"),
-    "cm": ("sbuf", [128, 8 * 64], "float32"), "ac": ("sbuf", [128, 9 * 64], "float32"),
+    "cm": ("sbuf", [128, 8 * 64], "bfloat16"),
     "Wt": ("sbuf", [128, 64], "uint16"), "Y": ("sbuf", [128, 1024], "bfloat16"),
     "ps1": ("psum", [128, 512], "float32"), "ps2": ("psum", [128, 512], "float32"),
-    "pn": ("psum", [128, 512], "float32"), "pw": ("psum", [128, 512], "float32"), "pl": ("psum", [128, 512], "float32"),
+    "pb": ("psum", [128, 512], "float32"), "pw": ("psum", [128, 512], "float32"), "pl": ("psum", [128, 512], "float32"),
+    "pz": ("psum", [128, 512], "float32"), "pe": ("psum", [128, 512], "float32"), "pk": ("psum", [128, 512], "float32"),
 }
 SEMAPHORES = (["qv", "qs", "qt", "qg", "drl", "ddl", "dval", "dy", "dz", "loc"]
               + ["%s%d" % (x, i) for x in "hvab" for i in range(8)])
@@ -62,6 +64,14 @@ def rank_program(g, core, T, topo):
     efar = topo.engines(core, cores[far[0]])
     eall = topo.engines(core, cores[near[0]])
     enear = [e for e in eall if e not in efar]
+
+    def shares(me, second):
+        ds = [r for r in home if r != me]
+        h = len(eall) // 2
+        one, two = eall[:h], eall[h:]
+        if second:
+            one, two = two, one
+        return {ds[0]: one, ds[1]: two[:h // 2], ds[2]: two[h // 2:]}
 
     q = {"qv": g.vector, "qs": g.scalar, "qt": g.tensor, "qg": g, "sync": g.sync}
     cnt = {"qv": 0, "qs": 0, "qt": 0, "qg": 0}
@@ -117,8 +127,8 @@ def rank_program(g, core, T, topo):
     def ms(ap, c, w):
         op("qv", lambda v: v.memset(ap, c), [], w)
 
-    def mm(out, l, rh, r, w):
-        op("qt", lambda t: t.matmul(out, l, rh, True, True), r, w)
+    def mm(out, l, rh, r, w, st=True, sp=True):
+        op("qt", lambda t: t.matmul(out, l, rh, st, sp), r, w)
 
     def scan(out, a, b, init, r, w):
         op("qv", lambda v: v.tensor_tensor_scan(out, a, b, init, A.mult, A.add), r, w)
@@ -139,14 +149,15 @@ def rank_program(g, core, T, topo):
     dma("qs", T.dli[:], T.dl[:], "ddl", [], ["dli"])
     dma("sync", T.valt[:, 0:256], T.val[:], "dval", [], ["val0"])
 
+    at = LV * rank
     op("qg", lambda x: x.iota(T.Pi[:], [[0, 1]], 0, 1), [], ["Pi"])
     op("qg", lambda x: x.iota(T.Kt[:], [[1, 8], [0, 16]], 0, 0, allow_small_or_imprecise_dtypes=True), [], ["Kt"])
     op("qg", lambda x: x.iota(T.J[:], [[1, 128]], 0, 0, allow_small_or_imprecise_dtypes=True), [], ["J"])
-    op("qg", lambda x: x.iota(T.K64[:], [[16, 64]], 0, 0, allow_small_or_imprecise_dtypes=True), [], ["K64"])
     ms(T.ones[:], 1.0, ["ones"])
+    ms(T.neg[:], -0.0625, ["neg"])
+    ms(T.neg2[:], -0.53125, ["neg2"])
     ms(T.valt[:, 256:272], -1.0, ["val1"])
-    ms(T.bt[:, 0:1], -256.0, ["bt0"])
-    ms(T.kf[:, 0:1], -16.0, ["kf0"])
+    ms(T.lv[:, at + 32:at + 40], 0.0, ["lvz"])
     ms(T.LD[:, 8 * BL:8 * BL + 16], -2.0, ["LDend"])
     for d in home[:3]:
         ms(T.WA[:, ST * d:ST * d + BL], -2.0, ["WA"])
@@ -160,113 +171,120 @@ def rank_program(g, core, T, topo):
     tt(T.bj[:], T.BO[:], T.J[:], A.mult, ["BO", "J"], ["bj"])
     ts(T.Bk[:], T.BO[:], 256.0, None, A.mult, None, ["BO"], ["Bk"])
     ts(T.Lo[:], T.bj[:], T.pc[:, 2:3], None, A.is_gt, None, ["bj", "pc2"], ["Lo"])
-    ts(T.Sh[:], T.bj[:], T.pc[:, 3:4], 32.0, A.is_equal, A.mult, ["bj", "pc3"], ["Sh"])
+    ts(T.Sh[:], T.bj[:], T.pc[:, 3:4], 2.0, A.is_equal, A.mult, ["bj", "pc3"], ["Sh"])
 
-    at = LV * rank
     ts(T.z[:], T.rli[:], -1.0, 1.0, A.mult, A.add, ["rli"], ["z"])
     cp(T.rb[:], T.rli[:], ["rli"], ["rb"])
     scan(T.cz[:], T.ones[:], T.z[:], 0.0, ["ones", "z"], ["cz"])
     scan(T.w0[:], T.rb[:], T.rb[:], 0.0, ["rb"], ["w0"])
     mm(T.ps1[:, 0:1], T.Lo[:], T.cz[:, 15:16], ["Lo", "cz"], ["ps1"])
     mm(T.ps1[:, 1:2], T.Sh[:], T.w0[:, 15:16], ["Sh", "w0"], ["ps1"])
-    ts(T.rw[:], T.rb[:], 32.0, None, A.mult, None, ["rb"], ["rw"])
-    cp(T.lv[:, at + 16:at + 17], T.cz[:, 15:16], ["cz"], ["lva"])
-    cp(T.lv[:, at + 17:at + 18], T.w0[:, 15:16], ["w0"], ["lvb"])
-    cp(T.lv[:, at + 18:at + 19], T.rb[:, 0:1], ["rb"], ["lvc"])
-    ts(T.e1[:], T.cz[:], T.ps1[:, 0:1], 256.0, A.add, A.mult, ["cz", "ps1"], ["e1"])
-    scan(T.w1[:], T.rb[:], T.rw[:], T.ps1[:, 1:2], ["rb", "rw", "ps1"], ["w1"])
-    cp(T.db[:], T.dli[:], ["dli"], ["db"])
-    tt(T.lv[:, at:at + 16], T.e1[:], T.w1[:], A.add, ["e1", "w1"], ["E%d" % rank])
-    own = ["lva", "lvb", "lvc", "E%d" % rank]
-    sl = T.lv[:, at:at + 19]
+    ts(T.rw[:], T.rb[:], 2.0, None, A.mult, None, ["rb"], ["rw"])
+    ts(T.lv[:, at + 40:at + 48], T.ones[:, 0:8], T.cz[:, 15:16], None, A.mult, None, ["cz", "ones"], ["lva"])
+    cp(T.lv[:, at + 48:at + 49], T.w0[:, 15:16], ["w0"], ["lvb"])
+    cp(T.lv[:, at + 49:at + 50], T.rb[:, 0:1], ["rb"], ["lvc"])
+    ts(T.lv[:, at:at + 16], T.cz[:, 0:16], T.ps1[:, 0:1], 16.0, A.add, A.mult, ["cz", "ps1"], ["lvr"])
+    scan(T.lv[:, at + 16:at + 32], T.rb[:], T.rw[:], T.ps1[:, 1:2], ["rb", "rw", "ps1"], ["lvw"])
+    own = ["lva", "lvb", "lvc", "lvr", "lvw", "lvz"]
+    sl = T.lv[:, at:at + LW]
     send([(sl, sl, far, efar, "h%d" % rank), (sl, sl, near, enear, "h%d" % rank)], own)
 
+    cp(T.db[:], T.dli[:], ["dli"], ["db"])
+    ts(T.S15[:], T.BO[:], T.pc[:, 4:5], None, A.mult, None, ["BO", "pc4"], ["S15"])
     scan(T.cd[:], T.ones[:], T.db[:], 0.0, ["ones", "db"], ["cd"])
     mm(T.ps2[:, 0:1], T.Lo[:], T.cd[:, 15:16], ["Lo", "cd"], ["ps2"])
-    ts(T.S15[:], T.BO[:], T.pc[:, 4:5], None, A.mult, None, ["BO", "pc4"], ["S15"])
+    ts(T.pc[:, 5:6], T.pd[:, 1:2], 0.0, None, A.is_equal, None, ["pd1"], ["pc5"])
+    ts(T.pc[:, 6:7], T.pd[:, 1:2], 16.0, None, A.add, None, ["pd1"], ["pc6"])
     ts(T.vx[:], T.cd[:], T.ps2[:, 0:1], -257.0, A.add, A.add, ["cd", "ps2"], ["vx"])
     tt(T.vy[:], T.vx[:], T.db[:], A.mult, ["vx", "db"], ["vy"])
     ts(T.l1[:], T.vy[:], 256.0, None, A.add, None, ["vy"], ["l1"])
     op("qs", lambda s: s.activation(T.ev[:], T.valt[:, 0:272].indirect(T.l1[:, 0:16]), F.Copy), ["val0", "val1", "l1"], ["ev"])
     send([(T.ev[:], T.pv[:], [peer], efar, "v%d" % rank)], ["ev"])
 
-    ts(T.pc[:, 5:6], T.pd[:, 1:2], 0.0, None, A.is_equal, None, ["pd1"], ["pc5"])
-    ts(T.pc[:, 6:7], T.pd[:, 1:2], 16.0, None, A.add, None, ["pd1"], ["pc6"])
+    ts(T.Id[:], T.J[:], T.pc[:, 2:3], 16.0, A.is_equal, A.mult, ["J", "pc2"], ["Id"])
     ts(T.pc[:, 7:8], T.pd[:, 1:2], 32.0, 512.0 * rank - 256.0, A.mult, A.add, ["pd1"], ["pc7"])
     ts(T.S0[:], T.BO[:], T.pc[:, 5:6], None, A.mult, None, ["BO", "pc5"], ["S0"])
-    ts(T.KR[:], T.K64[:], T.pc[:, 6:7], None, A.add, None, ["K64", "pc6"], ["KR"])
-    ts(T.VZ[:], T.K64[:], 256.0, T.pc[:, 7:8], A.mult, A.add, ["K64", "pc7"], ["VZ"])
+    ts(T.VZ[:], T.J[:, 0:64], 4096.0, T.pc[:, 7:8], A.mult, A.add, ["J", "pc7"], ["VZ"])
+    ts(T.lead[:, 0:16], T.lv[:, at:at + 16], 0.0, None, A.is_equal, None, ["lvr"], ["lead0"])
     for d in home[3:]:
         ms(T.WA[:, ST * d:ST * d + BL], -2.0, ["WA"])
     for d in home:
         ms(T.WB[:, ST * d:ST * d + BL], -2.0, ["WB"])
-    ts(T.lead[:, 0:16], T.lv[:, at:at + 16], 256.0, None, A.is_lt, None, ["E%d" % rank], ["lead0"])
 
     for s in near:
-        note(("h%d" % s, len(enear)), [], ["E%d" % s])
+        note(("h%d" % s, len(enear)), [], ["h%d" % s])
     for s in far:
-        note(("h%d" % s, len(efar)), [], ["E%d" % s])
+        note(("h%d" % s, len(efar)), [], ["h%d" % s])
     note(("v%d" % peer, len(efar)), [], ["pv"])
-    every = ["E%d" % s for s in near + far] + own
-    mm(T.pn[:, 0:8], T.Bk[:], T.lv[:, 16:8 * LV:LV], every + ["Bk"], ["pn"])
-    mm(T.pw[:, 0:8], T.S15[:], T.lv[:, 17:8 * LV:LV], every + ["S15"], ["pw"])
-    mm(T.pl[:, 0:8], T.S0[:], T.lv[:, 18:8 * LV:LV], every + ["S0"], ["pl"])
-
-    pa = LV * peer
-    ts(T.lead[:, 16:32], T.lv[:, pa:pa + 16], 256.0, None, A.is_lt, None, ["E%d" % peer], ["lead1"])
-    scan(T.bt[:, 1:9], T.ones[:, 0:8], T.pn[:, 0:8], -256.0, ["ones", "pn"], ["bt"])
+    every = ["h%d" % s for s in near + far] + own
     pages = [rank, peer]
+
+    def entries(i, keys):
+        a = LV * pages[i]
+        mm(T.pe[:, 16 * i:16 * i + 16], T.Id[:], T.lv[:, a:a + 16], ["Id"] + keys, [], True, False)
+        mm(T.pe[:, 16 * i:16 * i + 16], T.Id[:], T.lv[:, a + 16:a + 32], keys, ["pe%d" % i], False, True)
+
+    def add_base(s, keys, last):
+        a = LV * s + 39 - s
+        for p, k in ((T.pb, "pb"), (T.pk, "pk")):
+            mm(p[:, 0:9], T.Bk[:], T.lv[:, a:a + 9], keys, [k] if last else [], False, last)
+    entries(0, own)
+    mm(T.pb[:, 0:9], T.Bk[:], T.neg[:, 0:9], ["Bk", "neg"], [], True, False)
+    mm(T.pk[:, 0:9], T.Bk[:], T.neg2[:, 0:9], ["Bk", "neg2"], [], True, False)
+    add_base(rank, own, False)
+    order = near + [s for s in far if s != peer] + [peer]
+    for s in order[:-1]:
+        add_base(s, ["h%d" % s], False)
+    mm(T.pw[:, 0:8], T.S15[:], T.lv[:, 48:8 * LV:LV], every + ["S15"], ["pw"])
+    add_base(peer, ["h%d" % peer], True)
+    entries(1, ["h%d" % peer])
+    mm(T.pl[:, 0:8], T.S0[:], T.lv[:, 49:8 * LV:LV], every + ["S0"], ["pl"])
+
+    op("qs", lambda s: s.activation(T.kr[:], T.pk[:, 0:8], F.Copy, RND, 1.0 / 4096), ["pk"], ["kr"])
+    op("qs", lambda s: s.activation(T.kf[:], T.kr[:], F.Copy, -16.0 * RND, 16.0), ["kr"], ["kf"])
+    pa = LV * peer
+    ts(T.lead[:, 16:32], T.lv[:, pa:pa + 16], 0.0, None, A.is_equal, None, ["h%d" % peer], ["lead1"])
     for i, p in enumerate(pages):
-        ts(T.Aq[:, 16 * i:16 * i + 16], T.lead[:, 16 * i:16 * i + 16], T.pw[:, p - 1:p] if p else 0.0, T.bt[:, p:p + 1],
-           A.mult, A.add, ["lead%d" % i, "pw", "bt", "bt0"], ["A%d" % i])
-    cp(T.ki[:, 1:8], T.bt[:, 1:8], ["bt"], ["ki"])
+        ts(T.X1[:, 16 * i:16 * i + 16], T.lead[:, 16 * i:16 * i + 16], T.pw[:, p - 1:p] if p else 0.0, None, A.mult, None,
+           ["lead%d" % i, "pw"], ["X1%d" % i])
+    tt(T.X2[:], T.X1[:], T.pe[:, 0:32], A.add, ["X10", "X11", "pe0", "pe1"], ["X2"])
     for i, p in enumerate(pages):
-        tt(T.Zi[:, 16 * i:16 * i + 16], T.Aq[:, 16 * i:16 * i + 16], T.lv[:, LV * p:LV * p + 16], A.add,
-           ["A%d" % i, "E%d" % p], ["Z%d" % i])
-    ts(T.k2[:, 1:8], T.ki[:, 1:8], 8, 0xFFF0, A.logical_shift_right, A.bitwise_and, ["ki"], ["k2"])
+        ts(T.Zi[:, 16 * i:16 * i + 16], T.X2[:, 16 * i:16 * i + 16], T.pb[:, p:p + 1], None, A.add, None, ["X2", "pb"], ["Z%d" % i])
     zk = ["Z0", "Z1"]
     ts(T.Y1[:], T.Zi[:], 8, 0xFFF0, A.logical_shift_right, A.bitwise_and, zk, ["Y1"])
     ts(T.Y2[:], T.Zi[:], 5, 15, A.logical_shift_right, A.bitwise_and, zk, ["Y2"])
     ts(T.D[:], T.Zi[:], 0xE00, None, A.bitwise_and, None, zk, ["D"])
     tt(T.s1[:], T.Y1[:], T.Y2[:], A.add, ["Y1", "Y2"], ["s1"])
-    cp(T.kf[:, 1:8], T.k2[:, 1:8], ["k2"], ["kf"])
     tt(T.s2[:], T.s1[:], T.D[:], A.add, ["s1", "D"], ["s2"])
     for i, p in enumerate(pages):
         ts(T.off[:, 16 * i:16 * i + 16], T.s2[:, 16 * i:16 * i + 16], T.kf[:, p:p + 1], None, A.subtract, None,
-           ["s2", "kf", "kf0"], ["off%d" % i])
-    k = len(eall) // 4
+           ["s2", "kf"], ["off%d" % i])
     for i, (win, val, vk, tag) in enumerate([(T.WA, T.ev, "ev", "a"), (T.WB, T.pv, "pv", "b")]):
         wk = "WA" if i == 0 else "WB"
         cp(win[:, 0:8 * ST].indirect(T.off[:, 16 * i:16 * i + 16]), val[:], ["off%d" % i, vk, wk], [wk])
         p = pages[i]
-        send([(win[:, ST * d:ST * d + BL], T.LD[:, BL * p:BL * p + BL], [d],
-               [eall[(k * (j + i) + x) % len(eall)] for x in range(k)], "%s%d" % (tag, rank)) for j, d in enumerate(near)], [wk])
+        es = shares(rank, i == 1)
+        send([(win[:, ST * d:ST * d + BL], T.LD[:, BL * p:BL * p + BL], [d], es[d], "%s%d" % (tag, rank)) for d in near], [wk])
 
     ts(T.vs[:, 0:7], T.pw[:, 0:7], -224.0, None, A.add, None, ["pw"], ["vs"])
-    tt(T.dk[:, 0:7], T.kf[:, 0:7], T.kf[:, 1:8], A.subtract, ["kf", "kf0"], ["dk"])
+    tt(T.dk[:, 0:7], T.kf[:, 0:7], T.kf[:, 1:8], A.subtract, ["kf"], ["dk"])
     tt(T.vt[:, 0:7], T.vs[:, 0:7], T.pl[:, 1:8], A.mult, ["vs", "pl"], ["vt"])
-    ts(T.dl2[:, 0:7], T.dk[:, 0:7], float(BL), None, A.add, None, ["dk"], ["dl2"])
-    tt(T.vq[:, 0:7], T.vt[:, 0:7], T.bt[:, 1:8], A.add, ["vt", "bt"], ["vq"])
-    for x in range(8):
-        lim = T.vq[:, x:x + 1] if x < 7 else T.bt[:, 8:9]
-        ts(T.cm[:, 64 * x:64 * x + 64], T.VZ[:], lim, T.dl2[:, x:x + 1] if x < 7 else 16384.0, A.is_ge, A.mult,
-           ["VZ", "vq", "bt", "dl2"], ["cm%d" % x])
-    cm = [T.cm[:, 64 * x:64 * x + 64] for x in range(8)]
-    ac = [T.ac[:, 64 * x:64 * x + 64] for x in range(8)]
-    for x in range(4):
-        tt(ac[x], cm[2 * x], cm[2 * x + 1], A.add, ["cm%d" % (2 * x), "cm%d" % (2 * x + 1)], ["ac%d" % x])
-    for x in range(2):
-        tt(ac[4 + x], ac[2 * x], ac[2 * x + 1], A.add, ["ac%d" % (2 * x), "ac%d" % (2 * x + 1)], ["ac%d" % (4 + x)])
+    ts(T.dl2[:, 0:7], T.dk[:, 0:7], 0.0625, BL / 16.0, A.mult, A.add, ["dk"], ["dl2"])
+    tt(T.vq[:, 0:7], T.vt[:, 0:7], T.pb[:, 1:8], A.add, ["vt", "pb"], ["vq"])
+    mm(T.pz[:, 0:64], T.Id[:], T.J[:, 0:64], ["Id", "J"], [], True, False)
+    for x in [7, 0, 1, 2, 3, 4, 5, 6]:
+        lim = T.vq[:, x:x + 1] if x < 7 else T.pb[:, 8:9]
+        ts(T.cm[:, 64 * x:64 * x + 64], T.VZ[:], lim, T.dl2[:, x:x + 1] if x < 7 else 1024.0, A.is_ge, A.mult,
+           ["VZ", "vq", "dl2"] if x < 7 else ["VZ", "pb"], ["cm%d" % x])
+        mm(T.pz[:, 0:64], T.Id[:], T.cm[:, 64 * x:64 * x + 64], ["cm%d" % x], ["pz"] if x == 6 else [], False, x == 6)
     for i, (win, wk) in enumerate([(T.WA, "WA"), (T.WB, "WB")]):
         p = pages[i]
         cp(T.LD[:, BL * p:BL * p + BL], win[:, ST * rank:ST * rank + BL], [wk], ["L%d" % p])
-    tt(ac[6], ac[4], T.KR[:], A.add, ["ac4", "KR"], ["ac6"])
-    tt(ac[7], ac[6], ac[5], A.add, ["ac6", "ac5"], ["ac7"])
-    ts(T.Wt[:], ac[7], float(8 * BL), None, A.min, None, ["ac7"], ["Wt"])
+    ts(T.Wt[:], T.pz[:, 0:64], T.pc[:, 6:7], float(8 * BL), A.add, A.min, ["pz", "pc6"], ["Wt"])
 
     for s in near:
-        note(("a%d" % s, k), [], ["L%d" % s])
-        note(("b%d" % s, k), [], ["L%d" % peer_of(s)])
+        note(("a%d" % s, len(shares(s, False)[rank])), [], ["L%d" % s])
+        note(("b%d" % s, len(shares(s, True)[rank])), [], ["L%d" % peer_of(s)])
     rd = ["L%d" % s for s in home + far] + ["LDend", "Wt"]
     op("qs", lambda s: s.activation(T.Y[:, 512:1024], T.LD[:, 0:8 * BL + 16].indirect(T.Wt[:, 32:64]), F.Copy), rd, ["Yb"])
     cp(T.Y[:, 0:512], T.LD[:, 0:8 * BL + 16].indirect(T.Wt[:, 0:32]), rd, ["Ya"])

@@ -1,8 +1,8 @@
 from concourse.bass import DstId, RemoteDMATransfer
 from concourse.mybir import AluOpType as A, ActivationFunctionType as F
 
-LV = 56
-LW = 50
+LV = 24
+LW = 18
 BL = 272
 ST = 512
 RND = 12582912.0
@@ -14,11 +14,14 @@ SCRATCH = {
     "BO": ("sbuf", [128, 128], "bfloat16"), "bj": ("sbuf", [128, 128], "bfloat16"),
     "Lo": ("sbuf", [128, 128], "bfloat16"), "Sh": ("sbuf", [128, 128], "bfloat16"),
     "S15": ("sbuf", [128, 128], "bfloat16"), "S0": ("sbuf", [128, 128], "bfloat16"), "Bk": ("sbuf", [128, 128], "bfloat16"),
-    "ones": ("sbuf", [128, 16], "bfloat16"), "neg": ("sbuf", [128, 16], "bfloat16"), "neg2": ("sbuf", [128, 16], "bfloat16"),
-    "rli": ("sbuf", [128, 16], "int32"), "dli": ("sbuf", [128, 16], "int32"), "valt": ("sbuf", [128, 272], "bfloat16"),
-    "rb": ("sbuf", [128, 16], "bfloat16"), "rw": ("sbuf", [128, 16], "bfloat16"), "z": ("sbuf", [128, 16], "bfloat16"),
-    "cz": ("sbuf", [128, 16], "bfloat16"), "w0": ("sbuf", [128, 16], "bfloat16"),
-    "lv": ("sbuf", [128, 8 * LV], "bfloat16"),
+    "ones": ("sbuf", [128, 16], "bfloat16"), "mone": ("sbuf", [128, 16], "bfloat16"),
+    "neg": ("sbuf", [128, 16], "bfloat16"), "neg2": ("sbuf", [128, 16], "bfloat16"),
+    "rli": ("sbuf", [128, 16], "int32"), "rlp": ("sbuf", [128, 16], "int32"),
+    "dli": ("sbuf", [128, 16], "int32"), "valt": ("sbuf", [128, 272], "bfloat16"),
+    "rb": ("sbuf", [128, 32], "bfloat16"), "rw": ("sbuf", [128, 32], "bfloat16"), "z": ("sbuf", [128, 32], "bfloat16"),
+    "cr": ("sbuf", [128, 16], "bfloat16"),
+    "cz": ("sbuf", [128, 32], "bfloat16"), "w0": ("sbuf", [128, 32], "bfloat16"),
+    "lv": ("sbuf", [128, 8 * LV], "bfloat16"), "nr": ("sbuf", [128, 32], "bfloat16"), "nw": ("sbuf", [128, 32], "bfloat16"),
     "db": ("sbuf", [128, 16], "bfloat16"), "cd": ("sbuf", [128, 16], "bfloat16"), "vx": ("sbuf", [128, 16], "float32"),
     "vy": ("sbuf", [128, 16], "float32"), "l1": ("sbuf", [128, 16], "uint16"),
     "ev": ("sbuf", [128, 256], "bfloat16"), "pv": ("sbuf", [128, 256], "bfloat16"),
@@ -26,7 +29,7 @@ SCRATCH = {
     "X1": ("sbuf", [128, 32], "float32"), "X2": ("sbuf", [128, 32], "float32"),
     "Zi": ("sbuf", [128, 32], "int32"), "D": ("sbuf", [128, 32], "int32"), "Y1": ("sbuf", [128, 32], "int32"),
     "Y2": ("sbuf", [128, 32], "int32"), "s1": ("sbuf", [128, 32], "int32"), "s2": ("sbuf", [128, 32], "int32"),
-    "off": ("sbuf", [128, 32], "uint16"),
+    "off": ("sbuf", [128, 32], "uint16"), "fill": ("sbuf", [128, BL], "bfloat16"),
     "WA": ("sbuf", [128, 8 * ST], "bfloat16"), "WB": ("sbuf", [128, 8 * ST], "bfloat16"),
     "LD": ("sbuf", [128, 8 * BL + 16], "bfloat16"),
     "vs": ("sbuf", [128, 8], "float32"), "vt": ("sbuf", [128, 8], "float32"), "vq": ("sbuf", [128, 8], "float32"),
@@ -38,7 +41,7 @@ SCRATCH = {
     "pz": ("psum", [128, 512], "float32"), "pe": ("psum", [128, 512], "float32"), "pk": ("psum", [128, 512], "float32"),
 }
 SEMAPHORES = (["qv", "qs", "qt", "qg", "drl", "ddl", "dval", "dy", "dz", "loc"]
-              + ["%s%d" % (x, i) for x in "hvab" for i in range(8)])
+              + ["%s%d" % (x, i) for x in "huvab" for i in range(8)])
 
 
 def bits(es):
@@ -124,6 +127,9 @@ def rank_program(g, core, T, topo):
     def cp(out, a, r, w):
         op("qv", lambda v: v.tensor_copy(out, a), r, w)
 
+    def act(out, a, r, w, bias=0.0, scale=1.0):
+        op("qs", lambda s: s.activation(out, a, F.Copy, bias, scale), r, w)
+
     def ms(ap, c, w):
         op("qv", lambda v: v.memset(ap, c), [], w)
 
@@ -145,7 +151,7 @@ def rank_program(g, core, T, topo):
             loc[0] += len(es)
         g.remote_dma_fused(trs, local_sem=T.sem.loc)
 
-    dma("sync", T.rli[:], T.rl[:], "drl", [], ["rli"])
+    dma("sync", T.rli[:], T.rl[:], "drl", [], ["rli0"])
     dma("qs", T.dli[:], T.dl[:], "ddl", [], ["dli"])
     dma("sync", T.valt[:, 0:256], T.val[:], "dval", [], ["val0"])
 
@@ -153,14 +159,16 @@ def rank_program(g, core, T, topo):
     op("qg", lambda x: x.iota(T.Pi[:], [[0, 1]], 0, 1), [], ["Pi"])
     op("qg", lambda x: x.iota(T.Kt[:], [[1, 8], [0, 16]], 0, 0, allow_small_or_imprecise_dtypes=True), [], ["Kt"])
     op("qg", lambda x: x.iota(T.J[:], [[1, 128]], 0, 0, allow_small_or_imprecise_dtypes=True), [], ["J"])
+    send([(T.rli[:], T.rlp[:], [peer], efar, "u%d" % rank)], ["rli0"])
+    ms(T.fill[:], -2.0, ["fill"])
+    for d in home:
+        act(T.WA[:, ST * d:ST * d + BL], T.fill[:], ["fill"], ["WA"])
+    for d in home[:2]:
+        act(T.WB[:, ST * d:ST * d + BL], T.fill[:], ["fill"], ["WB"])
     ms(T.ones[:], 1.0, ["ones"])
-    ms(T.neg[:], -0.0625, ["neg"])
-    ms(T.neg2[:], -0.53125, ["neg2"])
+    ms(T.mone[:], -1.0, ["mone"])
+    ms(T.lv[:, at:at + 8], 0.0, ["lvz"])
     ms(T.valt[:, 256:272], -1.0, ["val1"])
-    ms(T.lv[:, at + 32:at + 40], 0.0, ["lvz"])
-    ms(T.LD[:, 8 * BL:8 * BL + 16], -2.0, ["LDend"])
-    for d in home[:3]:
-        ms(T.WA[:, ST * d:ST * d + BL], -2.0, ["WA"])
     ts(T.pd[:, 0:1], T.Pi[:], 4, None, A.logical_shift_right, None, ["Pi"], ["pd0"])
     ts(T.pd[:, 1:2], T.Pi[:], 15, None, A.bitwise_and, None, ["Pi"], ["pd1"])
     cp(T.pc[:, 2:3], T.Pi[:], ["Pi"], ["pc2"])
@@ -168,49 +176,70 @@ def rank_program(g, core, T, topo):
     cp(T.pc[:, 0:1], T.pd[:, 0:1], ["pd0"], ["pc0"])
     ts(T.pc[:, 4:5], T.pd[:, 1:2], 15.0, 32.0, A.is_equal, A.mult, ["pd1"], ["pc4"])
     ts(T.BO[:], T.Kt[:], T.pc[:, 0:1], None, A.is_equal, None, ["Kt", "pc0"], ["BO"])
+    ms(T.neg[:], -0.0625, ["neg"])
     tt(T.bj[:], T.BO[:], T.J[:], A.mult, ["BO", "J"], ["bj"])
     ts(T.Bk[:], T.BO[:], 256.0, None, A.mult, None, ["BO"], ["Bk"])
     ts(T.Lo[:], T.bj[:], T.pc[:, 2:3], None, A.is_gt, None, ["bj", "pc2"], ["Lo"])
     ts(T.Sh[:], T.bj[:], T.pc[:, 3:4], 2.0, A.is_equal, A.mult, ["bj", "pc3"], ["Sh"])
+    ts(T.S15[:], T.BO[:], T.pc[:, 4:5], None, A.mult, None, ["BO", "pc4"], ["S15"])
 
-    ts(T.z[:], T.rli[:], -1.0, 1.0, A.mult, A.add, ["rli"], ["z"])
-    cp(T.rb[:], T.rli[:], ["rli"], ["rb"])
-    scan(T.cz[:], T.ones[:], T.z[:], 0.0, ["ones", "z"], ["cz"])
-    scan(T.w0[:], T.rb[:], T.rb[:], 0.0, ["rb"], ["w0"])
-    mm(T.ps1[:, 0:1], T.Lo[:], T.cz[:, 15:16], ["Lo", "cz"], ["ps1"])
-    mm(T.ps1[:, 1:2], T.Sh[:], T.w0[:, 15:16], ["Sh", "w0"], ["ps1"])
-    ts(T.rw[:], T.rb[:], 2.0, None, A.mult, None, ["rb"], ["rw"])
-    ts(T.lv[:, at + 40:at + 48], T.ones[:, 0:8], T.cz[:, 15:16], None, A.mult, None, ["cz", "ones"], ["lva"])
-    cp(T.lv[:, at + 48:at + 49], T.w0[:, 15:16], ["w0"], ["lvb"])
-    cp(T.lv[:, at + 49:at + 50], T.rb[:, 0:1], ["rb"], ["lvc"])
-    ts(T.lv[:, at:at + 16], T.cz[:, 0:16], T.ps1[:, 0:1], 16.0, A.add, A.mult, ["cz", "ps1"], ["lvr"])
-    scan(T.lv[:, at + 16:at + 32], T.rb[:], T.rw[:], T.ps1[:, 1:2], ["rb", "rw", "ps1"], ["lvw"])
-    own = ["lva", "lvb", "lvc", "lvr", "lvw", "lvz"]
+    src = [T.rli, T.rlp]
+
+    def x16(t, i):
+        return t[:, 16 * i:16 * i + 16]
+
+    def items(i):
+        k = "%d" % i
+        cp(x16(T.rb, i), src[i][:], ["rli" + k], ["rb" + k])
+        scan(x16(T.w0, i), x16(T.rb, i), x16(T.rb, i), 0.0, ["rb" + k], ["w0" + k])
+
+    def starts(i):
+        k = "%d" % i
+        ts(x16(T.z, i), src[i][:], -1.0, 1.0, A.mult, A.add, ["rli" + k], ["z" + k])
+        scan(x16(T.cz, i), T.ones[:], x16(T.z, i), 0.0, ["ones", "z" + k], ["cz" + k])
+
+    def sums(i):
+        k = "%d" % i
+        c = 16 * i + 15
+        mm(T.ps1[:, 2 * i:2 * i + 1], T.Lo[:], T.cz[:, c:c + 1], ["Lo", "cz" + k], ["ps1"])
+        mm(T.ps1[:, 2 * i + 1:2 * i + 2], T.Sh[:], T.w0[:, c:c + 1], ["Sh", "w0" + k], ["ps1"])
+
+    def numbers(i):
+        k = "%d" % i
+        ts(x16(T.rw, i), x16(T.rb, i), 2.0, None, A.mult, None, ["rb" + k], ["rw" + k])
+        ts(x16(T.nr, i), x16(T.cz, i), T.ps1[:, 2 * i:2 * i + 1], 16.0, A.add, A.mult, ["cz" + k, "ps1"], ["nr" + k])
+        scan(x16(T.nw, i), x16(T.rb, i), x16(T.rw, i), T.ps1[:, 2 * i + 1:2 * i + 2], ["rb" + k, "rw" + k, "ps1"], ["nw" + k])
+        ts(x16(T.lead, i), x16(T.nr, i), 0.0, None, A.is_equal, None, ["nr" + k], ["lead" + k])
+
+    cp(T.rb[:, 0:16], T.rli[:], ["rli0"], ["rb0"])
+    cp(T.lv[:, at + 17:at + 18], T.rli[:, 0:1], ["rli0"], ["lvc"])
+    scan(T.cr[:], T.ones[:], T.rb[:, 0:16], 0.0, ["ones", "rb0"], ["cr"])
+    scan(T.w0[:, 0:16], T.rb[:, 0:16], T.rb[:, 0:16], 0.0, ["rb0"], ["w00"])
+    ts(T.lv[:, at + 8:at + 16], T.mone[:, 0:8], T.cr[:, 15:16], 16.0, A.mult, A.add, ["cr", "mone"], ["lva"])
+    cp(T.lv[:, at + 16:at + 17], T.w0[:, 15:16], ["w00"], ["lvb"])
+    own = ["lva", "lvb", "lvc", "lvz"]
     sl = T.lv[:, at:at + LW]
     send([(sl, sl, far, efar, "h%d" % rank), (sl, sl, near, enear, "h%d" % rank)], own)
 
     cp(T.db[:], T.dli[:], ["dli"], ["db"])
-    ts(T.S15[:], T.BO[:], T.pc[:, 4:5], None, A.mult, None, ["BO", "pc4"], ["S15"])
+    ts(T.z[:, 0:16], T.rli[:], -1.0, 1.0, A.mult, A.add, ["rli0"], ["z0"])
     scan(T.cd[:], T.ones[:], T.db[:], 0.0, ["ones", "db"], ["cd"])
     mm(T.ps2[:, 0:1], T.Lo[:], T.cd[:, 15:16], ["Lo", "cd"], ["ps2"])
+    scan(T.cz[:, 0:16], T.ones[:], T.z[:, 0:16], 0.0, ["ones", "z0"], ["cz0"])
+    sums(0)
     ts(T.pc[:, 5:6], T.pd[:, 1:2], 0.0, None, A.is_equal, None, ["pd1"], ["pc5"])
-    ts(T.pc[:, 6:7], T.pd[:, 1:2], 16.0, None, A.add, None, ["pd1"], ["pc6"])
     ts(T.vx[:], T.cd[:], T.ps2[:, 0:1], -257.0, A.add, A.add, ["cd", "ps2"], ["vx"])
-    tt(T.vy[:], T.vx[:], T.db[:], A.mult, ["vx", "db"], ["vy"])
-    ts(T.l1[:], T.vy[:], 256.0, None, A.add, None, ["vy"], ["l1"])
-    op("qs", lambda s: s.activation(T.ev[:], T.valt[:, 0:272].indirect(T.l1[:, 0:16]), F.Copy), ["val0", "val1", "l1"], ["ev"])
-    send([(T.ev[:], T.pv[:], [peer], efar, "v%d" % rank)], ["ev"])
-
     ts(T.Id[:], T.J[:], T.pc[:, 2:3], 16.0, A.is_equal, A.mult, ["J", "pc2"], ["Id"])
-    ts(T.pc[:, 7:8], T.pd[:, 1:2], 32.0, 512.0 * rank - 256.0, A.mult, A.add, ["pd1"], ["pc7"])
-    ts(T.S0[:], T.BO[:], T.pc[:, 5:6], None, A.mult, None, ["BO", "pc5"], ["S0"])
-    ts(T.VZ[:], T.J[:, 0:64], 4096.0, T.pc[:, 7:8], A.mult, A.add, ["J", "pc7"], ["VZ"])
-    ts(T.lead[:, 0:16], T.lv[:, at:at + 16], 0.0, None, A.is_equal, None, ["lvr"], ["lead0"])
-    for d in home[3:]:
-        ms(T.WA[:, ST * d:ST * d + BL], -2.0, ["WA"])
-    for d in home:
-        ms(T.WB[:, ST * d:ST * d + BL], -2.0, ["WB"])
+    tt(T.vy[:], T.vx[:], T.db[:], A.mult, ["vx", "db"], ["vy"])
+    ms(T.neg2[:], -0.53125, ["neg2"])
+    ts(T.l1[:], T.vy[:], 256.0, None, A.add, None, ["vy"], ["l1"])
+    act(T.ev[:], T.valt[:, 0:272].indirect(T.l1[:, 0:16]), ["val0", "val1", "l1"], ["ev"])
+    send([(T.ev[:], T.pv[:], [peer], efar, "v%d" % rank)], ["ev"])
+    for d in home[2:]:
+        act(T.WB[:, ST * d:ST * d + BL], T.fill[:], ["fill"], ["WB"])
+    numbers(0)
 
+    note(("u%d" % peer, len(efar)), [], ["rli1"])
     for s in near:
         note(("h%d" % s, len(enear)), [], ["h%d" % s])
     for s in far:
@@ -219,37 +248,40 @@ def rank_program(g, core, T, topo):
     every = ["h%d" % s for s in near + far] + own
     pages = [rank, peer]
 
-    def entries(i, keys):
-        a = LV * pages[i]
-        mm(T.pe[:, 16 * i:16 * i + 16], T.Id[:], T.lv[:, a:a + 16], ["Id"] + keys, [], True, False)
-        mm(T.pe[:, 16 * i:16 * i + 16], T.Id[:], T.lv[:, a + 16:a + 32], keys, ["pe%d" % i], False, True)
+    def entries(i):
+        k = "%d" % i
+        mm(x16(T.pe, i), T.Id[:], x16(T.nr, i), ["Id", "nr" + k], [], True, False)
+        mm(x16(T.pe, i), T.Id[:], x16(T.nw, i), ["nw" + k], ["pe" + k], False, True)
 
-    def add_base(s, keys, last):
-        a = LV * s + 39 - s
-        for p, k in ((T.pb, "pb"), (T.pk, "pk")):
-            mm(p[:, 0:9], T.Bk[:], T.lv[:, a:a + 9], keys, [k] if last else [], False, last)
-    entries(0, own)
+    def add_base(p, s, keys, key, last):
+        a = LV * s + 7 - s
+        mm(p[:, 0:9], T.Bk[:], T.lv[:, a:a + 9], keys, [key] if last else [], False, last)
     mm(T.pb[:, 0:9], T.Bk[:], T.neg[:, 0:9], ["Bk", "neg"], [], True, False)
     mm(T.pk[:, 0:9], T.Bk[:], T.neg2[:, 0:9], ["Bk", "neg2"], [], True, False)
-    add_base(rank, own, False)
-    order = near + [s for s in far if s != peer] + [peer]
-    for s in order[:-1]:
-        add_base(s, ["h%d" % s], False)
-    mm(T.pw[:, 0:8], T.S15[:], T.lv[:, 48:8 * LV:LV], every + ["S15"], ["pw"])
-    add_base(peer, ["h%d" % peer], True)
-    entries(1, ["h%d" % peer])
-    mm(T.pl[:, 0:8], T.S0[:], T.lv[:, 49:8 * LV:LV], every + ["S0"], ["pl"])
+    add_base(T.pb, rank, own, "pb", False)
+    add_base(T.pk, rank, own, "pk", False)
+    entries(0)
+    items(1)
+    starts(1)
+    sums(1)
+    numbers(1)
+    entries(1)
+    for s in near:
+        add_base(T.pb, s, ["h%d" % s], "pb", False)
+        add_base(T.pk, s, ["h%d" % s], "pk", False)
+    mm(T.pw[:, 0:8], T.S15[:], T.lv[:, 16:8 * LV:LV], every + ["S15"], ["pw"])
+    for s in far:
+        add_base(T.pb, s, ["h%d" % s], "pb", s == far[-1])
+    for s in far:
+        add_base(T.pk, s, ["h%d" % s], "pk", s == far[-1])
 
-    op("qs", lambda s: s.activation(T.kr[:], T.pk[:, 0:8], F.Copy, RND, 1.0 / 4096), ["pk"], ["kr"])
-    op("qs", lambda s: s.activation(T.kf[:], T.kr[:], F.Copy, -16.0 * RND, 16.0), ["kr"], ["kf"])
-    pa = LV * peer
-    ts(T.lead[:, 16:32], T.lv[:, pa:pa + 16], 0.0, None, A.is_equal, None, ["h%d" % peer], ["lead1"])
+    act(T.kr[:], T.pk[:, 0:8], ["pk"], ["kr"], RND, 1.0 / 4096)
+    act(T.kf[:], T.kr[:], ["kr"], ["kf"], -16.0 * RND, 16.0)
     for i, p in enumerate(pages):
-        ts(T.X1[:, 16 * i:16 * i + 16], T.lead[:, 16 * i:16 * i + 16], T.pw[:, p - 1:p] if p else 0.0, None, A.mult, None,
-           ["lead%d" % i, "pw"], ["X1%d" % i])
+        ts(x16(T.X1, i), x16(T.lead, i), T.pw[:, p - 1:p] if p else 0.0, None, A.mult, None, ["lead%d" % i, "pw"], ["X1%d" % i])
     tt(T.X2[:], T.X1[:], T.pe[:, 0:32], A.add, ["X10", "X11", "pe0", "pe1"], ["X2"])
     for i, p in enumerate(pages):
-        ts(T.Zi[:, 16 * i:16 * i + 16], T.X2[:, 16 * i:16 * i + 16], T.pb[:, p:p + 1], None, A.add, None, ["X2", "pb"], ["Z%d" % i])
+        ts(x16(T.Zi, i), x16(T.X2, i), T.pb[:, p:p + 1], None, A.add, None, ["X2", "pb"], ["Z%d" % i])
     zk = ["Z0", "Z1"]
     ts(T.Y1[:], T.Zi[:], 8, 0xFFF0, A.logical_shift_right, A.bitwise_and, zk, ["Y1"])
     ts(T.Y2[:], T.Zi[:], 5, 15, A.logical_shift_right, A.bitwise_and, zk, ["Y2"])
@@ -257,20 +289,25 @@ def rank_program(g, core, T, topo):
     tt(T.s1[:], T.Y1[:], T.Y2[:], A.add, ["Y1", "Y2"], ["s1"])
     tt(T.s2[:], T.s1[:], T.D[:], A.add, ["s1", "D"], ["s2"])
     for i, p in enumerate(pages):
-        ts(T.off[:, 16 * i:16 * i + 16], T.s2[:, 16 * i:16 * i + 16], T.kf[:, p:p + 1], None, A.subtract, None,
-           ["s2", "kf"], ["off%d" % i])
+        ts(x16(T.off, i), x16(T.s2, i), T.kf[:, p:p + 1], None, A.subtract, None, ["s2", "kf"], ["off%d" % i])
     for i, (win, val, vk, tag) in enumerate([(T.WA, T.ev, "ev", "a"), (T.WB, T.pv, "pv", "b")]):
         wk = "WA" if i == 0 else "WB"
-        cp(win[:, 0:8 * ST].indirect(T.off[:, 16 * i:16 * i + 16]), val[:], ["off%d" % i, vk, wk], [wk])
+        cp(win[:, 0:8 * ST].indirect(x16(T.off, i)), val[:], ["off%d" % i, vk, wk], [wk])
         p = pages[i]
         es = shares(rank, i == 1)
         send([(win[:, ST * d:ST * d + BL], T.LD[:, BL * p:BL * p + BL], [d], es[d], "%s%d" % (tag, rank)) for d in near], [wk])
 
+    ts(T.S0[:], T.BO[:], T.pc[:, 5:6], None, A.mult, None, ["BO", "pc5"], ["S0"])
+    mm(T.pl[:, 0:8], T.S0[:], T.lv[:, 17:8 * LV:LV], every + ["S0"], ["pl"])
+    ts(T.pc[:, 7:8], T.pd[:, 1:2], 32.0, 512.0 * rank - 256.0, A.mult, A.add, ["pd1"], ["pc7"])
     ts(T.vs[:, 0:7], T.pw[:, 0:7], -224.0, None, A.add, None, ["pw"], ["vs"])
     tt(T.dk[:, 0:7], T.kf[:, 0:7], T.kf[:, 1:8], A.subtract, ["kf"], ["dk"])
+    ts(T.VZ[:], T.J[:, 0:64], 4096.0, T.pc[:, 7:8], A.mult, A.add, ["J", "pc7"], ["VZ"])
     tt(T.vt[:, 0:7], T.vs[:, 0:7], T.pl[:, 1:8], A.mult, ["vs", "pl"], ["vt"])
     ts(T.dl2[:, 0:7], T.dk[:, 0:7], 0.0625, BL / 16.0, A.mult, A.add, ["dk"], ["dl2"])
+    ts(T.pc[:, 6:7], T.pd[:, 1:2], 16.0, None, A.add, None, ["pd1"], ["pc6"])
     tt(T.vq[:, 0:7], T.vt[:, 0:7], T.pb[:, 1:8], A.add, ["vt", "pb"], ["vq"])
+    ms(T.LD[:, 8 * BL:8 * BL + 16], -2.0, ["LDend"])
     mm(T.pz[:, 0:64], T.Id[:], T.J[:, 0:64], ["Id", "J"], [], True, False)
     for x in [7, 0, 1, 2, 3, 4, 5, 6]:
         lim = T.vq[:, x:x + 1] if x < 7 else T.pb[:, 8:9]
@@ -279,14 +316,14 @@ def rank_program(g, core, T, topo):
         mm(T.pz[:, 0:64], T.Id[:], T.cm[:, 64 * x:64 * x + 64], ["cm%d" % x], ["pz"] if x == 6 else [], False, x == 6)
     for i, (win, wk) in enumerate([(T.WA, "WA"), (T.WB, "WB")]):
         p = pages[i]
-        cp(T.LD[:, BL * p:BL * p + BL], win[:, ST * rank:ST * rank + BL], [wk], ["L%d" % p])
+        act(T.LD[:, BL * p:BL * p + BL], win[:, ST * rank:ST * rank + BL], [wk], ["L%d" % p])
     ts(T.Wt[:], T.pz[:, 0:64], T.pc[:, 6:7], float(8 * BL), A.add, A.min, ["pz", "pc6"], ["Wt"])
 
     for s in near:
         note(("a%d" % s, len(shares(s, False)[rank])), [], ["L%d" % s])
         note(("b%d" % s, len(shares(s, True)[rank])), [], ["L%d" % peer_of(s)])
     rd = ["L%d" % s for s in home + far] + ["LDend", "Wt"]
-    op("qs", lambda s: s.activation(T.Y[:, 512:1024], T.LD[:, 0:8 * BL + 16].indirect(T.Wt[:, 32:64]), F.Copy), rd, ["Yb"])
+    act(T.Y[:, 512:1024], T.LD[:, 0:8 * BL + 16].indirect(T.Wt[:, 32:64]), rd, ["Yb"])
     cp(T.Y[:, 0:512], T.LD[:, 0:8 * BL + 16].indirect(T.Wt[:, 0:32]), rd, ["Ya"])
     dma("qs", T.y[:, 512:1024], T.Y[:, 512:1024], "dz", ["Yb"], [])
     dma("sync", T.y[:, 0:512], T.Y[:, 0:512], "dy", ["Ya"], [])

@@ -1,47 +1,40 @@
 from concourse.bass import DstId, RemoteDMATransfer
-from concourse.mybir import AluOpType as A, ActivationFunctionType as F
+from concourse.mybir import AluOpType as A, ActivationFunctionType as F, AxisListType as X
 
-LV = 24
-LW = 18
-BL = 272
-ST = 512
-RND = 12582912.0
+PG = 256
+V0 = 16
 
 SCRATCH = {
-    "Kt": ("sbuf", [128, 128], "bfloat16"), "J": ("sbuf", [128, 128], "bfloat16"), "Pi": ("sbuf", [128, 1], "int32"),
-    "VZ": ("sbuf", [128, 64], "float32"), "Id": ("sbuf", [128, 128], "bfloat16"),
-    "pd": ("sbuf", [128, 2], "int32"), "pc": ("sbuf", [128, 8], "float32"),
-    "BO": ("sbuf", [128, 128], "bfloat16"), "bj": ("sbuf", [128, 128], "bfloat16"),
-    "Lo": ("sbuf", [128, 128], "bfloat16"), "Sh": ("sbuf", [128, 128], "bfloat16"),
-    "S15": ("sbuf", [128, 128], "bfloat16"), "S0": ("sbuf", [128, 128], "bfloat16"), "Bk": ("sbuf", [128, 128], "bfloat16"),
-    "ones": ("sbuf", [128, 16], "bfloat16"), "mone": ("sbuf", [128, 16], "bfloat16"),
-    "neg": ("sbuf", [128, 16], "bfloat16"), "neg2": ("sbuf", [128, 16], "bfloat16"),
-    "rli": ("sbuf", [128, 16], "int32"), "rlp": ("sbuf", [128, 16], "int32"),
-    "dli": ("sbuf", [128, 16], "int32"), "valt": ("sbuf", [128, 272], "bfloat16"),
-    "rb": ("sbuf", [128, 32], "bfloat16"), "rw": ("sbuf", [128, 32], "bfloat16"), "z": ("sbuf", [128, 32], "bfloat16"),
-    "cr": ("sbuf", [128, 16], "bfloat16"),
-    "cz": ("sbuf", [128, 32], "bfloat16"), "w0": ("sbuf", [128, 32], "bfloat16"),
-    "lv": ("sbuf", [128, 8 * LV], "bfloat16"), "nr": ("sbuf", [128, 32], "bfloat16"), "nw": ("sbuf", [128, 32], "bfloat16"),
-    "db": ("sbuf", [128, 16], "bfloat16"), "cd": ("sbuf", [128, 16], "bfloat16"), "vx": ("sbuf", [128, 16], "float32"),
-    "vy": ("sbuf", [128, 16], "float32"), "l1": ("sbuf", [128, 16], "uint16"),
-    "ev": ("sbuf", [128, 256], "bfloat16"), "pv": ("sbuf", [128, 256], "bfloat16"),
-    "kr": ("sbuf", [128, 8], "float32"), "kf": ("sbuf", [128, 8], "float32"), "lead": ("sbuf", [128, 32], "float32"),
-    "X1": ("sbuf", [128, 32], "float32"), "X2": ("sbuf", [128, 32], "float32"),
-    "Zi": ("sbuf", [128, 32], "int32"), "D": ("sbuf", [128, 32], "int32"), "Y1": ("sbuf", [128, 32], "int32"),
-    "Y2": ("sbuf", [128, 32], "int32"), "s1": ("sbuf", [128, 32], "int32"), "s2": ("sbuf", [128, 32], "int32"),
-    "off": ("sbuf", [128, 32], "uint16"), "fill": ("sbuf", [128, BL], "bfloat16"),
-    "WA": ("sbuf", [128, 8 * ST], "bfloat16"), "WB": ("sbuf", [128, 8 * ST], "bfloat16"),
-    "LD": ("sbuf", [128, 8 * BL + 16], "bfloat16"),
-    "vs": ("sbuf", [128, 8], "float32"), "vt": ("sbuf", [128, 8], "float32"), "vq": ("sbuf", [128, 8], "float32"),
-    "dk": ("sbuf", [128, 8], "float32"), "dl2": ("sbuf", [128, 8], "float32"),
-    "cm": ("sbuf", [128, 8 * 64], "bfloat16"),
+    "EI": ("sbuf", [128, 16], "int32"), "J": ("sbuf", [128, 128], "int32"), "VS": ("sbuf", [128, PG], "bfloat16"),
+    "QN": ("sbuf", [128, 8], "float32"), "t0w": ("sbuf", [128, 12], "float32"), "tr": ("sbuf", [128, 192], "float32"),
+    "ii": ("sbuf", [128, 8], "int32"), "pc": ("sbuf", [128, 16], "float32"), "ei": ("sbuf", [128, 16], "int32"),
+    "C": ("sbuf", [128, 16], "float32"), "Jg": ("sbuf", [128, 128], "int32"), "BO": ("sbuf", [128, 128], "bfloat16"),
+    "G": ("sbuf", [128, 128], "bfloat16"), "Lo": ("sbuf", [128, 128], "bfloat16"), "N5": ("sbuf", [128, 128], "bfloat16"),
+    "I": ("sbuf", [128, 128], "bfloat16"), "D0": ("sbuf", [128, 128], "bfloat16"), "D1": ("sbuf", [128, 128], "bfloat16"),
+    "ones": ("sbuf", [128, 16], "bfloat16"), "m8": ("sbuf", [128, 8], "float32"), "tw": ("sbuf", [128, 12], "float32"),
+    "rd0": ("sbuf", [128, 32], "int32"), "rd1": ("sbuf", [128, 32], "int32"),
+    "va0": ("sbuf", [128, PG + 16], "bfloat16"), "va1": ("sbuf", [128, PG + 16], "bfloat16"),
+    "lv": ("sbuf", [128, 64], "bfloat16"),
+    "B": ("sbuf", [128, 8], "float32"), "dt": ("sbuf", [128, 8], "float32"), "lm": ("sbuf", [128, 8], "float32"),
+    "lim": ("sbuf", [128, 1], "float32"), "cm": ("sbuf", [128, 96], "bfloat16"), "cq": ("sbuf", [128, 192], "bfloat16"),
+    "gs": ("sbuf", [128, 12], "float32"), "g1": ("sbuf", [128, 12], "uint16"), "Qs": ("sbuf", [128, 192], "bfloat16"),
+    "Sg": ("sbuf", [128, 192], "bfloat16"),
+    "st": ("sbuf", [128, 64], "float32"), "nz": ("sbuf", [128, 64], "float32"), "of": ("sbuf", [128, 64], "float32"),
     "Wt": ("sbuf", [128, 64], "uint16"), "Y": ("sbuf", [128, 1024], "bfloat16"),
-    "ps1": ("psum", [128, 512], "float32"), "ps2": ("psum", [128, 512], "float32"),
-    "pb": ("psum", [128, 512], "float32"), "pw": ("psum", [128, 512], "float32"), "pl": ("psum", [128, 512], "float32"),
-    "pz": ("psum", [128, 512], "float32"), "pe": ("psum", [128, 512], "float32"), "pk": ("psum", [128, 512], "float32"),
+    "LD": ("sbuf", [128, V0 + 8 * PG], "bfloat16"), "LP": ("sbuf", [128, 8 * PG + 16], "bfloat16"),
+    "pR": ("psum", [128, 512], "float32"), "pB": ("psum", [128, 512], "float32"), "pA": ("psum", [128, 512], "float32"),
+    "pT": ("psum", [128, 512], "float32"), "pG": ("psum", [128, 512], "float32"), "pQ": ("psum", [128, 512], "float32"),
+    "pS": ("psum", [128, 512], "float32"),
 }
-SEMAPHORES = (["qv", "qs", "qt", "qg", "drl", "ddl", "dval", "dy", "dz", "loc"]
-              + ["%s%d" % (x, i) for x in "huvab" for i in range(8)])
+for _i in "01":
+    SCRATCH.update({
+        "z" + _i: ("sbuf", [128, 16], "bfloat16"), "cz" + _i: ("sbuf", [128, 16], "bfloat16"),
+        "ti" + _i: ("sbuf", [128, 32], "bfloat16"), "tt" + _i: ("sbuf", [128, 32], "bfloat16"),
+        "mm" + _i: ("sbuf", [128, 16], "float32"), "sm" + _i: ("sbuf", [128, 16], "float32"),
+        "of" + _i: ("sbuf", [128, 16], "uint16"), "cs" + _i: ("sbuf", [128, 16], "float32"),
+        "xx" + _i: ("sbuf", [128, 16], "float32"), "l1" + _i: ("sbuf", [128, 16], "uint16")})
+SEMAPHORES = (["qv", "qs", "qt", "qg", "drl", "ddl", "dval", "dy", "dz", "loc", "u", "v"]
+              + ["%s%d" % (x, i) for x in "hpqef" for i in range(8)])
 
 
 def bits(es):
@@ -64,17 +57,10 @@ def rank_program(g, core, T, topo):
     def peer_of(r):
         return far[home.index(r)]
     peer = peer_of(rank)
+    pages = [rank, peer]
     efar = topo.engines(core, cores[far[0]])
     eall = topo.engines(core, cores[near[0]])
     enear = [e for e in eall if e not in efar]
-
-    def shares(me, second):
-        ds = [r for r in home if r != me]
-        h = len(eall) // 2
-        one, two = eall[:h], eall[h:]
-        if second:
-            one, two = two, one
-        return {ds[0]: one, ds[1]: two[:h // 2], ds[2]: two[h // 2:]}
 
     q = {"qv": g.vector, "qs": g.scalar, "qt": g.tensor, "qg": g, "sync": g.sync}
     cnt = {"qv": 0, "qs": 0, "qt": 0, "qg": 0}
@@ -139,6 +125,9 @@ def rank_program(g, core, T, topo):
     def scan(out, a, b, init, r, w):
         op("qv", lambda v: v.tensor_tensor_scan(out, a, b, init, A.mult, A.add), r, w)
 
+    def iota(out, pat, base, cm, w):
+        op("qg", lambda x: x.iota(out, pat, base, cm, allow_small_or_imprecise_dtypes=True), [], w)
+
     loc = [0]
 
     def send(parts, r):
@@ -151,180 +140,167 @@ def rank_program(g, core, T, topo):
             loc[0] += len(es)
         g.remote_dma_fused(trs, local_sem=T.sem.loc)
 
-    dma("sync", T.rli[:], T.rl[:], "drl", [], ["rli0"])
-    dma("qs", T.dli[:], T.dl[:], "ddl", [], ["dli"])
-    dma("sync", T.valt[:, 0:256], T.val[:], "dval", [], ["val0"])
+    dma("sync", T.rd0[:, 0:16], T.rl[:], "drl", [], ["rl0"])
+    dma("qs", T.rd0[:, 16:32], T.dl[:], "ddl", [], ["dl0"])
+    dma("sync", T.va0[:, 0:PG], T.val[:], "dval", [], ["va0"])
 
-    at = LV * rank
-    op("qg", lambda x: x.iota(T.Pi[:], [[0, 1]], 0, 1), [], ["Pi"])
-    op("qg", lambda x: x.iota(T.Kt[:], [[1, 8], [0, 16]], 0, 0, allow_small_or_imprecise_dtypes=True), [], ["Kt"])
-    op("qg", lambda x: x.iota(T.J[:], [[1, 128]], 0, 0, allow_small_or_imprecise_dtypes=True), [], ["J"])
-    send([(T.rli[:], T.rlp[:], [peer], efar, "u%d" % rank)], ["rli0"])
-    ms(T.fill[:], -2.0, ["fill"])
-    for d in home:
-        act(T.WA[:, ST * d:ST * d + BL], T.fill[:], ["fill"], ["WA"])
-    for d in home[:2]:
-        act(T.WB[:, ST * d:ST * d + BL], T.fill[:], ["fill"], ["WB"])
+    op("qg", lambda x: x.iota(T.EI[:], [[1, 16]], 0, 16), [], ["EI"])
+    op("qg", lambda x: x.iota(T.J[:], [[1, 128]], 0, 0), [], ["J"])
+    iota(T.VS[:], [[1, 16], [16, 16]], 0, 0, ["VS"])
+    send([(T.rd0[:], T.rd1[:], [peer], efar, "u")], ["rl0", "dl0"])
     ms(T.ones[:], 1.0, ["ones"])
-    ms(T.mone[:], -1.0, ["mone"])
-    ms(T.lv[:, at:at + 8], 0.0, ["lvz"])
-    ms(T.valt[:, 256:272], -1.0, ["val1"])
-    ts(T.pd[:, 0:1], T.Pi[:], 4, None, A.logical_shift_right, None, ["Pi"], ["pd0"])
-    ts(T.pd[:, 1:2], T.Pi[:], 15, None, A.bitwise_and, None, ["Pi"], ["pd1"])
-    cp(T.pc[:, 2:3], T.Pi[:], ["Pi"], ["pc2"])
-    ts(T.pc[:, 3:4], T.Pi[:], 1.0, None, A.add, None, ["Pi"], ["pc3"])
-    cp(T.pc[:, 0:1], T.pd[:, 0:1], ["pd0"], ["pc0"])
-    ts(T.pc[:, 4:5], T.pd[:, 1:2], 15.0, 32.0, A.is_equal, A.mult, ["pd1"], ["pc4"])
-    ts(T.BO[:], T.Kt[:], T.pc[:, 0:1], None, A.is_equal, None, ["Kt", "pc0"], ["BO"])
-    ms(T.neg[:], -0.0625, ["neg"])
-    tt(T.bj[:], T.BO[:], T.J[:], A.mult, ["BO", "J"], ["bj"])
-    ts(T.Bk[:], T.BO[:], 256.0, None, A.mult, None, ["BO"], ["Bk"])
-    ts(T.Lo[:], T.bj[:], T.pc[:, 2:3], None, A.is_gt, None, ["bj", "pc2"], ["Lo"])
-    ts(T.Sh[:], T.bj[:], T.pc[:, 3:4], 2.0, A.is_equal, A.mult, ["bj", "pc3"], ["Sh"])
-    ts(T.S15[:], T.BO[:], T.pc[:, 4:5], None, A.mult, None, ["BO", "pc4"], ["S15"])
+    ms(T.cs0[:], 0.0, ["cs0"])
+    ms(T.cs1[:], 0.0, ["cs1"])
+    e0 = T.EI[:, 0:1]
+    ts(T.ii[:, 0:1], e0, 8, None, A.logical_shift_right, None, ["EI"], ["ii0"])
+    ts(T.ii[:, 1:2], e0, 8, 1, A.logical_shift_right, A.bitwise_and, ["EI"], ["ii1"])
+    ts(T.ei[:], T.EI[:], 255, None, A.bitwise_and, None, ["EI"], ["ei"])
+    ts(T.pc[:, 3:4], e0, 0.0625, None, A.mult, None, ["EI"], ["pc3"])
+    cp(T.pc[:, 0:1], T.ii[:, 0:1], ["ii0"], ["pc0"])
+    cp(T.pc[:, 2:3], T.ii[:, 1:2], ["ii1"], ["pc2"])
+    ts(T.pc[:, 1:2], T.ii[:, 1:2], -1.0, 1.0, A.mult, A.add, ["ii1"], ["pc1"])
+    ts(T.C[:], T.ei[:], -1.0, 256.0, A.mult, A.add, ["ei"], ["C"])
+    ts(T.Jg[:], T.J[:], 4, None, A.logical_shift_right, None, ["J"], ["Jg"])
+    ts(T.G[:], T.J[:], T.pc[:, 3:4], None, A.is_gt, None, ["J", "pc3"], ["G"])
+    ts(T.BO[:], T.Jg[:], T.pc[:, 0:1], None, A.is_equal, None, ["Jg", "pc0"], ["BO"])
+    ts(T.N5[:], T.J[:], T.pc[:, 3:4], -512.0, A.is_equal, A.mult, ["J", "pc3"], ["N5"])
+    tt(T.Lo[:], T.G[:], T.BO[:], A.mult, ["G", "BO"], ["Lo"])
+    ts(T.pc[:, 4:5], T.C[:, 0:1], 128.0, None, A.is_gt, None, ["C"], ["pc4"])
+    ts(T.pc[:, 5:6], T.C[:, 0:1], 128.0, None, A.is_le, None, ["C"], ["pc5"])
+    own = LVR = "lv%d" % rank
 
-    src = [T.rli, T.rlp]
+    def t_(name, i):
+        return T["%s%d" % (name, i)]
 
-    def x16(t, i):
-        return t[:, 16 * i:16 * i + 16]
-
-    def items(i):
-        k = "%d" % i
-        cp(x16(T.rb, i), src[i][:], ["rli" + k], ["rb" + k])
-        scan(x16(T.w0, i), x16(T.rb, i), x16(T.rb, i), 0.0, ["rb" + k], ["w0" + k])
+    def k_(*names):
+        return lambda i: ["%s%d" % (x, i) for x in names]
 
     def starts(i):
-        k = "%d" % i
-        ts(x16(T.z, i), src[i][:], -1.0, 1.0, A.mult, A.add, ["rli" + k], ["z" + k])
-        scan(x16(T.cz, i), T.ones[:], x16(T.z, i), 0.0, ["ones", "z" + k], ["cz" + k])
+        s = "%d" % i
+        ts(t_("z", i)[:], t_("rd", i)[:, 0:16], -1.0, 1.0, A.mult, A.add, ["rl" + s], ["z" + s])
+        scan(t_("cz", i)[:], T.ones[:], t_("z", i)[:], 0.0, ["ones", "z" + s], ["cz" + s])
+
+    def turn(i):
+        s = "%d" % i
+        ts(t_("ti", i)[:, 0:16], t_("rd", i)[:, 16:32], T.pc[:, 1:2], None, A.mult, None, ["dl" + s, "pc1"], ["tia" + s])
+        ts(t_("ti", i)[:, 16:32], t_("rd", i)[:, 16:32], T.pc[:, 2:3], None, A.mult, None, ["dl" + s, "pc2"], ["tib" + s])
+        op("qv", lambda v: v.transpose(t_("tt", i)[:], t_("ti", i)[:]), ["tia" + s, "tib" + s], ["tt" + s])
 
     def sums(i):
-        k = "%d" % i
-        c = 16 * i + 15
-        mm(T.ps1[:, 2 * i:2 * i + 1], T.Lo[:], T.cz[:, c:c + 1], ["Lo", "cz" + k], ["ps1"])
-        mm(T.ps1[:, 2 * i + 1:2 * i + 2], T.Sh[:], T.w0[:, c:c + 1], ["Sh", "w0" + k], ["ps1"])
+        s = "%d" % i
+        mm(T.pR[:, i:i + 1], T.Lo[:], t_("cz", i)[:, 15:16], ["Lo", "cz" + s], ["pR"])
+        a, b = t_("tt", i)[:, 0:16], t_("tt", i)[:, 16:32]
+        mm(T.pB[:, 0:16], T.BO[:], a, ["BO", "tt" + s], ["pB"], True, False)
+        mm(T.pB[:, 0:16], T.BO[:], b, [], ["pB"], False, True)
+        mm(T.pA[:, 0:16], T.Lo[:], a, ["Lo"], ["pA"], True, False)
+        mm(T.pA[:, 0:16], T.Lo[:], b, [], [], False, False)
+        mm(T.pA[:, 0:16], T.N5[:], a, ["N5"], [], False, False)
+        mm(T.pA[:, 0:16], T.N5[:], b, ["tt" + s], ["pA"], False, True)
 
-    def numbers(i):
-        k = "%d" % i
-        ts(x16(T.rw, i), x16(T.rb, i), 2.0, None, A.mult, None, ["rb" + k], ["rw" + k])
-        ts(x16(T.nr, i), x16(T.cz, i), T.ps1[:, 2 * i:2 * i + 1], 16.0, A.add, A.mult, ["cz" + k, "ps1"], ["nr" + k])
-        scan(x16(T.nw, i), x16(T.rb, i), x16(T.rw, i), T.ps1[:, 2 * i + 1:2 * i + 2], ["rb" + k, "rw" + k, "ps1"], ["nw" + k])
-        ts(x16(T.lead, i), x16(T.nr, i), 0.0, None, A.is_equal, None, ["nr" + k], ["lead" + k])
+    def lists(i):
+        s = "%d" % i
+        tt(t_("mm", i)[:], t_("rd", i)[:, 0:16], T.C[:], A.mult, ["rl" + s, "C"], ["mm" + s])
+        tt(t_("sm", i)[:], t_("cz", i)[:], t_("mm", i)[:], A.add, ["cz" + s, "mm" + s], ["sm" + s])
+        scan(t_("cs", i)[:, 1:16], T.ones[:, 0:15], T.pB[:, 0:15], 0.0, ["ones", "pB", "cs" + s], ["cs" + s])
+        ts(t_("of", i)[:], t_("sm", i)[:], T.pR[:, i:i + 1], -1.0, A.add, A.add, ["sm" + s, "pR"], ["of" + s])
+        tt(t_("xx", i)[:], t_("cs", i)[:], T.pA[:, 0:16], A.add, ["cs" + s, "pA"], ["xx" + s])
+        ts(t_("l1", i)[:], t_("xx", i)[:], 512.0, 256.0, A.add, A.min, ["xx" + s], ["l1" + s])
 
-    cp(T.rb[:, 0:16], T.rli[:], ["rli0"], ["rb0"])
-    cp(T.lv[:, at + 17:at + 18], T.rli[:, 0:1], ["rli0"], ["lvc"])
-    scan(T.cr[:], T.ones[:], T.rb[:, 0:16], 0.0, ["ones", "rb0"], ["cr"])
-    scan(T.w0[:, 0:16], T.rb[:, 0:16], T.rb[:, 0:16], 0.0, ["rb0"], ["w00"])
-    ts(T.lv[:, at + 8:at + 16], T.mone[:, 0:8], T.cr[:, 15:16], 16.0, A.mult, A.add, ["cr", "mone"], ["lva"])
-    cp(T.lv[:, at + 16:at + 17], T.w0[:, 15:16], ["w00"], ["lvb"])
-    own = ["lva", "lvb", "lvc", "lvz"]
-    sl = T.lv[:, at:at + LW]
-    send([(sl, sl, far, efar, "h%d" % rank), (sl, sl, near, enear, "h%d" % rank)], own)
+    def table(i):
+        p = pages[i]
+        cp(T.LP[:, PG * p:PG * p + PG].indirect(t_("of", i)[:, 0:16]), T.VS[:], ["of%d" % i, "VS"], ["P%d" % p])
 
-    cp(T.db[:], T.dli[:], ["dli"], ["db"])
-    ts(T.z[:, 0:16], T.rli[:], -1.0, 1.0, A.mult, A.add, ["rli0"], ["z0"])
-    scan(T.cd[:], T.ones[:], T.db[:], 0.0, ["ones", "db"], ["cd"])
-    mm(T.ps2[:, 0:1], T.Lo[:], T.cd[:, 15:16], ["Lo", "cd"], ["ps2"])
-    scan(T.cz[:, 0:16], T.ones[:], T.z[:, 0:16], 0.0, ["ones", "z0"], ["cz0"])
+    def vals(i):
+        p = pages[i]
+        act(T.LD[:, V0 + PG * p:V0 + PG * p + PG], t_("va", i)[:, 0:PG + 16].indirect(t_("l1", i)[:, 0:16]),
+            ["va%d" % i, "vn%d" % i, "l1%d" % i], ["E%d" % p])
+
+    def share(buf, at, key, es, sem):
+        sl = buf[:, at:at + PG]
+        send([(sl, sl, near, es, "%s%d" % (sem, rank))], [key])
+
+    starts(0)
+    act(T.lv[:, 8 * rank:8 * rank + 2], T.cz0[:, 14:16], ["cz0"], [own])
+    cc = T.cz0[:, 14:16]
+    ld = T.lv[:, 8 * rank:8 * rank + 2]
+    send([(cc, ld, far, efar, "h%d" % rank), (cc, ld, near, enear, "h%d" % rank)], ["cz0"])
+    send([(T.va0[:, 0:PG], T.va1[:, 0:PG], [peer], efar, "v")], ["va0"])
+    turn(0)
     sums(0)
-    ts(T.pc[:, 5:6], T.pd[:, 1:2], 0.0, None, A.is_equal, None, ["pd1"], ["pc5"])
-    ts(T.vx[:], T.cd[:], T.ps2[:, 0:1], -257.0, A.add, A.add, ["cd", "ps2"], ["vx"])
-    ts(T.Id[:], T.J[:], T.pc[:, 2:3], 16.0, A.is_equal, A.mult, ["J", "pc2"], ["Id"])
-    tt(T.vy[:], T.vx[:], T.db[:], A.mult, ["vx", "db"], ["vy"])
-    ms(T.neg2[:], -0.53125, ["neg2"])
-    ts(T.l1[:], T.vy[:], 256.0, None, A.add, None, ["vy"], ["l1"])
-    act(T.ev[:], T.valt[:, 0:272].indirect(T.l1[:, 0:16]), ["val0", "val1", "l1"], ["ev"])
-    send([(T.ev[:], T.pv[:], [peer], efar, "v%d" % rank)], ["ev"])
-    for d in home[2:]:
-        act(T.WB[:, ST * d:ST * d + BL], T.fill[:], ["fill"], ["WB"])
-    numbers(0)
+    ms(T.va0[:, PG:PG + 16], -1.0, ["vn0"])
+    lists(0)
+    vals(0)
+    table(0)
+    iota(T.QN[:], [[-16, 8]], 256, 0, ["QN"])
+    iota(T.t0w[:], [[1, 3], [256, 4]], 256 + 2 * rank, 0, ["t0w"])
+    iota(T.tr[:], [[1, 3], [16, 64]], 2 * rank, 0, ["tr"])
+    share(T.LD, V0 + PG * rank, "E%d" % rank, enear, "e")
+    share(T.LP, PG * rank, "P%d" % rank, eall, "p")
+    ms(T.va1[:, PG:PG + 16], -1.0, ["vn1"])
+    ts(T.I[:], T.J[:], T.pc[:, 3:4], None, A.is_equal, None, ["J", "pc3"], ["I"])
+    act(T.D0[:], T.I[:], ["I", "pc4"], ["D0"], 0.0, T.pc[:, 4:5])
+    act(T.D1[:], T.I[:], ["I", "pc5"], ["D1"], 0.0, T.pc[:, 5:6])
 
-    note(("u%d" % peer, len(efar)), [], ["rli1"])
+    note(("u", len(efar)), [], ["rl1", "dl1"])
+    note(("v", len(efar)), [], ["va1"])
     for s in near:
-        note(("h%d" % s, len(enear)), [], ["h%d" % s])
+        note(("h%d" % s, len(enear)), [], ["lv%d" % s])
     for s in far:
-        note(("h%d" % s, len(efar)), [], ["h%d" % s])
-    note(("v%d" % peer, len(efar)), [], ["pv"])
-    every = ["h%d" % s for s in near + far] + own
-    pages = [rank, peer]
+        note(("h%d" % s, len(efar)), [], ["lv%d" % s])
 
-    def entries(i):
-        k = "%d" % i
-        mm(x16(T.pe, i), T.Id[:], x16(T.nr, i), ["Id", "nr" + k], [], True, False)
-        mm(x16(T.pe, i), T.Id[:], x16(T.nw, i), ["nw" + k], ["pe" + k], False, True)
-
-    def add_base(p, s, keys, key, last):
-        a = LV * s + 7 - s
-        mm(p[:, 0:9], T.Bk[:], T.lv[:, a:a + 9], keys, [key] if last else [], False, last)
-    mm(T.pb[:, 0:9], T.Bk[:], T.neg[:, 0:9], ["Bk", "neg"], [], True, False)
-    mm(T.pk[:, 0:9], T.Bk[:], T.neg2[:, 0:9], ["Bk", "neg2"], [], True, False)
-    add_base(T.pb, rank, own, "pb", False)
-    add_base(T.pk, rank, own, "pk", False)
-    entries(0)
-    items(1)
     starts(1)
+    turn(1)
     sums(1)
-    numbers(1)
-    entries(1)
-    for s in near:
-        add_base(T.pb, s, ["h%d" % s], "pb", False)
-        add_base(T.pk, s, ["h%d" % s], "pk", False)
-    mm(T.pw[:, 0:8], T.S15[:], T.lv[:, 16:8 * LV:LV], every + ["S15"], ["pw"])
-    for s in far:
-        add_base(T.pb, s, ["h%d" % s], "pb", s == far[-1])
-    for s in far:
-        add_base(T.pk, s, ["h%d" % s], "pk", s == far[-1])
+    lists(1)
+    table(1)
+    share(T.LP, PG * peer, "P%d" % peer, eall, "q")
+    vals(1)
+    share(T.LD, V0 + PG * peer, "E%d" % peer, eall, "f")
 
-    act(T.kr[:], T.pk[:, 0:8], ["pk"], ["kr"], RND, 1.0 / 4096)
-    act(T.kf[:], T.kr[:], ["kr"], ["kf"], -16.0 * RND, 16.0)
-    for i, p in enumerate(pages):
-        ts(x16(T.X1, i), x16(T.lead, i), T.pw[:, p - 1:p] if p else 0.0, None, A.mult, None, ["lead%d" % i, "pw"], ["X1%d" % i])
-    tt(T.X2[:], T.X1[:], T.pe[:, 0:32], A.add, ["X10", "X11", "pe0", "pe1"], ["X2"])
-    for i, p in enumerate(pages):
-        ts(x16(T.Zi, i), x16(T.X2, i), T.pb[:, p:p + 1], None, A.add, None, ["X2", "pb"], ["Z%d" % i])
-    zk = ["Z0", "Z1"]
-    ts(T.Y1[:], T.Zi[:], 8, 0xFFF0, A.logical_shift_right, A.bitwise_and, zk, ["Y1"])
-    ts(T.Y2[:], T.Zi[:], 5, 15, A.logical_shift_right, A.bitwise_and, zk, ["Y2"])
-    ts(T.D[:], T.Zi[:], 0xE00, None, A.bitwise_and, None, zk, ["D"])
-    tt(T.s1[:], T.Y1[:], T.Y2[:], A.add, ["Y1", "Y2"], ["s1"])
-    tt(T.s2[:], T.s1[:], T.D[:], A.add, ["s1", "D"], ["s2"])
-    for i, p in enumerate(pages):
-        ts(x16(T.off, i), x16(T.s2, i), T.kf[:, p:p + 1], None, A.subtract, None, ["s2", "kf"], ["off%d" % i])
-    for i, (win, val, vk, tag) in enumerate([(T.WA, T.ev, "ev", "a"), (T.WB, T.pv, "pv", "b")]):
-        wk = "WA" if i == 0 else "WB"
-        cp(win[:, 0:8 * ST].indirect(x16(T.off, i)), val[:], ["off%d" % i, vk, wk], [wk])
-        p = pages[i]
-        es = shares(rank, i == 1)
-        send([(win[:, ST * d:ST * d + BL], T.LD[:, BL * p:BL * p + BL], [d], es[d], "%s%d" % (tag, rank)) for d in near], [wk])
-
-    ts(T.S0[:], T.BO[:], T.pc[:, 5:6], None, A.mult, None, ["BO", "pc5"], ["S0"])
-    mm(T.pl[:, 0:8], T.S0[:], T.lv[:, 17:8 * LV:LV], every + ["S0"], ["pl"])
-    ts(T.pc[:, 7:8], T.pd[:, 1:2], 32.0, 512.0 * rank - 256.0, A.mult, A.add, ["pd1"], ["pc7"])
-    ts(T.vs[:, 0:7], T.pw[:, 0:7], -224.0, None, A.add, None, ["pw"], ["vs"])
-    tt(T.dk[:, 0:7], T.kf[:, 0:7], T.kf[:, 1:8], A.subtract, ["kf"], ["dk"])
-    ts(T.VZ[:], T.J[:, 0:64], 4096.0, T.pc[:, 7:8], A.mult, A.add, ["J", "pc7"], ["VZ"])
-    tt(T.vt[:, 0:7], T.vs[:, 0:7], T.pl[:, 1:8], A.mult, ["vs", "pl"], ["vt"])
-    ts(T.dl2[:, 0:7], T.dk[:, 0:7], 0.0625, BL / 16.0, A.mult, A.add, ["dk"], ["dl2"])
-    ts(T.pc[:, 6:7], T.pd[:, 1:2], 16.0, None, A.add, None, ["pd1"], ["pc6"])
-    tt(T.vq[:, 0:7], T.vt[:, 0:7], T.pb[:, 1:8], A.add, ["vt", "pb"], ["vq"])
-    ms(T.LD[:, 8 * BL:8 * BL + 16], -2.0, ["LDend"])
-    mm(T.pz[:, 0:64], T.Id[:], T.J[:, 0:64], ["Id", "J"], [], True, False)
-    for x in [7, 0, 1, 2, 3, 4, 5, 6]:
-        lim = T.vq[:, x:x + 1] if x < 7 else T.pb[:, 8:9]
-        ts(T.cm[:, 64 * x:64 * x + 64], T.VZ[:], lim, T.dl2[:, x:x + 1] if x < 7 else 1024.0, A.is_ge, A.mult,
-           ["VZ", "vq", "dl2"] if x < 7 else ["VZ", "pb"], ["cm%d" % x])
-        mm(T.pz[:, 0:64], T.Id[:], T.cm[:, 64 * x:64 * x + 64], ["cm%d" % x], ["pz"] if x == 6 else [], False, x == 6)
-    for i, (win, wk) in enumerate([(T.WA, "WA"), (T.WB, "WB")]):
-        p = pages[i]
-        act(T.LD[:, BL * p:BL * p + BL], win[:, ST * rank:ST * rank + BL], [wk], ["L%d" % p])
-    ts(T.Wt[:], T.pz[:, 0:64], T.pc[:, 6:7], float(8 * BL), A.add, A.min, ["pz", "pc6"], ["Wt"])
+    mm(T.pT[:, 0:8], T.BO[:], T.lv[:, 1:64:8], ["lv%d" % s for s in range(n)] + ["BO"], ["pT"])
+    ts(T.tw[:], T.t0w[:], T.C[:, 0:1], None, A.subtract, None, ["t0w", "C"], ["tw"])
+    ts(T.m8[:], T.QN[:], T.C[:, 0:1], None, A.is_equal, None, ["QN", "C"], ["m8"])
+    ms(T.LP[:, 8 * PG:8 * PG + 16], 0.0, ["Pend"])
+    ms(T.LD[:, 0:V0], -2.0, ["E"])
+    ts(T.pc[:, 7:8], T.pc[:, 4:5], 256.0, None, A.mult, None, ["pc4"], ["pc7"])
+    scan(T.B[:], T.ones[:, 0:8], T.pT[:, 0:8], 0.0, ["ones", "pT"], ["B"])
+    ts(T.dt[:], T.pT[:, 0:8], -1.0, 256.0, A.mult, A.add, ["pT"], ["dt"])
+    tt(T.lm[:], T.B[:], T.m8[:], A.mult, ["B", "m8"], ["lm"])
+    for x in range(8):
+        c = T.cm[:, 12 * x:12 * x + 12]
+        ts(c, T.tw[:], T.B[:, x:x + 1], T.dt[:, x:x + 1], A.is_ge, A.mult, ["tw", "B", "dt"], ["cm%d" % x])
+        mm(T.pG[:, 0:12], T.I[:], c, ["I", "cm%d" % x], ["pG"] if x == 7 else [], x == 0, x == 7)
+    op("qv", lambda v: v.tensor_reduce(T.lim[:], T.lm[:], X.X, A.add), ["lm"], ["lim"])
+    tt(T.gs[:], T.tw[:], T.pG[:, 0:12], A.add, ["tw", "pG"], ["gs"])
+    ts(T.cq[:], T.tr[:], T.lim[:], T.pc[:, 7:8], A.is_ge, A.mult, ["tr", "lim", "pc7"], ["cq"])
+    ts(T.g1[:], T.gs[:], float(8 * PG), None, A.min, None, ["gs"], ["g1"])
+    mm(T.pQ[:, 0:192], T.BO[:], T.cq[:], ["BO", "cq"], ["pQ"])
+    ts(T.ii[:, 2:3], e0, 4, 7, A.logical_shift_right, A.bitwise_and, ["EI"], ["ii2"])
+    cp(T.pc[:, 6:7], T.ii[:, 2:3], ["ii2"], ["pc6"])
+    act(T.Qs[:], T.pQ[:, 0:192], ["pQ"], ["Qs"], float(V0))
 
     for s in near:
-        note(("a%d" % s, len(shares(s, False)[rank])), [], ["L%d" % s])
-        note(("b%d" % s, len(shares(s, True)[rank])), [], ["L%d" % peer_of(s)])
-    rd = ["L%d" % s for s in home + far] + ["LDend", "Wt"]
-    act(T.Y[:, 512:1024], T.LD[:, 0:8 * BL + 16].indirect(T.Wt[:, 32:64]), rd, ["Yb"])
-    cp(T.Y[:, 0:512], T.LD[:, 0:8 * BL + 16].indirect(T.Wt[:, 0:32]), rd, ["Ya"])
+        note(("p%d" % s, len(eall)), [], ["P%d" % s])
+        note(("q%d" % s, len(eall)), [], ["P%d" % peer_of(s)])
+        note(("e%d" % s, len(enear)), [], ["E%d" % s])
+        note(("f%d" % s, len(eall)), [], ["E%d" % peer_of(s)])
+    rd = ["P%d" % s for s in range(n)] + ["Pend", "g1"]
+    win = T.LP[:, 0:8 * PG + 16]
+    act(T.Sg[:, 96:192], win.indirect(T.g1[:, 6:12]), rd, ["Sgb"])
+    cp(T.Sg[:, 0:96], win.indirect(T.g1[:, 0:6]), rd, ["Sga"])
+    mm(T.pS[:, 0:128], T.D0[:], T.Qs[:, 0:128], ["D0", "Qs"], [], True, False)
+    mm(T.pS[:, 0:128], T.D1[:], T.Qs[:, 64:192], ["D1"], [], False, False)
+    mm(T.pS[:, 0:128], T.D0[:], T.Sg[:, 0:128], ["Sga", "Sgb"], [], False, False)
+    mm(T.pS[:, 0:128], T.D1[:], T.Sg[:, 64:192], [], ["pS"], False, True)
+    ts(T.st[:], T.pS[:, 0:64], T.pc[:, 6:7], None, A.add, None, ["pS", "pc6"], ["st"])
+    tt(T.nz[:], T.st[:], T.pS[:, 64:128], A.is_lt, ["st", "pS"], ["nz"])
+    tt(T.of[:], T.st[:], T.nz[:], A.mult, ["st", "nz"], ["of"])
+    cp(T.Wt[:], T.of[:], ["of"], ["Wt"])
+
+    rd = ["E%d" % s for s in range(n)] + ["E", "Wt"]
+    win = T.LD[:, 0:V0 + 8 * PG]
+    act(T.Y[:, 512:1024], win.indirect(T.Wt[:, 32:64]), rd, ["Yb"])
+    cp(T.Y[:, 0:512], win.indirect(T.Wt[:, 0:32]), rd, ["Ya"])
     dma("qs", T.y[:, 512:1024], T.Y[:, 512:1024], "dz", ["Yb"], [])
     dma("sync", T.y[:, 0:512], T.Y[:, 0:512], "dy", ["Ya"], [])
 

@@ -2,39 +2,27 @@ from concourse.bass import DstId, RemoteDMATransfer
 from concourse.mybir import AluOpType as A, ActivationFunctionType as F, AxisListType as X
 
 PG = 256
+HF = 128
 V0 = 16
-
-SCRATCH = {
-    "EI": ("sbuf", [128, 16], "int32"), "J": ("sbuf", [128, 128], "int32"), "VS": ("sbuf", [128, PG], "bfloat16"),
-    "QN": ("sbuf", [128, 8], "float32"), "t0w": ("sbuf", [128, 12], "float32"), "tr": ("sbuf", [128, 192], "float32"),
-    "ii": ("sbuf", [128, 8], "int32"), "pc": ("sbuf", [128, 16], "float32"), "ei": ("sbuf", [128, 16], "int32"),
-    "C": ("sbuf", [128, 16], "float32"), "Jg": ("sbuf", [128, 128], "int32"), "BO": ("sbuf", [128, 128], "bfloat16"),
-    "G": ("sbuf", [128, 128], "bfloat16"), "Lo": ("sbuf", [128, 128], "bfloat16"), "N5": ("sbuf", [128, 128], "bfloat16"),
-    "I": ("sbuf", [128, 128], "bfloat16"), "D0": ("sbuf", [128, 128], "bfloat16"), "D1": ("sbuf", [128, 128], "bfloat16"),
-    "ones": ("sbuf", [128, 16], "bfloat16"), "m8": ("sbuf", [128, 8], "float32"), "tw": ("sbuf", [128, 12], "float32"),
-    "rd0": ("sbuf", [128, 32], "int32"), "rd1": ("sbuf", [128, 32], "int32"),
-    "va0": ("sbuf", [128, PG + 16], "bfloat16"), "va1": ("sbuf", [128, PG + 16], "bfloat16"),
-    "lv": ("sbuf", [128, 64], "bfloat16"),
-    "B": ("sbuf", [128, 8], "float32"), "dt": ("sbuf", [128, 8], "float32"), "lm": ("sbuf", [128, 8], "float32"),
-    "lim": ("sbuf", [128, 1], "float32"), "cm": ("sbuf", [128, 96], "bfloat16"), "cq": ("sbuf", [128, 192], "bfloat16"),
-    "gs": ("sbuf", [128, 12], "float32"), "g1": ("sbuf", [128, 12], "uint16"), "Qs": ("sbuf", [128, 192], "bfloat16"),
-    "Sg": ("sbuf", [128, 192], "bfloat16"),
-    "st": ("sbuf", [128, 64], "float32"), "nz": ("sbuf", [128, 64], "float32"), "of": ("sbuf", [128, 64], "float32"),
-    "Wt": ("sbuf", [128, 64], "uint16"), "Y": ("sbuf", [128, 1024], "bfloat16"),
-    "LD": ("sbuf", [128, V0 + 8 * PG], "bfloat16"), "LP": ("sbuf", [128, 8 * PG + 16], "bfloat16"),
-    "pR": ("psum", [128, 512], "float32"), "pB": ("psum", [128, 512], "float32"), "pA": ("psum", [128, 512], "float32"),
-    "pT": ("psum", [128, 512], "float32"), "pG": ("psum", [128, 512], "float32"), "pQ": ("psum", [128, 512], "float32"),
-    "pS": ("psum", [128, 512], "float32"),
-}
+b2, f4, i4, u2 = "bfloat16", "float32", "int32", "uint16"
+SCRATCH = {}
+for _n, _w, _d in [("EI", 16, i4), ("J", 128, i4), ("VS", PG, b2), ("QN", 8, f4), ("t0w", 12, f4), ("tr", 192, f4), ("ii", 8, i4),
+                   ("pc", 16, f4), ("ei", 16, i4), ("C", 16, f4), ("Jg", 128, i4), ("BO", 128, b2), ("G", 128, b2), ("Lo", 128, b2),
+                   ("N5", 128, b2), ("I", 128, b2), ("D0", 128, b2), ("D1", 128, b2), ("D2", 128, b2), ("D3", 128, b2),
+                   ("DW", 128, b2), ("ones", 64, b2), ("m8", 8, f4), ("tw", 12, f4),
+                   ("dli", 16, i4), ("lv", 64, b2), ("ti", 32, b2), ("tq", 32, b2), ("cs", 16, f4), ("xx", 16, f4), ("B", 8, f4),
+                   ("dt", 8, f4), ("lm", 8, f4), ("lim", 1, f4), ("cm", 96, b2), ("cq", 192, b2), ("gs", 12, f4), ("g1", 12, u2),
+                   ("Qs", 192, b2), ("Sg", 192, b2), ("nz", 64, f4), ("of", 64, f4), ("Wt", 64, u2), ("Y", 1024, b2),
+                   ("LD", V0 + 8 * PG, b2), ("LP", 8 * PG + 16, b2)]:
+    SCRATCH[_n] = ("sbuf", [128, _w], _d)
+for _n in "RBATGQSD":
+    SCRATCH["p" + _n] = ("psum", [128, 512], f4)
 for _i in "01":
-    SCRATCH.update({
-        "z" + _i: ("sbuf", [128, 16], "bfloat16"), "cz" + _i: ("sbuf", [128, 16], "bfloat16"),
-        "ti" + _i: ("sbuf", [128, 32], "bfloat16"), "tt" + _i: ("sbuf", [128, 32], "bfloat16"),
-        "mm" + _i: ("sbuf", [128, 16], "float32"), "sm" + _i: ("sbuf", [128, 16], "float32"),
-        "of" + _i: ("sbuf", [128, 16], "uint16"), "cs" + _i: ("sbuf", [128, 16], "float32"),
-        "xx" + _i: ("sbuf", [128, 16], "float32"), "l1" + _i: ("sbuf", [128, 16], "uint16")})
-SEMAPHORES = (["qv", "qs", "qt", "qg", "drl", "ddl", "dval", "dy", "dz", "loc", "u", "v"]
-              + ["%s%d" % (x, i) for x in "hpqef" for i in range(8)])
+    for _n, _w, _d in [("r", 16, i4), ("va", V0 + PG, b2), ("z", 16, b2), ("cz", 16, b2), ("mu", 16, f4), ("sm", 16, f4), ("o", 16, u2),
+                       ("l", 16, u2)]:
+        SCRATCH[_n + _i] = ("sbuf", [128, _w], _d)
+SEMAPHORES = (["qv", "qs", "qt", "qg", "drl", "ddl", "dval", "dy0", "dy1", "dy2", "dy3", "loc", "u", "w", "va", "vb"]
+              + ["%s%d" % (x, i) for x in "hpqek" for i in range(8)])
 
 
 def bits(es):
@@ -58,9 +46,10 @@ def rank_program(g, core, T, topo):
         return far[home.index(r)]
     peer = peer_of(rank)
     pages = [rank, peer]
-    efar = topo.engines(core, cores[far[0]])
+    efar = topo.engines(core, cores[peer])
     eall = topo.engines(core, cores[near[0]])
     enear = [e for e in eall if e not in efar]
+    EN = {"e": efar, "p": enear, "q": eall, "k": eall}
 
     q = {"qv": g.vector, "qs": g.scalar, "qt": g.tensor, "qg": g, "sync": g.sync}
     cnt = {"qv": 0, "qs": 0, "qt": 0, "qg": 0}
@@ -113,8 +102,8 @@ def rank_program(g, core, T, topo):
     def cp(out, a, r, w):
         op("qv", lambda v: v.tensor_copy(out, a), r, w)
 
-    def act(out, a, r, w, bias=0.0, scale=1.0):
-        op("qs", lambda s: s.activation(out, a, F.Copy, bias, scale), r, w)
+    def act(out, a, r, w, bias=0.0, scale=1.0, fn=F.Copy):
+        op("qs", lambda s: s.activation(out, a, fn, bias, scale), r, w)
 
     def ms(ap, c, w):
         op("qv", lambda v: v.memset(ap, c), [], w)
@@ -140,17 +129,23 @@ def rank_program(g, core, T, topo):
             loc[0] += len(es)
         g.remote_dma_fused(trs, local_sem=T.sem.loc)
 
-    dma("sync", T.rd0[:, 0:16], T.rl[:], "drl", [], ["rl0"])
-    dma("qs", T.rd0[:, 16:32], T.dl[:], "ddl", [], ["dl0"])
-    dma("sync", T.va0[:, 0:PG], T.val[:], "dval", [], ["va0"])
+    def share(parts):
+        send([(sl, sl, near, EN[x], "%s%d" % (x, rank)) for sl, key, x in parts], [p[1] for p in parts])
+
+    def arrive(x, s, key):
+        note(("%s%d" % (x, s), len(EN[x])), [], [key])
+
+    dma("sync", T.r0[:], T.rl[:], "drl", [], ["rl0"])
+    dma("qs", T.dli[:], T.dl[:], "ddl", [], ["dl"])
+    dma("sync", T.va0[:, V0:V0 + PG], T.val[:], "dval", [], ["va0"])
 
     op("qg", lambda x: x.iota(T.EI[:], [[1, 16]], 0, 16), [], ["EI"])
     op("qg", lambda x: x.iota(T.J[:], [[1, 128]], 0, 0), [], ["J"])
     iota(T.VS[:], [[1, 16], [16, 16]], 0, 0, ["VS"])
-    send([(T.rd0[:], T.rd1[:], [peer], efar, "u")], ["rl0", "dl0"])
+    send([(T.r0[:], T.r1[:], [peer], efar, "u")], ["rl0"])
     ms(T.ones[:], 1.0, ["ones"])
-    ms(T.cs0[:], 0.0, ["cs0"])
-    ms(T.cs1[:], 0.0, ["cs1"])
+    ms(T.cs[:], 0.0, ["cs"])
+    ms(T.va0[:, 0:V0], -1.0, ["vn0"])
     e0 = T.EI[:, 0:1]
     ts(T.ii[:, 0:1], e0, 8, None, A.logical_shift_right, None, ["EI"], ["ii0"])
     ts(T.ii[:, 1:2], e0, 8, 1, A.logical_shift_right, A.bitwise_and, ["EI"], ["ii1"])
@@ -163,106 +158,96 @@ def rank_program(g, core, T, topo):
     ts(T.Jg[:], T.J[:], 4, None, A.logical_shift_right, None, ["J"], ["Jg"])
     ts(T.G[:], T.J[:], T.pc[:, 3:4], None, A.is_gt, None, ["J", "pc3"], ["G"])
     ts(T.BO[:], T.Jg[:], T.pc[:, 0:1], None, A.is_equal, None, ["Jg", "pc0"], ["BO"])
-    ts(T.N5[:], T.J[:], T.pc[:, 3:4], -512.0, A.is_equal, A.mult, ["J", "pc3"], ["N5"])
     tt(T.Lo[:], T.G[:], T.BO[:], A.mult, ["G", "BO"], ["Lo"])
-    ts(T.pc[:, 4:5], T.C[:, 0:1], 128.0, None, A.is_gt, None, ["C"], ["pc4"])
-    ts(T.pc[:, 5:6], T.C[:, 0:1], 128.0, None, A.is_le, None, ["C"], ["pc5"])
-    own = LVR = "lv%d" % rank
-
-    def t_(name, i):
-        return T["%s%d" % (name, i)]
-
-    def k_(*names):
-        return lambda i: ["%s%d" % (x, i) for x in names]
 
     def starts(i):
         s = "%d" % i
-        ts(t_("z", i)[:], t_("rd", i)[:, 0:16], -1.0, 1.0, A.mult, A.add, ["rl" + s], ["z" + s])
-        scan(t_("cz", i)[:], T.ones[:], t_("z", i)[:], 0.0, ["ones", "z" + s], ["cz" + s])
+        z, cz = T["z" + s], T["cz" + s]
+        ts(z[:], T["r" + s][:], -1.0, 1.0, A.mult, A.add, ["rl" + s], ["z" + s])
+        scan(cz[:], T.ones[:, 0:16], z[:], 0.0, ["ones", "z" + s], ["cz" + s])
+        mm(T.pR[:, i:i + 1], T.Lo[:], cz[:, 15:16], ["Lo", "cz" + s], ["pR"])
 
-    def turn(i):
+    def places(i):
         s = "%d" % i
-        ts(t_("ti", i)[:, 0:16], t_("rd", i)[:, 16:32], T.pc[:, 1:2], None, A.mult, None, ["dl" + s, "pc1"], ["tia" + s])
-        ts(t_("ti", i)[:, 16:32], t_("rd", i)[:, 16:32], T.pc[:, 2:3], None, A.mult, None, ["dl" + s, "pc2"], ["tib" + s])
-        op("qv", lambda v: v.transpose(t_("tt", i)[:], t_("ti", i)[:]), ["tia" + s, "tib" + s], ["tt" + s])
+        tt(T["mu" + s][:], T["r" + s][:], T.C[:], A.mult, ["rl" + s, "C"], ["mu" + s])
+        tt(T["sm" + s][:], T["cz" + s][:], T["mu" + s][:], A.add, ["cz" + s, "mu" + s], ["sm" + s])
 
-    def sums(i):
+    def places_end(i):
         s = "%d" % i
-        mm(T.pR[:, i:i + 1], T.Lo[:], t_("cz", i)[:, 15:16], ["Lo", "cz" + s], ["pR"])
-        a, b = t_("tt", i)[:, 0:16], t_("tt", i)[:, 16:32]
-        mm(T.pB[:, 0:16], T.BO[:], a, ["BO", "tt" + s], ["pB"], True, False)
-        mm(T.pB[:, 0:16], T.BO[:], b, [], ["pB"], False, True)
-        mm(T.pA[:, 0:16], T.Lo[:], a, ["Lo"], ["pA"], True, False)
-        mm(T.pA[:, 0:16], T.Lo[:], b, [], [], False, False)
-        mm(T.pA[:, 0:16], T.N5[:], a, ["N5"], [], False, False)
-        mm(T.pA[:, 0:16], T.N5[:], b, ["tt" + s], ["pA"], False, True)
-
-    def lists(i):
-        s = "%d" % i
-        tt(t_("mm", i)[:], t_("rd", i)[:, 0:16], T.C[:], A.mult, ["rl" + s, "C"], ["mm" + s])
-        tt(t_("sm", i)[:], t_("cz", i)[:], t_("mm", i)[:], A.add, ["cz" + s, "mm" + s], ["sm" + s])
-        scan(t_("cs", i)[:, 1:16], T.ones[:, 0:15], T.pB[:, 0:15], 0.0, ["ones", "pB", "cs" + s], ["cs" + s])
-        ts(t_("of", i)[:], t_("sm", i)[:], T.pR[:, i:i + 1], -1.0, A.add, A.add, ["sm" + s, "pR"], ["of" + s])
-        tt(t_("xx", i)[:], t_("cs", i)[:], T.pA[:, 0:16], A.add, ["cs" + s, "pA"], ["xx" + s])
-        ts(t_("l1", i)[:], t_("xx", i)[:], 512.0, 256.0, A.add, A.min, ["xx" + s], ["l1" + s])
+        ts(T["o" + s][:], T["sm" + s][:], T.pR[:, i:i + 1], -1.0, A.add, A.add, ["sm" + s, "pR"], ["o" + s])
 
     def table(i):
         p = pages[i]
-        cp(T.LP[:, PG * p:PG * p + PG].indirect(t_("of", i)[:, 0:16]), T.VS[:], ["of%d" % i, "VS"], ["P%d" % p])
+        cp(T.LP[:, PG * p:PG * p + PG].indirect(T["o%d" % i][:]), T.VS[:], ["o%d" % i, "VS"], ["P%d" % p])
 
-    def vals(i):
-        p = pages[i]
-        act(T.LD[:, V0 + PG * p:V0 + PG * p + PG], t_("va", i)[:, 0:PG + 16].indirect(t_("l1", i)[:, 0:16]),
-            ["va%d" % i, "vn%d" % i, "l1%d" % i], ["E%d" % p])
-
-    def share(buf, at, key, es, sem):
-        sl = buf[:, at:at + PG]
-        send([(sl, sl, near, es, "%s%d" % (sem, rank))], [key])
-
+    own = "lv%d" % rank
     starts(0)
-    act(T.lv[:, 8 * rank:8 * rank + 2], T.cz0[:, 14:16], ["cz0"], [own])
-    cc = T.cz0[:, 14:16]
     ld = T.lv[:, 8 * rank:8 * rank + 2]
+    cc = T.cz0[:, 14:16]
+    act(ld, cc, ["cz0"], [own])
     send([(cc, ld, far, efar, "h%d" % rank), (cc, ld, near, enear, "h%d" % rank)], ["cz0"])
-    send([(T.va0[:, 0:PG], T.va1[:, 0:PG], [peer], efar, "v")], ["va0"])
-    turn(0)
-    sums(0)
-    ms(T.va0[:, PG:PG + 16], -1.0, ["vn0"])
-    lists(0)
-    vals(0)
-    table(0)
-    iota(T.QN[:], [[-16, 8]], 256, 0, ["QN"])
-    iota(T.t0w[:], [[1, 3], [256, 4]], 256 + 2 * rank, 0, ["t0w"])
-    iota(T.tr[:], [[1, 3], [16, 64]], 2 * rank, 0, ["tr"])
-    share(T.LD, V0 + PG * rank, "E%d" % rank, enear, "e")
-    share(T.LP, PG * rank, "P%d" % rank, eall, "p")
-    ms(T.va1[:, PG:PG + 16], -1.0, ["vn1"])
-    ts(T.I[:], T.J[:], T.pc[:, 3:4], None, A.is_equal, None, ["J", "pc3"], ["I"])
-    act(T.D0[:], T.I[:], ["I", "pc4"], ["D0"], 0.0, T.pc[:, 4:5])
-    act(T.D1[:], T.I[:], ["I", "pc5"], ["D1"], 0.0, T.pc[:, 5:6])
+    send([(T.va0[:, V0:V0 + HF], T.va1[:, V0:V0 + HF], [peer], efar, "va")], ["va0"])
+    ts(T.ti[:, 0:16], T.dli[:], T.pc[:, 1:2], None, A.mult, None, ["dl", "pc1"], ["tia"])
+    ts(T.ti[:, 16:32], T.dli[:], T.pc[:, 2:3], None, A.mult, None, ["dl", "pc2"], ["tib"])
+    op("qv", lambda v: v.transpose(T.tq[:], T.ti[:]), ["tia", "tib"], ["tq"])
+    ts(T.N5[:], T.J[:], T.pc[:, 3:4], 512.0, A.is_equal, A.mult, ["J", "pc3"], ["N5"])
+    a, b = T.tq[:, 0:16], T.tq[:, 16:32]
+    mm(T.pB[:, 0:16], T.BO[:], a, ["BO", "tq"], [], True, False)
+    mm(T.pB[:, 0:16], T.BO[:], b, [], ["pB"], False, True)
+    mm(T.pA[:, 0:16], T.Lo[:], a, [], [], True, False)
+    mm(T.pA[:, 0:16], T.Lo[:], b, [], [], False, False)
+    mm(T.pA[:, 0:16], T.N5[:], a, ["N5"], [], False, False)
+    mm(T.pA[:, 0:16], T.N5[:], b, [], ["pA"], False, True)
+    places(0)
+    scan(T.cs[:, 1:16], T.ones[:, 0:15], T.pB[:, 0:15], 0.0, ["ones", "pB", "cs"], ["cs"])
+    places_end(0)
+    tt(T.xx[:], T.cs[:], T.pA[:, 0:16], A.add, ["cs", "pA"], ["xx"])
+    ts(T.l0[:], T.xx[:], V0 - 512.0, 0.0, A.add, A.max, ["xx"], ["l0"])
+    send([(T.l0[:], T.l1[:], [peer], efar, "w")], ["l0"])
+    send([(T.va0[:, V0 + HF:V0 + PG], T.va1[:, V0 + HF:V0 + PG], [peer], efar, "vb")], ["va0"])
 
-    note(("u", len(efar)), [], ["rl1", "dl1"])
-    note(("v", len(efar)), [], ["va1"])
+    at = V0 + PG * rank
+    act(T.LD[:, at:at + PG], T.va0[:].indirect(T.l0[:]), ["va0", "vn0", "l0"], ["E%d" % rank])
+    table(0)
+    share([(T.LD[:, at:at + PG], "E%d" % rank, "e"), (T.LP[:, PG * rank:PG * rank + PG], "P%d" % rank, "p")])
+    iota(T.t0w[:], [[1, 3], [256, 4]], 256 + 2 * rank, 0, ["t0w"])
+    iota(T.QN[:], [[-16, 8]], 256, 0, ["QN"])
+    iota(T.tr[:], [[1, 3], [16, 64]], 2 * rank, 0, ["tr"])
+    ms(T.va1[:, 0:V0], -1.0, ["vn1"])
+    ts(T.pc[:, 4:5], T.C[:, 0:1], 128.0, None, A.is_gt, None, ["C"], ["pc4"])
+    ts(T.pc[:, 5:6], T.C[:, 0:1], 128.0, None, A.is_le, None, ["C"], ["pc5"])
+    ts(T.I[:], T.J[:], T.pc[:, 3:4], None, A.is_equal, None, ["J", "pc3"], ["I"])
+    act(T.pc[:, 10:11], T.C[:, 0:1], ["C"], ["pc10"], 16.0, -0.0625)
+    act(T.pc[:, 8:9], T.pc[:, 5:6], ["pc5"], ["pc8"], -1.0, 2.0)
+    act(T.pc[:, 9:10], T.pc[:, 5:6], ["pc5"], ["pc9"], 0.0, -1.0)
+    act(T.pc[:, 7:8], T.pc[:, 4:5], ["pc4"], ["pc7"], 0.0, 256.0)
+    act(T.pc[:, 6:7], T.pc[:, 5:6], ["pc5", "pc10"], ["pc6"], T.pc[:, 10:11], -8.0, F.Identity)
+    for d, c in ((0, 4), (1, 5), (2, 8), (3, 9)):
+        act(T["D%d" % d][:], T.I[:], ["I", "pc%d" % c], ["D%d" % d], 0.0, T.pc[:, c:c + 1])
+    act(T.DW[:], T.I[:], ["I", "pc6"], ["DW"], 0.0, T.pc[:, 6:7])
+
+    note(("u", len(efar)), [], ["rl1"])
+    note(("w", len(efar)), [], ["l1"])
+    note(("va", len(efar)), [], ["va1a"])
+    note(("vb", len(efar)), [], ["va1b"])
     for s in near:
         note(("h%d" % s, len(enear)), [], ["lv%d" % s])
     for s in far:
         note(("h%d" % s, len(efar)), [], ["lv%d" % s])
 
     starts(1)
-    turn(1)
-    sums(1)
-    lists(1)
+    places(1)
+    places_end(1)
     table(1)
-    share(T.LP, PG * peer, "P%d" % peer, eall, "q")
-    vals(1)
-    share(T.LD, V0 + PG * peer, "E%d" % peer, eall, "f")
+    share([(T.LP[:, PG * peer:PG * peer + PG], "P%d" % peer, "q")])
+    at = V0 + PG * peer
+    act(T.LD[:, at:at + HF], T.va1[:, 0:V0 + HF].indirect(T.l1[:, 0:8]), ["va1a", "vn1", "l1"], ["E%d" % peer])
+    act(T.LD[:, at + HF:at + PG], T.va1[:].indirect(T.l1[:, 8:16]), ["va1a", "va1b", "vn1", "l1"], ["E%d" % peer])
+    share([(T.LD[:, at:at + PG], "E%d" % peer, "k")])
 
     mm(T.pT[:, 0:8], T.BO[:], T.lv[:, 1:64:8], ["lv%d" % s for s in range(n)] + ["BO"], ["pT"])
     ts(T.tw[:], T.t0w[:], T.C[:, 0:1], None, A.subtract, None, ["t0w", "C"], ["tw"])
     ts(T.m8[:], T.QN[:], T.C[:, 0:1], None, A.is_equal, None, ["QN", "C"], ["m8"])
-    ms(T.LP[:, 8 * PG:8 * PG + 16], 0.0, ["Pend"])
-    ms(T.LD[:, 0:V0], -2.0, ["E"])
-    ts(T.pc[:, 7:8], T.pc[:, 4:5], 256.0, None, A.mult, None, ["pc4"], ["pc7"])
     scan(T.B[:], T.ones[:, 0:8], T.pT[:, 0:8], 0.0, ["ones", "pT"], ["B"])
     ts(T.dt[:], T.pT[:, 0:8], -1.0, 256.0, A.mult, A.add, ["pT"], ["dt"])
     tt(T.lm[:], T.B[:], T.m8[:], A.mult, ["B", "m8"], ["lm"])
@@ -272,37 +257,41 @@ def rank_program(g, core, T, topo):
         mm(T.pG[:, 0:12], T.I[:], c, ["I", "cm%d" % x], ["pG"] if x == 7 else [], x == 0, x == 7)
     op("qv", lambda v: v.tensor_reduce(T.lim[:], T.lm[:], X.X, A.add), ["lm"], ["lim"])
     tt(T.gs[:], T.tw[:], T.pG[:, 0:12], A.add, ["tw", "pG"], ["gs"])
-    ts(T.cq[:], T.tr[:], T.lim[:], T.pc[:, 7:8], A.is_ge, A.mult, ["tr", "lim", "pc7"], ["cq"])
     ts(T.g1[:], T.gs[:], float(8 * PG), None, A.min, None, ["gs"], ["g1"])
+    ts(T.cq[:], T.tr[:], T.lim[:], T.pc[:, 7:8], A.is_ge, A.mult, ["tr", "lim", "pc7"], ["cq"])
     mm(T.pQ[:, 0:192], T.BO[:], T.cq[:], ["BO", "cq"], ["pQ"])
-    ts(T.ii[:, 2:3], e0, 4, 7, A.logical_shift_right, A.bitwise_and, ["EI"], ["ii2"])
-    cp(T.pc[:, 6:7], T.ii[:, 2:3], ["ii2"], ["pc6"])
+    ms(T.LP[:, 8 * PG:8 * PG + 16], 0.0, ["Pend"])
+    ms(T.LD[:, 0:V0], -2.0, ["E"])
     act(T.Qs[:], T.pQ[:, 0:192], ["pQ"], ["Qs"], float(V0))
 
     for s in near:
-        note(("p%d" % s, len(eall)), [], ["P%d" % s])
-        note(("q%d" % s, len(eall)), [], ["P%d" % peer_of(s)])
-        note(("e%d" % s, len(enear)), [], ["E%d" % s])
-        note(("f%d" % s, len(eall)), [], ["E%d" % peer_of(s)])
+        arrive("p", s, "P%d" % s)
+        arrive("q", s, "P%d" % peer_of(s))
+        arrive("e", s, "E%d" % s)
+        arrive("k", s, "E%d" % peer_of(s))
     rd = ["P%d" % s for s in range(n)] + ["Pend", "g1"]
-    win = T.LP[:, 0:8 * PG + 16]
-    act(T.Sg[:, 96:192], win.indirect(T.g1[:, 6:12]), rd, ["Sgb"])
-    cp(T.Sg[:, 0:96], win.indirect(T.g1[:, 0:6]), rd, ["Sga"])
-    mm(T.pS[:, 0:128], T.D0[:], T.Qs[:, 0:128], ["D0", "Qs"], [], True, False)
-    mm(T.pS[:, 0:128], T.D1[:], T.Qs[:, 64:192], ["D1"], [], False, False)
-    mm(T.pS[:, 0:128], T.D0[:], T.Sg[:, 0:128], ["Sga", "Sgb"], [], False, False)
-    mm(T.pS[:, 0:128], T.D1[:], T.Sg[:, 64:192], [], ["pS"], False, True)
-    ts(T.st[:], T.pS[:, 0:64], T.pc[:, 6:7], None, A.add, None, ["pS", "pc6"], ["st"])
-    tt(T.nz[:], T.st[:], T.pS[:, 64:128], A.is_lt, ["st", "pS"], ["nz"])
-    tt(T.of[:], T.st[:], T.nz[:], A.mult, ["st", "nz"], ["of"])
+    act(T.Sg[:, 96:192], T.LP[:].indirect(T.g1[:, 6:12]), rd, ["Sgb"])
+    cp(T.Sg[:, 0:96], T.LP[:].indirect(T.g1[:, 0:6]), rd, ["Sga"])
+    pS, pD = T.pS[:, 0:64], T.pD[:, 0:64]
+    dw = [(T.D0, "D0"), (T.D2, "D2"), (T.D3, "D3")]
+    mm(pS, T.DW[:], T.ones[:], ["DW", "ones"], [], True, False)
+    mm(pS, T.D0[:], T.Qs[:, 0:64], ["D0", "Qs"], [], False, False)
+    mm(pS, T.D1[:], T.Qs[:, 64:128], ["D1"], [], False, False)
+    for j, (d, k) in enumerate(dw):
+        mm(pD, d[:], T.Qs[:, 64 * j:64 * j + 64], [k], [], j == 0, False)
+    for j, (d, k) in enumerate(dw):
+        mm(pD, d[:], T.Sg[:, 64 * j:64 * j + 64], ["Sga", "Sgb"], ["pD"] if j == 2 else [], False, j == 2)
+    mm(pS, T.D0[:], T.Sg[:, 0:64], [], [], False, False)
+    mm(pS, T.D1[:], T.Sg[:, 64:128], [], ["pS"], False, True)
+    ts(T.nz[:], pD, T.pc[:, 6:7], 0.0, A.add, A.is_lt, ["pD", "pc6"], ["nz"])
+    tt(T.of[:], T.nz[:], pS, A.mult, ["nz", "pS"], ["of"])
     cp(T.Wt[:], T.of[:], ["of"], ["Wt"])
 
     rd = ["E%d" % s for s in range(n)] + ["E", "Wt"]
-    win = T.LD[:, 0:V0 + 8 * PG]
-    act(T.Y[:, 512:1024], win.indirect(T.Wt[:, 32:64]), rd, ["Yb"])
-    cp(T.Y[:, 0:512], win.indirect(T.Wt[:, 0:32]), rd, ["Ya"])
-    dma("qs", T.y[:, 512:1024], T.Y[:, 512:1024], "dz", ["Yb"], [])
-    dma("sync", T.y[:, 0:512], T.Y[:, 0:512], "dy", ["Ya"], [])
+    for i, fn in ((1, act), (0, cp), (3, act), (2, cp)):
+        fn(T.Y[:, 256 * i:256 * i + 256], T.LD[:].indirect(T.Wt[:, 16 * i:16 * i + 16]), rd, ["Y%d" % i])
+    for i, e in ((0, "sync"), (1, "sync"), (2, "sync"), (3, "qs")):
+        dma(e, T.y[:, 256 * i:256 * i + 256], T.Y[:, 256 * i:256 * i + 256], "dy%d" % i, ["Y%d" % i], [])
 
     g.wait_ge(T.sem.loc, loc[0])
-    need("qg", [(e, cnt[e]) for e in cnt if cnt[e]] + [(s, 16) for s in ("drl", "ddl", "dval", "dy", "dz")])
+    need("qg", [(e, cnt[e]) for e in cnt if cnt[e]] + [(s, 16) for s in ("drl", "ddl", "dval", "dy0", "dy1", "dy2", "dy3")])

from concourse.bass import DstId, RemoteDMATransfer
from concourse.mybir import AluOpType as A, ActivationFunctionType as F, AxisListType as X

PG = 256
HF = 128
V0 = 16
b2, f4, i4, u2 = "bfloat16", "float32", "int32", "uint16"
SCRATCH = {}
for _n, _w, _d in [("EI", 16, i4), ("J", 128, i4), ("VS", PG, b2), ("QN", 8, f4), ("t0w", 12, f4), ("tr", 192, f4), ("ii", 8, i4),
                   ("pc", 16, f4), ("ei", 16, i4), ("C", 16, f4), ("Jg", 128, i4), ("BO", 128, b2), ("G", 128, b2), ("Lo", 128, b2),
                   ("N5", 128, b2), ("I", 128, b2), ("D0", 128, b2), ("D1", 128, b2), ("D2", 128, b2), ("D3", 128, b2),
                   ("DW", 128, b2), ("ones", 64, b2), ("m8", 8, f4), ("tw", 12, f4),
                   ("dli", 16, i4), ("lv", 64, b2), ("ti", 32, b2), ("tq", 32, b2), ("cs", 16, f4), ("xx", 16, f4), ("B", 8, f4),
                   ("dt", 8, f4), ("lm", 8, f4), ("lim", 1, f4), ("cm", 96, b2), ("cq", 192, b2), ("gs", 12, f4), ("g1", 12, u2),
                   ("Qs", 192, b2), ("Sg", 192, b2), ("nz", 64, f4), ("of", 64, f4), ("Wt", 64, u2), ("Y", 1024, b2),
                   ("LD", V0 + 8 * PG, b2), ("LP", 8 * PG + 16, b2)]:
    SCRATCH[_n] = ("sbuf", [128, _w], _d)
for _n in "RBATGQSD":
    SCRATCH["p" + _n] = ("psum", [128, 512], f4)
for _i in "01":
    for _n, _w, _d in [("r", 16, i4), ("va", V0 + PG, b2), ("z", 16, b2), ("cz", 16, b2), ("mu", 16, f4), ("sm", 16, f4), ("o", 16, u2),
                       ("l", 16, u2)]:
        SCRATCH[_n + _i] = ("sbuf", [128, _w], _d)
SEMAPHORES = (["qv", "qs", "qt", "qg", "drl", "ddl", "dval", "dy0", "dy1", "dy2", "dy3", "loc", "u", "w", "va", "vb"]
              + ["%s%d" % (x, i) for x in "hpqek" for i in range(8)])


def bits(es):
    m = 0
    for e in es:
        m |= 1 << e
    return m


def rank_program(g, core, T, topo):
    rank = T.rank_of(core)
    if rank is None:
        return
    cores = list(T.cores)
    n = len(cores)
    near = [r for r in range(n) if r != rank and topo.chip(cores[r]) == topo.chip(core)]
    home = sorted(near + [rank])
    far = [r for r in range(n) if r not in home]

    def peer_of(r):
        return far[home.index(r)]
    peer = peer_of(rank)
    pages = [rank, peer]
    efar = topo.engines(core, cores[peer])
    eall = topo.engines(core, cores[near[0]])
    enear = [e for e in eall if e not in efar]
    EN = {"e": efar, "p": enear, "q": eall, "k": eall}

    q = {"qv": g.vector, "qs": g.scalar, "qt": g.tensor, "qg": g, "sync": g.sync}
    cnt = {"qv": 0, "qs": 0, "qt": 0, "qg": 0}
    seen = {e: {} for e in q}
    lastw = {}
    readers = {}

    def need(e, deps):
        best = {}
        for s, k in deps:
            if seen[e].get(s, 0) < k:
                best[s] = max(best.get(s, 0), k)
        for s, k in best.items():
            q[e].wait_ge(T.sem[s], k)
            seen[e][s] = k

    def deps_of(e, r, w):
        d = [lastw[k] for k in list(r) + list(w) if k in lastw]
        for k in w:
            d += [x for x in readers.get(k, []) if x[0] != e]
        return d

    def note(tag, r, w):
        for k in r:
            readers.setdefault(k, []).append(tag)
        for k in w:
            lastw[k] = tag
            readers[k] = []

    def op(e, fn, r, w):
        need(e, deps_of(e, r, w))
        fn(q[e]).then_inc(T.sem[e], 1)
        cnt[e] += 1
        note((e, cnt[e]), r, w)

    def dma(e, out, in_, sem, r, w):
        need(e, deps_of(e, r, w))
        q[e].dma_start(out, in_).then_inc(T.sem[sem], 16)
        note((sem, 16), r, w)

    def ts(out, in0, s1, s2, op0, op1, r, w):
        if op1 is None:
            op("qv", lambda v: v.tensor_scalar(out, in0, s1, s2, op0), r, w)
        else:
            op("qv", lambda v: v.tensor_scalar(out, in0, s1, s2, op0, op1), r, w)

    def tt(out, a, b, o, r, w):
        op("qv", lambda v: v.tensor_tensor(out, a, b, o), r, w)

    def cp(out, a, r, w):
        op("qv", lambda v: v.tensor_copy(out, a), r, w)

    def act(out, a, r, w, bias=0.0, scale=1.0, fn=F.Copy):
        op("qs", lambda s: s.activation(out, a, fn, bias, scale), r, w)

    def ms(ap, c, w):
        op("qv", lambda v: v.memset(ap, c), [], w)

    def mm(out, l, rh, r, w, st=True, sp=True):
        op("qt", lambda t: t.matmul(out, l, rh, st, sp), r, w)

    def scan(out, a, b, init, r, w):
        op("qv", lambda v: v.tensor_tensor_scan(out, a, b, init, A.mult, A.add), r, w)

    def iota(out, pat, base, cm, w):
        op("qg", lambda x: x.iota(out, pat, base, cm, allow_small_or_imprecise_dtypes=True), [], w)

    loc = [0]

    def send(parts, r):
        need("qg", deps_of("qg", r, []))
        trs = []
        for src, dst, ds, es, sem in parts:
            ad = [topo.addr(cores[d]) for d in ds]
            trs.append(RemoteDMATransfer(srcs=[src], dsts=[dst for d in ds], dst_ids=[DstId(rid=a[0], pnc=a[1]) for a in ad],
                                         dma_engine_mask=bits(es), remote_sem=T.sem[sem]))
            loc[0] += len(es)
        g.remote_dma_fused(trs, local_sem=T.sem.loc)

    def share(parts):
        send([(sl, sl, near, EN[x], "%s%d" % (x, rank)) for sl, key, x in parts], [p[1] for p in parts])

    def arrive(x, s, key):
        note(("%s%d" % (x, s), len(EN[x])), [], [key])

    dma("sync", T.r0[:], T.rl[:], "drl", [], ["rl0"])
    dma("qs", T.dli[:], T.dl[:], "ddl", [], ["dl"])
    dma("sync", T.va0[:, V0:V0 + PG], T.val[:], "dval", [], ["va0"])

    op("qg", lambda x: x.iota(T.EI[:], [[1, 16]], 0, 16), [], ["EI"])
    op("qg", lambda x: x.iota(T.J[:], [[1, 128]], 0, 0), [], ["J"])
    iota(T.VS[:], [[1, 16], [16, 16]], 0, 0, ["VS"])
    send([(T.r0[:], T.r1[:], [peer], efar, "u")], ["rl0"])
    ms(T.ones[:], 1.0, ["ones"])
    ms(T.cs[:], 0.0, ["cs"])
    ms(T.va0[:, 0:V0], -1.0, ["vn0"])
    e0 = T.EI[:, 0:1]
    ts(T.ii[:, 0:1], e0, 8, None, A.logical_shift_right, None, ["EI"], ["ii0"])
    ts(T.ii[:, 1:2], e0, 8, 1, A.logical_shift_right, A.bitwise_and, ["EI"], ["ii1"])
    ts(T.ei[:], T.EI[:], 255, None, A.bitwise_and, None, ["EI"], ["ei"])
    ts(T.pc[:, 3:4], e0, 0.0625, None, A.mult, None, ["EI"], ["pc3"])
    cp(T.pc[:, 0:1], T.ii[:, 0:1], ["ii0"], ["pc0"])
    cp(T.pc[:, 2:3], T.ii[:, 1:2], ["ii1"], ["pc2"])
    ts(T.pc[:, 1:2], T.ii[:, 1:2], -1.0, 1.0, A.mult, A.add, ["ii1"], ["pc1"])
    ts(T.C[:], T.ei[:], -1.0, 256.0, A.mult, A.add, ["ei"], ["C"])
    ts(T.Jg[:], T.J[:], 4, None, A.logical_shift_right, None, ["J"], ["Jg"])
    ts(T.G[:], T.J[:], T.pc[:, 3:4], None, A.is_gt, None, ["J", "pc3"], ["G"])
    ts(T.BO[:], T.Jg[:], T.pc[:, 0:1], None, A.is_equal, None, ["Jg", "pc0"], ["BO"])
    tt(T.Lo[:], T.G[:], T.BO[:], A.mult, ["G", "BO"], ["Lo"])

    def starts(i):
        s = "%d" % i
        z, cz = T["z" + s], T["cz" + s]
        ts(z[:], T["r" + s][:], -1.0, 1.0, A.mult, A.add, ["rl" + s], ["z" + s])
        scan(cz[:], T.ones[:, 0:16], z[:], 0.0, ["ones", "z" + s], ["cz" + s])
        mm(T.pR[:, i:i + 1], T.Lo[:], cz[:, 15:16], ["Lo", "cz" + s], ["pR"])

    def places(i):
        s = "%d" % i
        tt(T["mu" + s][:], T["r" + s][:], T.C[:], A.mult, ["rl" + s, "C"], ["mu" + s])
        tt(T["sm" + s][:], T["cz" + s][:], T["mu" + s][:], A.add, ["cz" + s, "mu" + s], ["sm" + s])

    def places_end(i):
        s = "%d" % i
        ts(T["o" + s][:], T["sm" + s][:], T.pR[:, i:i + 1], -1.0, A.add, A.add, ["sm" + s, "pR"], ["o" + s])

    def table(i):
        p = pages[i]
        cp(T.LP[:, PG * p:PG * p + PG].indirect(T["o%d" % i][:]), T.VS[:], ["o%d" % i, "VS"], ["P%d" % p])

    own = "lv%d" % rank
    starts(0)
    ld = T.lv[:, 8 * rank:8 * rank + 2]
    cc = T.cz0[:, 14:16]
    act(ld, cc, ["cz0"], [own])
    send([(cc, ld, far, efar, "h%d" % rank), (cc, ld, near, enear, "h%d" % rank)], ["cz0"])
    send([(T.va0[:, V0:V0 + HF], T.va1[:, V0:V0 + HF], [peer], efar, "va")], ["va0"])
    ts(T.ti[:, 0:16], T.dli[:], T.pc[:, 1:2], None, A.mult, None, ["dl", "pc1"], ["tia"])
    ts(T.ti[:, 16:32], T.dli[:], T.pc[:, 2:3], None, A.mult, None, ["dl", "pc2"], ["tib"])
    op("qv", lambda v: v.transpose(T.tq[:], T.ti[:]), ["tia", "tib"], ["tq"])
    ts(T.N5[:], T.J[:], T.pc[:, 3:4], 512.0, A.is_equal, A.mult, ["J", "pc3"], ["N5"])
    a, b = T.tq[:, 0:16], T.tq[:, 16:32]
    mm(T.pB[:, 0:16], T.BO[:], a, ["BO", "tq"], [], True, False)
    mm(T.pB[:, 0:16], T.BO[:], b, [], ["pB"], False, True)
    mm(T.pA[:, 0:16], T.Lo[:], a, [], [], True, False)
    mm(T.pA[:, 0:16], T.Lo[:], b, [], [], False, False)
    mm(T.pA[:, 0:16], T.N5[:], a, ["N5"], [], False, False)
    mm(T.pA[:, 0:16], T.N5[:], b, [], ["pA"], False, True)
    places(0)
    scan(T.cs[:, 1:16], T.ones[:, 0:15], T.pB[:, 0:15], 0.0, ["ones", "pB", "cs"], ["cs"])
    places_end(0)
    tt(T.xx[:], T.cs[:], T.pA[:, 0:16], A.add, ["cs", "pA"], ["xx"])
    ts(T.l0[:], T.xx[:], V0 - 512.0, 0.0, A.add, A.max, ["xx"], ["l0"])
    send([(T.l0[:], T.l1[:], [peer], efar, "w")], ["l0"])
    send([(T.va0[:, V0 + HF:V0 + PG], T.va1[:, V0 + HF:V0 + PG], [peer], efar, "vb")], ["va0"])

    at = V0 + PG * rank
    act(T.LD[:, at:at + PG], T.va0[:].indirect(T.l0[:]), ["va0", "vn0", "l0"], ["E%d" % rank])
    table(0)
    share([(T.LD[:, at:at + PG], "E%d" % rank, "e"), (T.LP[:, PG * rank:PG * rank + PG], "P%d" % rank, "p")])
    iota(T.t0w[:], [[1, 3], [256, 4]], 256 + 2 * rank, 0, ["t0w"])
    iota(T.QN[:], [[-16, 8]], 256, 0, ["QN"])
    iota(T.tr[:], [[1, 3], [16, 64]], 2 * rank, 0, ["tr"])
    ms(T.va1[:, 0:V0], -1.0, ["vn1"])
    ts(T.pc[:, 4:5], T.C[:, 0:1], 128.0, None, A.is_gt, None, ["C"], ["pc4"])
    ts(T.pc[:, 5:6], T.C[:, 0:1], 128.0, None, A.is_le, None, ["C"], ["pc5"])
    ts(T.I[:], T.J[:], T.pc[:, 3:4], None, A.is_equal, None, ["J", "pc3"], ["I"])
    act(T.pc[:, 10:11], T.C[:, 0:1], ["C"], ["pc10"], 16.0, -0.0625)
    act(T.pc[:, 8:9], T.pc[:, 5:6], ["pc5"], ["pc8"], -1.0, 2.0)
    act(T.pc[:, 9:10], T.pc[:, 5:6], ["pc5"], ["pc9"], 0.0, -1.0)
    act(T.pc[:, 7:8], T.pc[:, 4:5], ["pc4"], ["pc7"], 0.0, 256.0)
    act(T.pc[:, 6:7], T.pc[:, 5:6], ["pc5", "pc10"], ["pc6"], T.pc[:, 10:11], -8.0, F.Identity)
    for d, c in ((0, 4), (1, 5), (2, 8), (3, 9)):
        act(T["D%d" % d][:], T.I[:], ["I", "pc%d" % c], ["D%d" % d], 0.0, T.pc[:, c:c + 1])
    act(T.DW[:], T.I[:], ["I", "pc6"], ["DW"], 0.0, T.pc[:, 6:7])

    note(("u", len(efar)), [], ["rl1"])
    note(("w", len(efar)), [], ["l1"])
    note(("va", len(efar)), [], ["va1a"])
    note(("vb", len(efar)), [], ["va1b"])
    for s in near:
        note(("h%d" % s, len(enear)), [], ["lv%d" % s])
    for s in far:
        note(("h%d" % s, len(efar)), [], ["lv%d" % s])

    starts(1)
    places(1)
    places_end(1)
    table(1)
    share([(T.LP[:, PG * peer:PG * peer + PG], "P%d" % peer, "q")])
    at = V0 + PG * peer
    act(T.LD[:, at:at + HF], T.va1[:, 0:V0 + HF].indirect(T.l1[:, 0:8]), ["va1a", "vn1", "l1"], ["E%d" % peer])
    act(T.LD[:, at + HF:at + PG], T.va1[:].indirect(T.l1[:, 8:16]), ["va1a", "va1b", "vn1", "l1"], ["E%d" % peer])
    share([(T.LD[:, at:at + PG], "E%d" % peer, "k")])

    mm(T.pT[:, 0:8], T.BO[:], T.lv[:, 1:64:8], ["lv%d" % s for s in range(n)] + ["BO"], ["pT"])
    ts(T.tw[:], T.t0w[:], T.C[:, 0:1], None, A.subtract, None, ["t0w", "C"], ["tw"])
    ts(T.m8[:], T.QN[:], T.C[:, 0:1], None, A.is_equal, None, ["QN", "C"], ["m8"])
    scan(T.B[:], T.ones[:, 0:8], T.pT[:, 0:8], 0.0, ["ones", "pT"], ["B"])
    ts(T.dt[:], T.pT[:, 0:8], -1.0, 256.0, A.mult, A.add, ["pT"], ["dt"])
    tt(T.lm[:], T.B[:], T.m8[:], A.mult, ["B", "m8"], ["lm"])
    for x in range(8):
        c = T.cm[:, 12 * x:12 * x + 12]
        ts(c, T.tw[:], T.B[:, x:x + 1], T.dt[:, x:x + 1], A.is_ge, A.mult, ["tw", "B", "dt"], ["cm%d" % x])
        mm(T.pG[:, 0:12], T.I[:], c, ["I", "cm%d" % x], ["pG"] if x == 7 else [], x == 0, x == 7)
    op("qv", lambda v: v.tensor_reduce(T.lim[:], T.lm[:], X.X, A.add), ["lm"], ["lim"])
    tt(T.gs[:], T.tw[:], T.pG[:, 0:12], A.add, ["tw", "pG"], ["gs"])
    ts(T.g1[:], T.gs[:], float(8 * PG), None, A.min, None, ["gs"], ["g1"])
    ts(T.cq[:], T.tr[:], T.lim[:], T.pc[:, 7:8], A.is_ge, A.mult, ["tr", "lim", "pc7"], ["cq"])
    mm(T.pQ[:, 0:192], T.BO[:], T.cq[:], ["BO", "cq"], ["pQ"])
    ms(T.LP[:, 8 * PG:8 * PG + 16], 0.0, ["Pend"])
    ms(T.LD[:, 0:V0], -2.0, ["E"])
    act(T.Qs[:], T.pQ[:, 0:192], ["pQ"], ["Qs"], float(V0))

    for s in near:
        arrive("p", s, "P%d" % s)
        arrive("q", s, "P%d" % peer_of(s))
        arrive("e", s, "E%d" % s)
        arrive("k", s, "E%d" % peer_of(s))
    rd = ["P%d" % s for s in range(n)] + ["Pend", "g1"]
    act(T.Sg[:, 96:192], T.LP[:].indirect(T.g1[:, 6:12]), rd, ["Sgb"])
    cp(T.Sg[:, 0:96], T.LP[:].indirect(T.g1[:, 0:6]), rd, ["Sga"])
    pS, pD = T.pS[:, 0:64], T.pD[:, 0:64]
    dw = [(T.D0, "D0"), (T.D2, "D2"), (T.D3, "D3")]
    mm(pS, T.DW[:], T.ones[:], ["DW", "ones"], [], True, False)
    mm(pS, T.D0[:], T.Qs[:, 0:64], ["D0", "Qs"], [], False, False)
    mm(pS, T.D1[:], T.Qs[:, 64:128], ["D1"], [], False, False)
    for j, (d, k) in enumerate(dw):
        mm(pD, d[:], T.Qs[:, 64 * j:64 * j + 64], [k], [], j == 0, False)
    for j, (d, k) in enumerate(dw):
        mm(pD, d[:], T.Sg[:, 64 * j:64 * j + 64], ["Sga", "Sgb"], ["pD"] if j == 2 else [], False, j == 2)
    mm(pS, T.D0[:], T.Sg[:, 0:64], [], [], False, False)
    mm(pS, T.D1[:], T.Sg[:, 64:128], [], ["pS"], False, True)
    ts(T.nz[:], pD, T.pc[:, 6:7], 0.0, A.add, A.is_lt, ["pD", "pc6"], ["nz"])
    tt(T.of[:], T.nz[:], pS, A.mult, ["nz", "pS"], ["of"])
    cp(T.Wt[:], T.of[:], ["of"], ["Wt"])

    rd = ["E%d" % s for s in range(n)] + ["E", "Wt"]
    for i, fn in ((1, act), (0, cp), (3, act), (2, cp)):
        fn(T.Y[:, 256 * i:256 * i + 256], T.LD[:].indirect(T.Wt[:, 16 * i:16 * i + 16]), rd, ["Y%d" % i])
    for i, e in ((0, "sync"), (1, "sync"), (2, "sync"), (3, "qs")):
        dma(e, T.y[:, 256 * i:256 * i + 256], T.Y[:, 256 * i:256 * i + 256], "dy%d" % i, ["Y%d" % i], [])

    g.wait_ge(T.sem.loc, loc[0])
    need("qg", [(e, cnt[e]) for e in cnt if cnt[e]] + [(s, 16) for s in ("drl", "ddl", "dval", "dy0", "dy1", "dy2", "dy3")])
